import numpy as np
import ml_dtypes


def mxq(x, axis, fmt="e4m3"):
    dtype, down = {"e4m3": (ml_dtypes.float8_e4m3fn, 7), "e5m2": (ml_dtypes.float8_e5m2, 14)}[fmt]
    v = np.moveaxis(np.asarray(x, np.float32).astype(ml_dtypes.bfloat16).astype(np.float64), axis, -1)
    blocks = v.reshape(v.shape[:-1] + (-1, 32))
    amax = np.abs(blocks).max(-1, keepdims=True)
    byte = np.maximum(np.where(amax > 0, np.frexp(amax)[1] - 1 + 127, 0) - down, 1)
    scale = np.exp2(byte - 127.0)
    codes = (blocks / scale).astype(np.float32).astype(dtype).astype(np.float64)
    return np.moveaxis((codes * scale).reshape(v.shape), -1, axis)


WIDE = False


def mx_kscale(k):
    if not WIDE:
        return np.ones(k)
    levels = np.array([10, -10, 5, -5, 0])
    if k % 512:
        return np.exp2(np.random.permutation(np.resize(levels, k // 32))).repeat(32)
    a = np.empty((k // 512, 16))
    for p in range(k // 512):
        a[p, :8] = np.random.permutation(np.resize(levels, 8))
        for g in range(8):
            far = levels[np.abs(levels - a[p, g]) >= 10]
            a[p, g + 8] = far[np.random.randint(len(far))]
    return np.exp2(a.ravel()).repeat(32)


def f64(x):
    return np.asarray(x).astype(np.float64)


def striped(idx):
    return np.tile(idx.reshape(-1, 16).T, (8, 1)).astype(np.uint16)


def unstriped(offs):
    return offs[:16].T.reshape(-1).astype(np.int64)


def sigmoid(v):
    return 1.0 / (1.0 + np.exp(-np.maximum(v, -700.0)))


K, T, S, H, N = 512, 4096, 1536, 1024, 128


def setup_inputs():
    n = np.random.standard_normal
    s = mx_kscale(K)[:, None]
    u = mx_kscale(H)
    return {
        "xT": (n((K, T)) * s).astype(np.float32),
        "w1": (n((K, H)) / np.sqrt(K) / s).astype(np.float32),
        "w3": (n((K, H)) / np.sqrt(K) / s * u).astype(np.float32),
        "w2": (n((H, N)) / np.sqrt(H) / u[:, None]).astype(np.float32),
        "offs": striped(np.random.permutation(T)[:S]),
    }


def reference(xT, w1, w3, w2, offs):
    idx = unstriped(offs)
    xq = mxq(f64(xT)[:, idx], 0, "e4m3")
    h = sigmoid(mxq(f64(w1), 0, "e4m3").T @ xq) * (mxq(f64(w3), 0, "e4m3").T @ xq)
    y = mxq(f64(w2), 0, "e4m3").T @ mxq(h, 0, "e4m3")
    return y

@@ -1,0 +1,233 @@
+from contextlib import ExitStack
+from functools import partial
+
+import concourse.mybir as mybir
+
+K, T, S, H, N = 512, 4096, 1536, 1024, 128
+FLOPS = 2 * S * (2 * K * H + H * N)
+
+P = 128
+PACK = 4
+F32 = mybir.dt.float32
+BF16 = mybir.dt.bfloat16
+U32 = mybir.dt.uint32
+U16 = mybir.dt.uint16
+U8 = mybir.dt.uint8
+FP8X4 = mybir.dt.float8_e4m3fn_x4
+Copy = mybir.ActivationFunctionType.Copy
+Sigmoid = mybir.ActivationFunctionType.Sigmoid
+mult = mybir.AluOpType.mult
+add = mybir.AluOpType.add
+
+CHUNK = 1024
+SLICE = 512
+GROUP = 128
+RUN = 2
+HALF = 512
+
+
+def tile_picked_pick_glu_sigmoid_sub_e_kernel(tc, xT, w1, w3, w2, offs, out):
+    nc = tc.nc
+    slices = S // SLICE
+    halves = H // HALF
+    with ExitStack() as ctx:
+        keep = ctx.enter_context(tc.tile_pool(name="keep", bufs=1))
+        stage = ctx.enter_context(tc.tile_pool(name="stage", bufs=8))
+        work = ctx.enter_context(tc.tile_pool(name="work", bufs=4))
+        res = ctx.enter_context(tc.tile_pool(name="res", bufs=3))
+        psum_1 = ctx.enter_context(tc.psum_pool(name="psum_1", bufs=4))
+        psum_3 = ctx.enter_context(tc.psum_pool(name="psum_3", bufs=4))
+
+        offsets = keep.tile([P, S // 16], U16, name="offsets")
+        nc.sync.dma_start(offsets[:], offs)
+
+        warm = keep.tile([P, 8], F32, name="warm")
+        nc.vector.memset(warm[:], 0.0)
+        nc.scalar.activation(warm[:, 0:1], warm[:, 0:1], Sigmoid)
+
+        x_rows = xT.rearrange("(p j) t -> p j t", j=PACK)
+        pairs = [keep.tile([P, 2 * T], BF16, align_bytes=64, name=f"pairs{u}") for u in range(2)]
+        picked = [keep.tile([P, SLICE * PACK], BF16, align_bytes=64, name=f"picked{s}") for s in range(slices)]
+        x_codes = [keep.tile([P, SLICE], U32, align_bytes=64, name=f"x_codes{s}") for s in range(slices)]
+        x_scales = [keep.tile([P, SLICE], U8, align_bytes=64, name=f"x_scales{s}") for s in range(slices)]
+
+        def load_x(u, t0, width, engines):
+            raw = stage.tile([P, 2, width], F32, name="raw")
+            nc.sync.dma_start(out=raw[:], in_=x_rows[:, 2 * u : 2 * u + 2, t0 : t0 + width])
+            part = width // len(engines)
+            for i, engine in enumerate(engines):
+                a = t0 + i * part
+                dst = pairs[u][:, 2 * a : 2 * (a + part)].rearrange("p (t e) -> p t e", e=2)
+                src = raw[:, :, i * part : (i + 1) * part].rearrange("p e t -> p t e")
+                if engine == "V":
+                    nc.vector.tensor_copy(dst, src)
+                else:
+                    nc.scalar.activation(dst, src, Copy)
+
+        def gather(u, s):
+            words = picked[s][:].bitcast(U32).rearrange("p (n u) -> p n u", u=2)
+            window = pairs[u][:].bitcast(U32)
+            cols = offsets[:, s * (SLICE // 16) : (s + 1) * (SLICE // 16)]
+            nc.vector.tensor_copy(words[:, :, u], window.indirect(cols))
+
+        for i in range(4):
+            load_x(0, i * CHUNK, CHUNK, "SV"[i % 2])
+        load_x(1, 0, CHUNK, "S")
+        gather(0, 0)
+        load_x(1, CHUNK, CHUNK, "V")
+        gather(0, 1)
+        load_x(1, 2 * CHUNK, CHUNK, "S")
+        gather(0, 2)
+        load_x(1, 3 * CHUNK, CHUNK // 2, "VS")
+        load_x(1, 3 * CHUNK + CHUNK // 2, CHUNK // 2, "V")
+
+        w_codes = {}
+        w_scales = {}
+
+        def load_w(name, w, h, engines):
+            raw = stage.tile([P, PACK, HALF], F32, name="raw")
+            rows = w.rearrange("(p j) c -> p j c", j=PACK)
+            nc.sync.dma_start(out=raw[:], in_=rows[:, :, h * HALF : (h + 1) * HALF])
+            grouped = keep.tile([P, HALF * PACK], BF16, align_bytes=64, name=f"{name}_grouped{h}")
+            for t, engine in enumerate(engines):
+                order = "p t q r j" if engine == "G" else "p t q j r"
+                src = raw[:].rearrange("p j (q t r) -> " + order, t=PACK, r=RUN)
+                dst = grouped[:].rearrange("p (t q r j) -> " + order, t=PACK, r=RUN, j=PACK)
+                if engine == "S":
+                    nc.scalar.activation(dst[:, t], src[:, t], Copy)
+                elif engine == "V":
+                    nc.vector.tensor_copy(dst[:, t], src[:, t])
+                else:
+                    nc.gpsimd.tensor_scalar(dst[:, t], src[:, t], 1.0, 0.0, mult, add)
+            return grouped
+
+        def quantize_w(name, h, grouped):
+            codes = keep.tile([P, HALF], U32, align_bytes=64, name=f"{name}_codes{h}")
+            scales = keep.tile([P, HALF], U8, align_bytes=64, name=f"{name}_scales{h}")
+            nc.vector.quantize_mx(out=codes[:].bitcast(FP8X4), scales=scales[:], in_=grouped[:])
+            w_codes[name, h] = codes
+            w_scales[name, h] = scales
+
+        def quantize_x(s):
+            nc.vector.quantize_mx(out=x_codes[s][:].bitcast(FP8X4), scales=x_scales[s][:], in_=picked[s][:])
+
+        gather(1, 0)
+        gather(1, 1)
+        quantize_x(0)
+        gather(1, 2)
+        quantize_x(1)
+        w3a = load_w("w3", w3, 0, "SSSS")
+        w1a = load_w("w1", w1, 0, "SSVS")
+        quantize_w("w3", 0, w3a)
+        quantize_x(2)
+        quantize_w("w1", 0, w1a)
+
+        later = []
+
+        def load_b():
+            later.append(load_w("w1", w1, 1, "GGGG"))
+            later.append(load_w("w3", w3, 1, "GGGG"))
+
+        w2_raw = keep.tile([P, halves, PACK, N], F32, name="w2_raw")
+        w2_grouped = keep.tile([P, halves * N * PACK], BF16, align_bytes=64, name="w2_grouped")
+        w2_codes = keep.tile([P, halves * N], U32, align_bytes=64, name="w2_codes")
+        w2_scales = keep.tile([P, halves * N], U8, align_bytes=64, name="w2_scales")
+        w2_rows = w2.rearrange("(g q t r) m -> g t q r m", g=halves, t=PACK, r=RUN)
+
+        def load_w2():
+            for g in range(halves):
+                for t in range(PACK):
+                    nc.sync.dma_start(out=w2_raw[:, g, t, :], in_=w2_rows[g, t])
+            for g in range(halves):
+                nc.gpsimd.tensor_scalar(
+                    w2_grouped[:, g * N * PACK : (g + 1) * N * PACK].rearrange("p (m t) -> p m t", t=PACK),
+                    w2_raw[:, g].rearrange("p t m -> p m t"),
+                    1.0, 0.0, mult, add,
+                )
+            nc.vector.quantize_mx(out=w2_codes[:].bitcast(FP8X4), scales=w2_scales[:], in_=w2_grouped[:])
+
+        h_codes = {}
+        h_scales = {}
+        pending = []
+
+        def finish(h, s, hidden, start, done):
+            n_cols = slice(start, done)
+            nc.vector.quantize_mx(
+                out=h_codes[h, s][:, n_cols].bitcast(FP8X4),
+                scales=h_scales[h, s][:, n_cols],
+                in_=hidden[:, start * PACK : done * PACK],
+            )
+            if h < halves - 1:
+                return
+            acc = psum_1.tile([P, done - start], F32, name="acc", tag="w1_bank")
+            for g in range(halves):
+                nc.tensor.matmul_mx(
+                    out=acc[:],
+                    lhsT=w2_codes[:, g * N : (g + 1) * N].bitcast(FP8X4),
+                    lhsT_scale=w2_scales[:, g * N : (g + 1) * N],
+                    rhs=h_codes[g, s][:, n_cols].bitcast(FP8X4),
+                    rhs_scale=h_scales[g, s][:, n_cols],
+                    start=(g == 0),
+                    stop=(g == halves - 1),
+                )
+            y = res.tile([P, done - start], F32, name="y")
+            nc.scalar.copy(y[:], acc[:])
+            nc.sync.dma_start(out=out[:, s * SLICE + start : s * SLICE + done], in_=y[:])
+
+        for h in range(halves):
+            for s in range(slices):
+                hidden = work.tile([P, SLICE * PACK], BF16, align_bytes=64, name="hidden")
+                codes = keep.tile([P, SLICE], U32, align_bytes=64, name=f"h_codes{h}_{s}")
+                scales = keep.tile([P, SLICE], U8, align_bytes=64, name=f"h_scales{h}_{s}")
+                h_codes[h, s] = codes
+                h_scales[h, s] = scales
+                last = h == halves - 1 and s == slices - 1
+                ends = [256, 512] if last else [SLICE]
+                for c in range(SLICE // GROUP):
+                    n_cols = slice(c * GROUP, (c + 1) * GROUP)
+                    banks = []
+                    for name in ("w3", "w1"):
+                        pool = psum_1 if name == "w1" else psum_3
+                        bank = pool.tile([P, PACK * GROUP], F32, name=f"{name}_bank", tag=f"{name}_bank")
+                        for t in range(PACK):
+                            m_cols = slice(t * P, (t + 1) * P)
+                            nc.tensor.matmul_mx(
+                                out=bank[:, t * GROUP : (t + 1) * GROUP],
+                                lhsT=w_codes[name, h][:, m_cols].bitcast(FP8X4),
+                                lhsT_scale=w_scales[name, h][:, m_cols],
+                                rhs=x_codes[s][:, n_cols].bitcast(FP8X4),
+                                rhs_scale=x_scales[s][:, n_cols],
+                                start=True,
+                                stop=True,
+                            )
+                        banks.append(bank)
+                    gate = work.tile([P, GROUP * PACK], F32, name="gate")
+                    in_quads = "p (t c i) -> p c t i"
+                    nc.scalar.activation(
+                        gate[:].rearrange("p (c t i) -> p c t i", t=PACK, i=RUN),
+                        banks[1][:].rearrange(in_quads, t=PACK, i=RUN),
+                        Sigmoid,
+                    )
+                    into = hidden[:, c * GROUP * PACK : (c + 1) * GROUP * PACK]
+                    nc.vector.tensor_tensor(
+                        into.rearrange("p (c i t) -> p c t i", t=PACK, i=RUN),
+                        gate[:].rearrange("p (c t i) -> p c t i", t=PACK, i=RUN),
+                        banks[0][:].rearrange(in_quads, t=PACK, i=RUN),
+                        mult,
+                    )
+                    for job in pending:
+                        job()
+                    pending.clear()
+                    if (h, s, c) == (0, 0, 2):
+                        load_b()
+                    if (h, s, c) == (0, 2, 0):
+                        quantize_w("w1", 1, later[0])
+                    if (h, s, c) == (0, 2, 2):
+                        quantize_w("w3", 1, later[1])
+                        load_w2()
+                    done = (c + 1) * GROUP
+                    if done in ends:
+                        start = ([0] + ends)[ends.index(done)]
+                        pending.append(partial(finish, h, s, hidden, start, done))
+        for job in pending:
+            job()

@@ -11,6 +11,7 @@ PACK = 4
 F32 = mybir.dt.float32
 BF16 = mybir.dt.bfloat16
 U32 = mybir.dt.uint32
+I32 = mybir.dt.int32
 U16 = mybir.dt.uint16
 U8 = mybir.dt.uint8
 FP8X4 = mybir.dt.float8_e4m3fn_x4
@@ -39,7 +40,6 @@ def tile_picked_pick_glu_sigmoid_sub_e_kernel(tc, xT, w1, w3, w2, offs, out):
         psum_3 = ctx.enter_context(tc.psum_pool(name="psum_3", bufs=4))
 
         offsets = keep.tile([P, S // 16], U16, name="offsets")
-        nc.sync.dma_start(offsets[:], offs)
 
         warm = keep.tile([P, 8], F32, name="warm")
         nc.vector.memset(warm[:], 0.0)
@@ -48,6 +48,7 @@ def tile_picked_pick_glu_sigmoid_sub_e_kernel(tc, xT, w1, w3, w2, offs, out):
         x_rows = xT.rearrange("(p j) t -> p j t", j=PACK)
         pairs = [keep.tile([P, 2 * T], BF16, align_bytes=64, name=f"pairs{u}") for u in range(2)]
         picked = [keep.tile([P, SLICE * PACK], BF16, align_bytes=64, name=f"picked{s}") for s in range(slices)]
+        halves_of = [keep.tile([P, 2 * SLICE], U32, align_bytes=64, name=f"words{s}") for s in range(slices)]
         x_codes = [keep.tile([P, SLICE], U32, align_bytes=64, name=f"x_codes{s}") for s in range(slices)]
         x_scales = [keep.tile([P, SLICE], U8, align_bytes=64, name=f"x_scales{s}") for s in range(slices)]
 
@@ -65,13 +66,22 @@ def tile_picked_pick_glu_sigmoid_sub_e_kernel(tc, xT, w1, w3, w2, offs, out):
                     nc.scalar.activation(dst, src, Copy)
 
         def gather(u, s):
-            words = picked[s][:].bitcast(U32).rearrange("p (n u) -> p n u", u=2)
             window = pairs[u][:].bitcast(U32)
             cols = offsets[:, s * (SLICE // 16) : (s + 1) * (SLICE // 16)]
-            nc.vector.tensor_copy(words[:, :, u], window.indirect(cols))
+            nc.vector.tensor_copy(halves_of[s][:, u * SLICE : (u + 1) * SLICE], window.indirect(cols))
+
+        def weave(s, engine):
+            dst = picked[s][:].bitcast(U32).rearrange("p (n u) -> p n u", u=2)
+            src = halves_of[s][:].rearrange("p (u n) -> p n u", u=2)
+            if engine == "V":
+                nc.vector.tensor_copy(dst.bitcast(I32), src.bitcast(I32))
+            else:
+                nc.scalar.copy(dst, src)
 
         for i in range(4):
             load_x(0, i * CHUNK, CHUNK, "SV"[i % 2])
+            if i == 0:
+                nc.sync.dma_start(offsets[:], offs)
         load_x(1, 0, CHUNK, "S")
         gather(0, 0)
         load_x(1, CHUNK, CHUNK, "V")
@@ -101,6 +111,25 @@ def tile_picked_pick_glu_sigmoid_sub_e_kernel(tc, xT, w1, w3, w2, offs, out):
                     nc.gpsimd.tensor_scalar(dst[:, t], src[:, t], 1.0, 0.0, mult, add)
             return grouped
 
+        def load_w_pieces(name, w, h, pieces):
+            rows = w.rearrange("(p j) c -> p j c", j=PACK)
+            grouped = keep.tile([P, HALF * PACK], BF16, align_bytes=64, name=f"{name}_grouped{h}")
+            whole = grouped[:].rearrange("p (t q r j) -> p t q j r", t=PACK, r=RUN, j=PACK)
+            c0 = 0
+            for width, shares in pieces:
+                raw = stage.tile([P, PACK, width], F32, name="raw")
+                nc.sync.dma_start(out=raw[:], in_=rows[:, :, h * HALF + c0 : h * HALF + c0 + width])
+                src = raw[:].rearrange("p j (q t r) -> p t q j r", t=PACK, r=RUN)
+                q0 = c0 // (PACK * RUN)
+                dst = whole[:, :, q0 : q0 + width // (PACK * RUN)]
+                for engine, t0, t1 in shares:
+                    if engine == "S":
+                        nc.scalar.copy(dst[:, t0:t1], src[:, t0:t1])
+                    else:
+                        nc.vector.tensor_copy(dst[:, t0:t1], src[:, t0:t1])
+                c0 += width
+            return grouped
+
         def quantize_w(name, h, grouped):
             codes = keep.tile([P, HALF], U32, align_bytes=64, name=f"{name}_codes{h}")
             scales = keep.tile([P, HALF], U8, align_bytes=64, name=f"{name}_scales{h}")
@@ -113,14 +142,13 @@ def tile_picked_pick_glu_sigmoid_sub_e_kernel(tc, xT, w1, w3, w2, offs, out):
 
         gather(1, 0)
         gather(1, 1)
-        quantize_x(0)
+        weave(0, "V")
         gather(1, 2)
-        quantize_x(1)
-        w3a = load_w("w3", w3, 0, "SSSS")
-        w1a = load_w("w1", w1, 0, "SSVS")
-        quantize_w("w3", 0, w3a)
-        quantize_x(2)
+        quantize_x(0)
+        w1a = load_w_pieces("w1", w1, 0, [(256, [("S", 0, 4)]), (256, [("S", 0, 4)])])
         quantize_w("w1", 0, w1a)
+        w3a = load_w_pieces("w3", w3, 0, [(256, [("S", 0, 4)]), (256, [("S", 0, 2), ("V", 2, 4)])])
+        quantize_w("w3", 0, w3a)
 
         later = []
 
@@ -186,7 +214,7 @@ def tile_picked_pick_glu_sigmoid_sub_e_kernel(tc, xT, w1, w3, w2, offs, out):
                 for c in range(SLICE // GROUP):
                     n_cols = slice(c * GROUP, (c + 1) * GROUP)
                     banks = []
-                    for name in ("w3", "w1"):
+                    for name in ("w1", "w3"):
                         pool = psum_1 if name == "w1" else psum_3
                         bank = pool.tile([P, PACK * GROUP], F32, name=f"{name}_bank", tag=f"{name}_bank")
                         for t in range(PACK):
@@ -205,19 +233,22 @@ def tile_picked_pick_glu_sigmoid_sub_e_kernel(tc, xT, w1, w3, w2, offs, out):
                     in_quads = "p (t c i) -> p c t i"
                     nc.scalar.activation(
                         gate[:].rearrange("p (c t i) -> p c t i", t=PACK, i=RUN),
-                        banks[1][:].rearrange(in_quads, t=PACK, i=RUN),
+                        banks[0][:].rearrange(in_quads, t=PACK, i=RUN),
                         Sigmoid,
                     )
                     into = hidden[:, c * GROUP * PACK : (c + 1) * GROUP * PACK]
                     nc.vector.tensor_tensor(
                         into.rearrange("p (c i t) -> p c t i", t=PACK, i=RUN),
                         gate[:].rearrange("p (c t i) -> p c t i", t=PACK, i=RUN),
-                        banks[0][:].rearrange(in_quads, t=PACK, i=RUN),
+                        banks[1][:].rearrange(in_quads, t=PACK, i=RUN),
                         mult,
                     )
                     for job in pending:
                         job()
                     pending.clear()
+                    if h == 0 and s + 1 < slices and c == 0:
+                        weave(s + 1, "S")
+                        pending.append(partial(quantize_x, s + 1))
                     if (h, s, c) == (0, 0, 2):
                         load_b()
                     if (h, s, c) == (0, 2, 0):

@@ -33,9 +33,7 @@ def tile_picked_pick_glu_sigmoid_sub_e_kernel(tc, xT, w1, w3, w2, offs, out):
     halves = H // HALF
     with ExitStack() as ctx:
         keep = ctx.enter_context(tc.tile_pool(name="keep", bufs=1))
-        stage = ctx.enter_context(tc.tile_pool(name="stage", bufs=8))
         work = ctx.enter_context(tc.tile_pool(name="work", bufs=4))
-        res = ctx.enter_context(tc.tile_pool(name="res", bufs=3))
         psum_1 = ctx.enter_context(tc.psum_pool(name="psum_1", bufs=4))
         psum_3 = ctx.enter_context(tc.psum_pool(name="psum_3", bufs=4))
 
@@ -52,18 +50,15 @@ def tile_picked_pick_glu_sigmoid_sub_e_kernel(tc, xT, w1, w3, w2, offs, out):
         x_codes = [keep.tile([P, SLICE], U32, align_bytes=64, name=f"x_codes{s}") for s in range(slices)]
         x_scales = [keep.tile([P, SLICE], U8, align_bytes=64, name=f"x_scales{s}") for s in range(slices)]
 
-        def load_x(u, t0, width, engines):
-            raw = stage.tile([P, 2, width], F32, name="raw")
+        def load_x(u, t0, width, on_scalar):
+            raw = keep.tile([P, 2, width], F32, name=f"x_raw{u}_{t0}")
             nc.sync.dma_start(out=raw[:], in_=x_rows[:, 2 * u : 2 * u + 2, t0 : t0 + width])
-            part = width // len(engines)
-            for i, engine in enumerate(engines):
-                a = t0 + i * part
-                dst = pairs[u][:, 2 * a : 2 * (a + part)].rearrange("p (t e) -> p t e", e=2)
-                src = raw[:, :, i * part : (i + 1) * part].rearrange("p e t -> p t e")
-                if engine == "V":
-                    nc.vector.tensor_copy(dst, src)
-                else:
-                    nc.scalar.activation(dst, src, Copy)
+            dst = pairs[u][:, 2 * t0 : 2 * (t0 + width)].rearrange("p (t e) -> p t e", e=2)
+            src = raw[:].rearrange("p e t -> p t e")
+            if on_scalar > 0:
+                nc.scalar.copy(dst[:, :on_scalar], src[:, :on_scalar])
+            if on_scalar < width:
+                nc.vector.tensor_copy(dst[:, on_scalar:], src[:, on_scalar:])
 
         def gather(u, s):
             window = pairs[u][:].bitcast(U32)
@@ -78,38 +73,35 @@ def tile_picked_pick_glu_sigmoid_sub_e_kernel(tc, xT, w1, w3, w2, offs, out):
             else:
                 nc.scalar.copy(dst, src)
 
-        for i in range(4):
-            load_x(0, i * CHUNK, CHUNK, "SV"[i % 2])
-            if i == 0:
-                nc.sync.dma_start(offsets[:], offs)
-        load_x(1, 0, CHUNK, "S")
-        gather(0, 0)
-        load_x(1, CHUNK, CHUNK, "V")
-        gather(0, 1)
-        load_x(1, 2 * CHUNK, CHUNK, "S")
-        gather(0, 2)
-        load_x(1, 3 * CHUNK, CHUNK // 2, "VS")
-        load_x(1, 3 * CHUNK + CHUNK // 2, CHUNK // 2, "V")
+        load_x(0, 0, 2048, 1024)
+        nc.sync.dma_start(offsets[:], offs)
+        load_x(0, 2048, 2048, 768)
+        for s in range(slices):
+            gather(0, s)
+        load_x(1, 0, 2048, 1024)
+        load_x(1, 2048, 1024, 512)
+        load_x(1, 3072, 768, 256)
+        load_x(1, 3840, 256, 0)
 
         w_codes = {}
         w_scales = {}
 
-        def load_w(name, w, h, engines):
-            raw = stage.tile([P, PACK, HALF], F32, name="raw")
+        def load_w(name, w, h):
+            raw = keep.tile([P, PACK, HALF], F32, name=f"{name}_raw{h}")
             rows = w.rearrange("(p j) c -> p j c", j=PACK)
             nc.sync.dma_start(out=raw[:], in_=rows[:, :, h * HALF : (h + 1) * HALF])
             grouped = keep.tile([P, HALF * PACK], BF16, align_bytes=64, name=f"{name}_grouped{h}")
-            for t, engine in enumerate(engines):
-                order = "p t q r j" if engine == "G" else "p t q j r"
-                src = raw[:].rearrange("p j (q t r) -> " + order, t=PACK, r=RUN)
-                dst = grouped[:].rearrange("p (t q r j) -> " + order, t=PACK, r=RUN, j=PACK)
-                if engine == "S":
-                    nc.scalar.activation(dst[:, t], src[:, t], Copy)
-                elif engine == "V":
-                    nc.vector.tensor_copy(dst[:, t], src[:, t])
-                else:
-                    nc.gpsimd.tensor_scalar(dst[:, t], src[:, t], 1.0, 0.0, mult, add)
-            return grouped
+            return raw, grouped
+
+        def cast_w(loaded, t, engine):
+            raw, grouped = loaded
+            order = "p t q r j" if engine == "G" else "p t q j r"
+            src = raw[:].rearrange("p j (q t r) -> " + order, t=PACK, r=RUN)
+            dst = grouped[:].rearrange("p (t q r j) -> " + order, t=PACK, r=RUN, j=PACK)
+            if engine == "S":
+                nc.scalar.copy(dst[:, t], src[:, t])
+            else:
+                nc.gpsimd.tensor_scalar(dst[:, t], src[:, t], 1.0, 0.0, mult, add)
 
         def load_w_pieces(name, w, h, pieces):
             rows = w.rearrange("(p j) c -> p j c", j=PACK)
@@ -117,7 +109,7 @@ def tile_picked_pick_glu_sigmoid_sub_e_kernel(tc, xT, w1, w3, w2, offs, out):
             whole = grouped[:].rearrange("p (t q r j) -> p t q j r", t=PACK, r=RUN, j=PACK)
             c0 = 0
             for width, shares in pieces:
-                raw = stage.tile([P, PACK, width], F32, name="raw")
+                raw = keep.tile([P, PACK, width], F32, name=f"{name}_raw{h}_{c0}")
                 nc.sync.dma_start(out=raw[:], in_=rows[:, :, h * HALF + c0 : h * HALF + c0 + width])
                 src = raw[:].rearrange("p j (q t r) -> p t q j r", t=PACK, r=RUN)
                 q0 = c0 // (PACK * RUN)
@@ -150,11 +142,12 @@ def tile_picked_pick_glu_sigmoid_sub_e_kernel(tc, xT, w1, w3, w2, offs, out):
         w3a = load_w_pieces("w3", w3, 0, [(256, [("S", 0, 4)]), (256, [("S", 0, 2), ("V", 2, 4)])])
         quantize_w("w3", 0, w3a)
 
-        later = []
-
-        def load_b():
-            later.append(load_w("w1", w1, 1, "GGGG"))
-            later.append(load_w("w3", w3, 1, "GGGG"))
+        w1b = load_w("w1", w1, 1)
+        w3b = load_w("w3", w3, 1)
+        for t in range(PACK):
+            cast_w(w1b, t, "G")
+        for t in range(2):
+            cast_w(w3b, t, "G")
 
         w2_raw = keep.tile([P, halves, PACK, N], F32, name="w2_raw")
         w2_grouped = keep.tile([P, halves * N * PACK], BF16, align_bytes=64, name="w2_grouped")
@@ -172,7 +165,8 @@ def tile_picked_pick_glu_sigmoid_sub_e_kernel(tc, xT, w1, w3, w2, offs, out):
                     w2_raw[:, g].rearrange("p t m -> p m t"),
                     1.0, 0.0, mult, add,
                 )
-            nc.vector.quantize_mx(out=w2_codes[:].bitcast(FP8X4), scales=w2_scales[:], in_=w2_grouped[:])
+
+        load_w2()
 
         h_codes = {}
         h_scales = {}
@@ -198,7 +192,7 @@ def tile_picked_pick_glu_sigmoid_sub_e_kernel(tc, xT, w1, w3, w2, offs, out):
                     start=(g == 0),
                     stop=(g == halves - 1),
                 )
-            y = res.tile([P, done - start], F32, name="y")
+            y = keep.tile([P, done - start], F32, name=f"y{s}_{start}")
             nc.scalar.copy(y[:], acc[:])
             nc.sync.dma_start(out=out[:, s * SLICE + start : s * SLICE + done], in_=y[:])
 
@@ -210,7 +204,7 @@ def tile_picked_pick_glu_sigmoid_sub_e_kernel(tc, xT, w1, w3, w2, offs, out):
                 h_codes[h, s] = codes
                 h_scales[h, s] = scales
                 last = h == halves - 1 and s == slices - 1
-                ends = [256, 512] if last else [SLICE]
+                ends = [256, 384, 512] if last else [SLICE]
                 for c in range(SLICE // GROUP):
                     n_cols = slice(c * GROUP, (c + 1) * GROUP)
                     banks = []
@@ -249,13 +243,16 @@ def tile_picked_pick_glu_sigmoid_sub_e_kernel(tc, xT, w1, w3, w2, offs, out):
                     if h == 0 and s + 1 < slices and c == 0:
                         weave(s + 1, "S")
                         pending.append(partial(quantize_x, s + 1))
-                    if (h, s, c) == (0, 0, 2):
-                        load_b()
+                    if (h, s, c) == (0, 1, 1):
+                        cast_w(w3b, 2, "S")
+                    if (h, s, c) == (0, 1, 3):
+                        cast_w(w3b, 3, "S")
                     if (h, s, c) == (0, 2, 0):
-                        quantize_w("w1", 1, later[0])
+                        quantize_w("w1", 1, w1b[1])
                     if (h, s, c) == (0, 2, 2):
-                        quantize_w("w3", 1, later[1])
-                        load_w2()
+                        quantize_w("w3", 1, w3b[1])
+                    if (h, s, c) == (1, 0, 2):
+                        nc.vector.quantize_mx(out=w2_codes[:].bitcast(FP8X4), scales=w2_scales[:], in_=w2_grouped[:])
                     done = (c + 1) * GROUP
                     if done in ends:
                         start = ([0] + ends)[ends.index(done)]

@@ -224,17 +224,17 @@ def tile_picked_pick_glu_sigmoid_sub_e_kernel(tc, xT, w1, w3, w2, offs, out):
                             )
                         banks.append(bank)
                     gate = work.tile([P, GROUP * PACK], F32, name="gate")
-                    in_quads = "p (t c i) -> p c t i"
+                    by_token = "p (t c) -> p c t"
                     nc.scalar.activation(
-                        gate[:].rearrange("p (c t i) -> p c t i", t=PACK, i=RUN),
-                        banks[0][:].rearrange(in_quads, t=PACK, i=RUN),
+                        gate[:].rearrange("p (c t) -> p c t", t=PACK),
+                        banks[0][:].rearrange(by_token, t=PACK),
                         Sigmoid,
                     )
                     into = hidden[:, c * GROUP * PACK : (c + 1) * GROUP * PACK]
                     nc.vector.tensor_tensor(
-                        into.rearrange("p (c i t) -> p c t i", t=PACK, i=RUN),
-                        gate[:].rearrange("p (c t i) -> p c t i", t=PACK, i=RUN),
-                        banks[1][:].rearrange(in_quads, t=PACK, i=RUN),
+                        into.rearrange("p (c t) -> p c t", t=PACK),
+                        gate[:].rearrange("p (c t) -> p c t", t=PACK),
+                        banks[1][:].rearrange(by_token, t=PACK),
                         mult,
                     )
                     for job in pending:

@@ -51,7 +51,7 @@ def tile_picked_pick_glu_sigmoid_sub_e_kernel(tc, xT, w1, w3, w2, offs, out):
         x_scales = [keep.tile([P, SLICE], U8, align_bytes=64, name=f"x_scales{s}") for s in range(slices)]
 
         def load_x(u, t0, width, on_scalar):
-            raw = keep.tile([P, 2, width], F32, name=f"x_raw{u}_{t0}")
+            raw = keep.tile([P, 2, width], F32, align_bytes=64, name="raw", tag=f"x_raw{u}_{t0}")
             nc.sync.dma_start(out=raw[:], in_=x_rows[:, 2 * u : 2 * u + 2, t0 : t0 + width])
             dst = pairs[u][:, 2 * t0 : 2 * (t0 + width)].rearrange("p (t e) -> p t e", e=2)
             src = raw[:].rearrange("p e t -> p t e")
@@ -78,6 +78,9 @@ def tile_picked_pick_glu_sigmoid_sub_e_kernel(tc, xT, w1, w3, w2, offs, out):
         load_x(0, 2048, 2048, 768)
         for s in range(slices):
             gather(0, s)
+        warm_codes = keep.tile([P, SLICE], U32, align_bytes=64, name="warm_codes", tag="x_raw0_0")
+        warm_scales = keep.tile([P, SLICE], U8, align_bytes=64, name="warm_scales", tag="x_raw0_2048")
+        nc.vector.quantize_mx(out=warm_codes[:].bitcast(FP8X4), scales=warm_scales[:], in_=pairs[0][:, : SLICE * PACK])
         load_x(1, 0, 2048, 1024)
         load_x(1, 2048, 1024, 512)
         load_x(1, 3072, 768, 256)
@@ -134,6 +137,24 @@ def tile_picked_pick_glu_sigmoid_sub_e_kernel(tc, xT, w1, w3, w2, offs, out):
 
         gather(1, 0)
         gather(1, 1)
+        start_codes = keep.tile([P, P], U32, align_bytes=64, name="start_codes", tag="x_raw1_0")
+        start_scales = keep.tile([P, P], U8, align_bytes=64, name="start_scales")
+        nc.vector.quantize_mx(
+            out=start_codes[:].bitcast(FP8X4),
+            scales=start_scales[:],
+            in_=halves_of[0][:, SLICE : SLICE + P * PACK // 2].bitcast(BF16),
+        )
+        warm_bank = psum_3.tile([P, SLICE], F32, name="warm_bank", tag="w3_bank")
+        for i in range(6):
+            nc.tensor.matmul_mx(
+                out=warm_bank[:],
+                lhsT=start_codes[:].bitcast(FP8X4),
+                lhsT_scale=start_scales[:],
+                rhs=warm_codes[:].bitcast(FP8X4),
+                rhs_scale=warm_scales[:],
+                start=True,
+                stop=True,
+            )
         weave(0, "V")
         gather(1, 2)
         quantize_x(0)

@@ -1,5 +1,4 @@
 from contextlib import ExitStack
-from functools import partial
 
 import concourse.mybir as mybir
 
@@ -126,7 +125,7 @@ def tile_picked_pick_glu_sigmoid_sub_e_kernel(tc, xT, w1, w3, w2, offs, out):
             return grouped
 
         def quantize_w(name, h, grouped):
-            codes = keep.tile([P, HALF], U32, align_bytes=64, name=f"{name}_codes{h}")
+            codes = keep.tile([P, HALF], U32, align_bytes=64, name="codes", tag=f"{name}_codes{h}")
             scales = keep.tile([P, HALF], U8, align_bytes=64, name=f"{name}_scales{h}")
             nc.vector.quantize_mx(out=codes[:].bitcast(FP8X4), scales=scales[:], in_=grouped[:])
             w_codes[name, h] = codes
@@ -171,30 +170,24 @@ def tile_picked_pick_glu_sigmoid_sub_e_kernel(tc, xT, w1, w3, w2, offs, out):
             cast_w(w3b, t, "G")
 
         w2_raw = keep.tile([P, halves, PACK, N], F32, name="w2_raw")
-        w2_grouped = keep.tile([P, halves * N * PACK], BF16, align_bytes=64, name="w2_grouped")
         w2_codes = keep.tile([P, halves * N], U32, align_bytes=64, name="w2_codes")
         w2_scales = keep.tile([P, halves * N], U8, align_bytes=64, name="w2_scales")
         w2_rows = w2.rearrange("(g q t r) m -> g t q r m", g=halves, t=PACK, r=RUN)
 
-        def load_w2():
-            for g in range(halves):
-                for t in range(PACK):
-                    nc.sync.dma_start(out=w2_raw[:, g, t, :], in_=w2_rows[g, t])
-            for g in range(halves):
-                nc.gpsimd.tensor_scalar(
-                    w2_grouped[:, g * N * PACK : (g + 1) * N * PACK].rearrange("p (m t) -> p m t", t=PACK),
-                    w2_raw[:, g].rearrange("p t m -> p m t"),
-                    1.0, 0.0, mult, add,
-                )
-
-        load_w2()
+        for g in range(halves):
+            for t in range(PACK):
+                nc.sync.dma_start(out=w2_raw[:, g, t, :], in_=w2_rows[g, t])
 
         h_codes = {}
         h_scales = {}
-        pending = []
+        hiddens = {}
+        handed_on = {8: "w1_codes1", 9: "h_codes0_0", 10: "h_codes0_1", 11: "w2_grouped"}
 
-        def finish(h, s, hidden, start, done):
+        def finish(h, s, start, done):
             n_cols = slice(start, done)
+            hidden = hiddens[h, s]
+            if start == 0:
+                h_codes[h, s] = keep.tile([P, SLICE], U32, align_bytes=64, name="h_codes", tag=f"h_codes{h}_{s}")
             nc.vector.quantize_mx(
                 out=h_codes[h, s][:, n_cols].bitcast(FP8X4),
                 scales=h_scales[h, s][:, n_cols],
@@ -220,12 +213,8 @@ def tile_picked_pick_glu_sigmoid_sub_e_kernel(tc, xT, w1, w3, w2, offs, out):
         for h in range(halves):
             for s in range(slices):
                 hidden = work.tile([P, SLICE * PACK], BF16, align_bytes=64, name="hidden")
-                codes = keep.tile([P, SLICE], U32, align_bytes=64, name=f"h_codes{h}_{s}")
-                scales = keep.tile([P, SLICE], U8, align_bytes=64, name=f"h_scales{h}_{s}")
-                h_codes[h, s] = codes
-                h_scales[h, s] = scales
-                last = h == halves - 1 and s == slices - 1
-                ends = [256, 384, 512] if last else [SLICE]
+                hiddens[h, s] = hidden
+                h_scales[h, s] = keep.tile([P, SLICE], U8, align_bytes=64, name=f"h_scales{h}_{s}")
                 for c in range(SLICE // GROUP):
                     n_cols = slice(c * GROUP, (c + 1) * GROUP)
                     banks = []
@@ -244,7 +233,11 @@ def tile_picked_pick_glu_sigmoid_sub_e_kernel(tc, xT, w1, w3, w2, offs, out):
                                 stop=True,
                             )
                         banks.append(bank)
-                    gate = work.tile([P, GROUP * PACK], F32, name="gate")
+                    step = (h * slices + s) * (SLICE // GROUP) + c
+                    if step in handed_on:
+                        gate = keep.tile([P, GROUP * PACK], F32, align_bytes=64, name="gate", tag=handed_on[step])
+                    else:
+                        gate = work.tile([P, GROUP * PACK], F32, name="gate")
                     by_token = "p (t c) -> p c t"
                     nc.scalar.activation(
                         gate[:].rearrange("p (c t) -> p c t", t=PACK),
@@ -258,25 +251,36 @@ def tile_picked_pick_glu_sigmoid_sub_e_kernel(tc, xT, w1, w3, w2, offs, out):
                         banks[1][:].rearrange(by_token, t=PACK),
                         mult,
                     )
-                    for job in pending:
-                        job()
-                    pending.clear()
-                    if h == 0 and s + 1 < slices and c == 0:
+                    if step in (0, 4):
                         weave(s + 1, "S")
-                        pending.append(partial(quantize_x, s + 1))
-                    if (h, s, c) == (0, 1, 1):
-                        cast_w(w3b, 2, "S")
-                    if (h, s, c) == (0, 1, 3):
-                        cast_w(w3b, 3, "S")
-                    if (h, s, c) == (0, 2, 0):
+                    if step in (1, 5):
+                        quantize_x(s + 1)
+                    if step in (5, 7):
+                        cast_w(w3b, 2 + (step - 5) // 2, "S")
+                    if step == 9:
                         quantize_w("w1", 1, w1b[1])
-                    if (h, s, c) == (0, 2, 2):
+                    if step == 10:
+                        finish(0, 0, 0, SLICE)
+                    if step == 11:
                         quantize_w("w3", 1, w3b[1])
-                    if (h, s, c) == (1, 0, 2):
+                        finish(0, 1, 0, SLICE)
+                        w2_grouped = keep.tile(
+                            [P, halves * N * PACK], BF16, align_bytes=64, name="w2_grouped", tag="w2_grouped"
+                        )
+                        nc.scalar.copy(
+                            w2_grouped[:].rearrange("p (g m t) -> p g m t", g=halves, t=PACK),
+                            w2_raw[:].rearrange("p g t m -> p g m t"),
+                        )
+                    if step == 12:
+                        finish(0, 2, 0, SLICE)
+                    if step == 14:
                         nc.vector.quantize_mx(out=w2_codes[:].bitcast(FP8X4), scales=w2_scales[:], in_=w2_grouped[:])
-                    done = (c + 1) * GROUP
-                    if done in ends:
-                        start = ([0] + ends)[ends.index(done)]
-                        pending.append(partial(finish, h, s, hidden, start, done))
-        for job in pending:
-            job()
+                    if step == 16:
+                        finish(1, 0, 0, SLICE)
+                    if step == 20:
+                        finish(1, 1, 0, SLICE)
+                    if step == 22:
+                        finish(1, 2, 0, 256)
+                    if step == 23:
+                        finish(1, 2, 256, 384)
+                        finish(1, 2, 384, 512)

@@ -10,30 +10,30 @@ PACK = 4
 F32 = mybir.dt.float32
 BF16 = mybir.dt.bfloat16
 U32 = mybir.dt.uint32
-I32 = mybir.dt.int32
 U16 = mybir.dt.uint16
 U8 = mybir.dt.uint8
 FP8X4 = mybir.dt.float8_e4m3fn_x4
 Copy = mybir.ActivationFunctionType.Copy
 Sigmoid = mybir.ActivationFunctionType.Sigmoid
 mult = mybir.AluOpType.mult
-add = mybir.AluOpType.add
 
-CHUNK = 1024
 SLICE = 512
 GROUP = 128
 RUN = 2
 HALF = 512
+SCALAR_SLICE = 1
 
 
 def tile_picked_pick_glu_sigmoid_sub_e_kernel(tc, xT, w1, w3, w2, offs, out):
     nc = tc.nc
     slices = S // SLICE
     halves = H // HALF
+    groups = SLICE // GROUP
     with ExitStack() as ctx:
         keep = ctx.enter_context(tc.tile_pool(name="keep", bufs=1))
         work = ctx.enter_context(tc.tile_pool(name="work", bufs=4))
-        psum_1 = ctx.enter_context(tc.psum_pool(name="psum_1", bufs=4))
+        psum_1 = ctx.enter_context(tc.psum_pool(name="psum_1", bufs=3))
+        psum_y = ctx.enter_context(tc.psum_pool(name="psum_y", bufs=1))
         psum_3 = ctx.enter_context(tc.psum_pool(name="psum_3", bufs=4))
 
         offsets = keep.tile([P, S // 16], U16, name="offsets")
@@ -43,159 +43,120 @@ def tile_picked_pick_glu_sigmoid_sub_e_kernel(tc, xT, w1, w3, w2, offs, out):
         nc.scalar.activation(warm[:, 0:1], warm[:, 0:1], Sigmoid)
 
         x_rows = xT.rearrange("(p j) t -> p j t", j=PACK)
-        pairs = [keep.tile([P, 2 * T], BF16, align_bytes=64, name=f"pairs{u}") for u in range(2)]
+        pairs = keep.tile([P, 2 * T], BF16, align_bytes=64, name="pairs")
+        planes = {j: keep.tile([P, T], F32, align_bytes=64, name=f"plane{j}") for j in (2, 3)}
         picked = [keep.tile([P, SLICE * PACK], BF16, align_bytes=64, name=f"picked{s}") for s in range(slices)]
-        halves_of = [keep.tile([P, 2 * SLICE], U32, align_bytes=64, name=f"words{s}") for s in range(slices)]
-        x_codes = [keep.tile([P, SLICE], U32, align_bytes=64, name=f"x_codes{s}") for s in range(slices)]
+        late_rows = keep.tile([P, 2 * SLICE], BF16, align_bytes=64, name="late_rows")
+        x_codes = {}
         x_scales = [keep.tile([P, SLICE], U8, align_bytes=64, name=f"x_scales{s}") for s in range(slices)]
 
-        def load_x(u, t0, width, on_scalar):
-            raw = keep.tile([P, 2, width], F32, align_bytes=64, name="raw", tag=f"x_raw{u}_{t0}")
-            nc.sync.dma_start(out=raw[:], in_=x_rows[:, 2 * u : 2 * u + 2, t0 : t0 + width])
-            dst = pairs[u][:, 2 * t0 : 2 * (t0 + width)].rearrange("p (t e) -> p t e", e=2)
+        def entries(s):
+            return offsets[:, s * (SLICE // 16) : (s + 1) * (SLICE // 16)]
+
+        def load_pairs(t0, width, on_scalar):
+            raw = keep.tile([P, 2, width], F32, align_bytes=64, name="raw", tag=f"x_raw{t0}")
+            nc.sync.dma_start(out=raw[:], in_=x_rows[:, 0:2, t0 : t0 + width])
+            dst = pairs[:, 2 * t0 : 2 * (t0 + width)].rearrange("p (t e) -> p t e", e=2)
             src = raw[:].rearrange("p e t -> p t e")
-            if on_scalar > 0:
-                nc.scalar.copy(dst[:, :on_scalar], src[:, :on_scalar])
-            if on_scalar < width:
-                nc.vector.tensor_copy(dst[:, on_scalar:], src[:, on_scalar:])
+            nc.scalar.copy(dst[:, :on_scalar], src[:, :on_scalar])
+            nc.vector.tensor_copy(dst[:, on_scalar:], src[:, on_scalar:])
 
-        def gather(u, s):
-            window = pairs[u][:].bitcast(U32)
-            cols = offsets[:, s * (SLICE // 16) : (s + 1) * (SLICE // 16)]
-            nc.vector.tensor_copy(halves_of[s][:, u * SLICE : (u + 1) * SLICE], window.indirect(cols))
+        def gather_pairs(s):
+            words = picked[s][:].bitcast(U32).rearrange("p (n u) -> p n u", u=2)
+            nc.vector.tensor_copy(words[:, :, 0], pairs[:].bitcast(U32).indirect(entries(s)))
 
-        def weave(s, engine):
-            dst = picked[s][:].bitcast(U32).rearrange("p (n u) -> p n u", u=2)
-            src = halves_of[s][:].rearrange("p (u n) -> p n u", u=2)
-            if engine == "V":
-                nc.vector.tensor_copy(dst.bitcast(I32), src.bitcast(I32))
+        def gather_plane(j, s):
+            window = planes[j][:].indirect(entries(s))
+            if s == SCALAR_SLICE:
+                nc.scalar.activation(late_rows[:, (j - 2) * SLICE : (j - 1) * SLICE], window, Copy)
             else:
-                nc.scalar.copy(dst, src)
+                nc.vector.tensor_copy(picked[s][:].rearrange("p (n j) -> p n j", j=PACK)[:, :, j], window)
 
-        load_x(0, 0, 2048, 1024)
+        def quantize_x(s, tag):
+            x_codes[s] = keep.tile([P, SLICE], U32, align_bytes=64, name="x_codes", tag=tag)
+            nc.vector.quantize_mx(out=x_codes[s][:].bitcast(FP8X4), scales=x_scales[s][:], in_=picked[s][:])
+
+        load_pairs(0, 2048, 1024)
         nc.sync.dma_start(offsets[:], offs)
-        load_x(0, 2048, 2048, 768)
+        load_pairs(2048, 1024, 512)
+        load_pairs(3072, 1024, 384)
         for s in range(slices):
-            gather(0, s)
-        warm_codes = keep.tile([P, SLICE], U32, align_bytes=64, name="warm_codes", tag="x_raw0_0")
-        warm_scales = keep.tile([P, SLICE], U8, align_bytes=64, name="warm_scales", tag="x_raw0_2048")
-        nc.vector.quantize_mx(out=warm_codes[:].bitcast(FP8X4), scales=warm_scales[:], in_=pairs[0][:, : SLICE * PACK])
-        load_x(1, 0, 2048, 1024)
-        load_x(1, 2048, 1024, 512)
-        load_x(1, 3072, 768, 256)
-        load_x(1, 3840, 256, 0)
+            gather_pairs(s)
+        for j in (2, 3):
+            nc.sync.dma_start(out=planes[j][:], in_=x_rows[:, j, :])
+            for s in range(slices):
+                gather_plane(j, s)
+        nc.scalar.copy(
+            picked[SCALAR_SLICE][:].rearrange("p (n j) -> p n j", j=PACK)[:, :, 2:4],
+            late_rows[:].rearrange("p (e n) -> p n e", e=2),
+        )
 
         w_codes = {}
         w_scales = {}
 
         def load_w(name, w, h):
-            raw = keep.tile([P, PACK, HALF], F32, name=f"{name}_raw{h}")
+            raw = keep.tile([P, PACK, HALF], F32, align_bytes=64, name="raw", tag=f"{name}_raw{h}")
             rows = w.rearrange("(p j) c -> p j c", j=PACK)
             nc.sync.dma_start(out=raw[:], in_=rows[:, :, h * HALF : (h + 1) * HALF])
             grouped = keep.tile([P, HALF * PACK], BF16, align_bytes=64, name=f"{name}_grouped{h}")
             return raw, grouped
 
-        def cast_w(loaded, t, engine):
+        def cast_w(loaded, t0, t1, engine):
             raw, grouped = loaded
-            order = "p t q r j" if engine == "G" else "p t q j r"
-            src = raw[:].rearrange("p j (q t r) -> " + order, t=PACK, r=RUN)
-            dst = grouped[:].rearrange("p (t q r j) -> " + order, t=PACK, r=RUN, j=PACK)
+            src = raw[:].rearrange("p j (q t r) -> p t q j r", t=PACK, r=RUN)
+            dst = grouped[:].rearrange("p (t q r j) -> p t q j r", t=PACK, r=RUN, j=PACK)
             if engine == "S":
-                nc.scalar.copy(dst[:, t], src[:, t])
+                nc.scalar.copy(dst[:, t0:t1], src[:, t0:t1])
             else:
-                nc.gpsimd.tensor_scalar(dst[:, t], src[:, t], 1.0, 0.0, mult, add)
+                nc.vector.tensor_copy(dst[:, t0:t1], src[:, t0:t1])
 
-        def load_w_pieces(name, w, h, pieces):
-            rows = w.rearrange("(p j) c -> p j c", j=PACK)
-            grouped = keep.tile([P, HALF * PACK], BF16, align_bytes=64, name=f"{name}_grouped{h}")
-            whole = grouped[:].rearrange("p (t q r j) -> p t q j r", t=PACK, r=RUN, j=PACK)
-            c0 = 0
-            for width, shares in pieces:
-                raw = keep.tile([P, PACK, width], F32, name=f"{name}_raw{h}_{c0}")
-                nc.sync.dma_start(out=raw[:], in_=rows[:, :, h * HALF + c0 : h * HALF + c0 + width])
-                src = raw[:].rearrange("p j (q t r) -> p t q j r", t=PACK, r=RUN)
-                q0 = c0 // (PACK * RUN)
-                dst = whole[:, :, q0 : q0 + width // (PACK * RUN)]
-                for engine, t0, t1 in shares:
-                    if engine == "S":
-                        nc.scalar.copy(dst[:, t0:t1], src[:, t0:t1])
-                    else:
-                        nc.vector.tensor_copy(dst[:, t0:t1], src[:, t0:t1])
-                c0 += width
-            return grouped
-
-        def quantize_w(name, h, grouped):
-            codes = keep.tile([P, HALF], U32, align_bytes=64, name="codes", tag=f"{name}_codes{h}")
+        def quantize_w(name, h, loaded):
+            codes = keep.tile([P, HALF], U32, align_bytes=64, name=f"{name}_codes{h}")
             scales = keep.tile([P, HALF], U8, align_bytes=64, name=f"{name}_scales{h}")
-            nc.vector.quantize_mx(out=codes[:].bitcast(FP8X4), scales=scales[:], in_=grouped[:])
+            nc.vector.quantize_mx(out=codes[:].bitcast(FP8X4), scales=scales[:], in_=loaded[1][:])
             w_codes[name, h] = codes
             w_scales[name, h] = scales
 
-        def quantize_x(s):
-            nc.vector.quantize_mx(out=x_codes[s][:].bitcast(FP8X4), scales=x_scales[s][:], in_=picked[s][:])
-
-        gather(1, 0)
-        gather(1, 1)
-        start_codes = keep.tile([P, P], U32, align_bytes=64, name="start_codes", tag="x_raw1_0")
-        start_scales = keep.tile([P, P], U8, align_bytes=64, name="start_scales")
-        nc.vector.quantize_mx(
-            out=start_codes[:].bitcast(FP8X4),
-            scales=start_scales[:],
-            in_=halves_of[0][:, SLICE : SLICE + P * PACK // 2].bitcast(BF16),
-        )
-        warm_bank = psum_3.tile([P, SLICE], F32, name="warm_bank", tag="w3_bank")
-        for i in range(6):
-            nc.tensor.matmul_mx(
-                out=warm_bank[:],
-                lhsT=start_codes[:].bitcast(FP8X4),
-                lhsT_scale=start_scales[:],
-                rhs=warm_codes[:].bitcast(FP8X4),
-                rhs_scale=warm_scales[:],
-                start=True,
-                stop=True,
-            )
-        weave(0, "V")
-        gather(1, 2)
-        quantize_x(0)
-        w1a = load_w_pieces("w1", w1, 0, [(256, [("S", 0, 4)]), (256, [("S", 0, 4)])])
-        quantize_w("w1", 0, w1a)
-        w3a = load_w_pieces("w3", w3, 0, [(256, [("S", 0, 4)]), (256, [("S", 0, 2), ("V", 2, 4)])])
-        quantize_w("w3", 0, w3a)
-
+        w1a = load_w("w1", w1, 0)
+        w3a = load_w("w3", w3, 0)
         w1b = load_w("w1", w1, 1)
         w3b = load_w("w3", w3, 1)
-        for t in range(PACK):
-            cast_w(w1b, t, "G")
-        for t in range(2):
-            cast_w(w3b, t, "G")
-
         w2_raw = keep.tile([P, halves, PACK, N], F32, name="w2_raw")
+        w2_grouped = keep.tile([P, halves * N * PACK], BF16, align_bytes=64, name="w2_grouped")
         w2_codes = keep.tile([P, halves * N], U32, align_bytes=64, name="w2_codes")
         w2_scales = keep.tile([P, halves * N], U8, align_bytes=64, name="w2_scales")
         w2_rows = w2.rearrange("(g q t r) m -> g t q r m", g=halves, t=PACK, r=RUN)
-
         for g in range(halves):
             for t in range(PACK):
                 nc.sync.dma_start(out=w2_raw[:, g, t, :], in_=w2_rows[g, t])
 
+        quantize_x(0, "x_codes0")
+        cast_w(w1a, 0, 3, "S")
+        cast_w(w1a, 3, 4, "V")
+        quantize_w("w1", 0, w1a)
+        cast_w(w3a, 0, 2, "S")
+        cast_w(w3a, 2, 4, "V")
+        quantize_x(1, "w1_raw0")
+        quantize_w("w3", 0, w3a)
+        quantize_x(2, "w3_raw0")
+
         h_codes = {}
         h_scales = {}
         hiddens = {}
-        handed_on = {8: "w1_codes1", 9: "h_codes0_0", 10: "h_codes0_1", 11: "w2_grouped"}
 
         def finish(h, s, start, done):
             n_cols = slice(start, done)
-            hidden = hiddens[h, s]
-            if start == 0:
-                h_codes[h, s] = keep.tile([P, SLICE], U32, align_bytes=64, name="h_codes", tag=f"h_codes{h}_{s}")
             nc.vector.quantize_mx(
                 out=h_codes[h, s][:, n_cols].bitcast(FP8X4),
                 scales=h_scales[h, s][:, n_cols],
-                in_=hidden[:, start * PACK : done * PACK],
+                in_=hiddens[h, s][:, start * PACK : done * PACK],
             )
             if h < halves - 1:
                 return
-            acc = psum_1.tile([P, done - start], F32, name="acc", tag="w1_bank")
+            if done - start == SLICE:
+                acc = psum_y.tile([P, SLICE], F32, name="acc")
+            else:
+                acc = psum_1.tile([P, done - start], F32, name="acc", tag="w1_bank")
             for g in range(halves):
                 nc.tensor.matmul_mx(
                     out=acc[:],
@@ -212,10 +173,11 @@ def tile_picked_pick_glu_sigmoid_sub_e_kernel(tc, xT, w1, w3, w2, offs, out):
 
         for h in range(halves):
             for s in range(slices):
-                hidden = work.tile([P, SLICE * PACK], BF16, align_bytes=64, name="hidden")
+                hidden = work.tile([P, SLICE * PACK], BF16, align_bytes=64, name="hidden", bufs=2)
                 hiddens[h, s] = hidden
+                h_codes[h, s] = keep.tile([P, SLICE], U32, align_bytes=64, name=f"h_codes{h}_{s}")
                 h_scales[h, s] = keep.tile([P, SLICE], U8, align_bytes=64, name=f"h_scales{h}_{s}")
-                for c in range(SLICE // GROUP):
+                for c in range(groups):
                     n_cols = slice(c * GROUP, (c + 1) * GROUP)
                     banks = []
                     for name in ("w1", "w3"):
@@ -233,11 +195,8 @@ def tile_picked_pick_glu_sigmoid_sub_e_kernel(tc, xT, w1, w3, w2, offs, out):
                                 stop=True,
                             )
                         banks.append(bank)
-                    step = (h * slices + s) * (SLICE // GROUP) + c
-                    if step in handed_on:
-                        gate = keep.tile([P, GROUP * PACK], F32, align_bytes=64, name="gate", tag=handed_on[step])
-                    else:
-                        gate = work.tile([P, GROUP * PACK], F32, name="gate")
+                    step = (h * slices + s) * groups + c
+                    gate = work.tile([P, GROUP * PACK], F32, name="gate")
                     by_token = "p (t c) -> p c t"
                     nc.scalar.activation(
                         gate[:].rearrange("p (c t) -> p c t", t=PACK),
@@ -251,36 +210,29 @@ def tile_picked_pick_glu_sigmoid_sub_e_kernel(tc, xT, w1, w3, w2, offs, out):
                         banks[1][:].rearrange(by_token, t=PACK),
                         mult,
                     )
-                    if step in (0, 4):
-                        weave(s + 1, "S")
-                    if step in (1, 5):
-                        quantize_x(s + 1)
-                    if step in (5, 7):
-                        cast_w(w3b, 2 + (step - 5) // 2, "S")
+                    if step in (2, 3):
+                        cast_w(w1b, step - 2, step - 1, "S")
+                    if step == 2:
+                        cast_w(w1b, 2, 4, "V")
+                    if step == 5:
+                        quantize_w("w1", 1, w1b)
+                    if step in (5, 6, 7):
+                        cast_w(w3b, step - 5, step - 4, "S")
+                    if step == 6:
+                        cast_w(w3b, 3, 4, "V")
                     if step == 9:
-                        quantize_w("w1", 1, w1b[1])
-                    if step == 10:
-                        finish(0, 0, 0, SLICE)
-                    if step == 11:
-                        quantize_w("w3", 1, w3b[1])
-                        finish(0, 1, 0, SLICE)
-                        w2_grouped = keep.tile(
-                            [P, halves * N * PACK], BF16, align_bytes=64, name="w2_grouped", tag="w2_grouped"
-                        )
+                        quantize_w("w3", 1, w3b)
+                    if step == 12:
                         nc.scalar.copy(
                             w2_grouped[:].rearrange("p (g m t) -> p g m t", g=halves, t=PACK),
                             w2_raw[:].rearrange("p g t m -> p g m t"),
                         )
-                    if step == 12:
-                        finish(0, 2, 0, SLICE)
                     if step == 14:
                         nc.vector.quantize_mx(out=w2_codes[:].bitcast(FP8X4), scales=w2_scales[:], in_=w2_grouped[:])
-                    if step == 16:
-                        finish(1, 0, 0, SLICE)
-                    if step == 20:
-                        finish(1, 1, 0, SLICE)
                     if step == 22:
                         finish(1, 2, 0, 256)
                     if step == 23:
                         finish(1, 2, 256, 384)
                         finish(1, 2, 384, 512)
+                    elif c == groups - 1:
+                        finish(h, s, 0, SLICE)

@@ -43,32 +43,19 @@ def tile_picked_pick_glu_sigmoid_sub_e_kernel(tc, xT, w1, w3, w2, offs, out):
         nc.scalar.activation(warm[:, 0:1], warm[:, 0:1], Sigmoid)
 
         x_rows = xT.rearrange("(p j) t -> p j t", j=PACK)
-        pairs = keep.tile([P, 2 * T], BF16, align_bytes=64, name="pairs")
-        planes = {j: keep.tile([P, T], F32, align_bytes=64, name=f"plane{j}") for j in (2, 3)}
+        planes = {j: keep.tile([P, T], F32, align_bytes=64, name=f"plane{j}") for j in range(PACK)}
         picked = [keep.tile([P, SLICE * PACK], BF16, align_bytes=64, name=f"picked{s}") for s in range(slices)]
-        late_rows = keep.tile([P, 2 * SLICE], BF16, align_bytes=64, name="late_rows")
+        rows = keep.tile([P, PACK * SLICE], BF16, align_bytes=64, name="rows")
         x_codes = {}
         x_scales = [keep.tile([P, SLICE], U8, align_bytes=64, name=f"x_scales{s}") for s in range(slices)]
 
         def entries(s):
             return offsets[:, s * (SLICE // 16) : (s + 1) * (SLICE // 16)]
 
-        def load_pairs(t0, width, on_scalar):
-            raw = keep.tile([P, 2, width], F32, align_bytes=64, name="raw", tag=f"x_raw{t0}")
-            nc.sync.dma_start(out=raw[:], in_=x_rows[:, 0:2, t0 : t0 + width])
-            dst = pairs[:, 2 * t0 : 2 * (t0 + width)].rearrange("p (t e) -> p t e", e=2)
-            src = raw[:].rearrange("p e t -> p t e")
-            nc.scalar.copy(dst[:, :on_scalar], src[:, :on_scalar])
-            nc.vector.tensor_copy(dst[:, on_scalar:], src[:, on_scalar:])
-
-        def gather_pairs(s):
-            words = picked[s][:].bitcast(U32).rearrange("p (n u) -> p n u", u=2)
-            nc.vector.tensor_copy(words[:, :, 0], pairs[:].bitcast(U32).indirect(entries(s)))
-
         def gather_plane(j, s):
             window = planes[j][:].indirect(entries(s))
             if s == SCALAR_SLICE:
-                nc.scalar.activation(late_rows[:, (j - 2) * SLICE : (j - 1) * SLICE], window, Copy)
+                nc.scalar.activation(rows[:, j * SLICE : (j + 1) * SLICE], window, Copy)
             else:
                 nc.vector.tensor_copy(picked[s][:].rearrange("p (n j) -> p n j", j=PACK)[:, :, j], window)
 
@@ -76,20 +63,17 @@ def tile_picked_pick_glu_sigmoid_sub_e_kernel(tc, xT, w1, w3, w2, offs, out):
             x_codes[s] = keep.tile([P, SLICE], U32, align_bytes=64, name="x_codes", tag=tag)
             nc.vector.quantize_mx(out=x_codes[s][:].bitcast(FP8X4), scales=x_scales[s][:], in_=picked[s][:])
 
-        load_pairs(0, 2048, 1024)
-        nc.sync.dma_start(offsets[:], offs)
-        load_pairs(2048, 1024, 512)
-        load_pairs(3072, 1024, 384)
-        for s in range(slices):
-            gather_pairs(s)
-        for j in (2, 3):
+        for j in range(PACK):
             nc.sync.dma_start(out=planes[j][:], in_=x_rows[:, j, :])
+            if j == 0:
+                nc.sync.dma_start(offsets[:], offs)
             for s in range(slices):
                 gather_plane(j, s)
-        nc.scalar.copy(
-            picked[SCALAR_SLICE][:].rearrange("p (n j) -> p n j", j=PACK)[:, :, 2:4],
-            late_rows[:].rearrange("p (e n) -> p n e", e=2),
-        )
+            if j % 2 == 1:
+                nc.scalar.copy(
+                    picked[SCALAR_SLICE][:].rearrange("p (n j) -> p n j", j=PACK)[:, :, j - 1 : j + 1],
+                    rows[:].rearrange("p (j n) -> p n j", j=PACK)[:, :, j - 1 : j + 1],
+                )
 
         w_codes = {}
         w_scales = {}

@@ -16,6 +16,7 @@ FP8X4 = mybir.dt.float8_e4m3fn_x4
 Copy = mybir.ActivationFunctionType.Copy
 Sigmoid = mybir.ActivationFunctionType.Sigmoid
 mult = mybir.AluOpType.mult
+add = mybir.AluOpType.add
 
 SLICE = 512
 GROUP = 128
@@ -44,7 +45,7 @@ def tile_picked_pick_glu_sigmoid_sub_e_kernel(tc, xT, w1, w3, w2, offs, out):
 
         x_rows = xT.rearrange("(p j) t -> p j t", j=PACK)
         planes = {j: keep.tile([P, T], F32, align_bytes=64, name=f"plane{j}") for j in range(PACK)}
-        picked = [keep.tile([P, SLICE * PACK], BF16, align_bytes=64, name=f"picked{s}") for s in range(slices)]
+        picked = [keep.tile([P, SLICE * PACK], BF16, align_bytes=64, name="picked", tag=f"picked{s}") for s in range(slices)]
         rows = keep.tile([P, PACK * SLICE], BF16, align_bytes=64, name="rows")
         x_codes = {}
         x_scales = [keep.tile([P, SLICE], U8, align_bytes=64, name=f"x_scales{s}") for s in range(slices)]
@@ -82,20 +83,26 @@ def tile_picked_pick_glu_sigmoid_sub_e_kernel(tc, xT, w1, w3, w2, offs, out):
             raw = keep.tile([P, PACK, HALF], F32, align_bytes=64, name="raw", tag=f"{name}_raw{h}")
             rows = w.rearrange("(p j) c -> p j c", j=PACK)
             nc.sync.dma_start(out=raw[:], in_=rows[:, :, h * HALF : (h + 1) * HALF])
-            grouped = keep.tile([P, HALF * PACK], BF16, align_bytes=64, name=f"{name}_grouped{h}")
-            return raw, grouped
+            return [raw]
+
+        def make_room(loaded, tag):
+            loaded.append(keep.tile([P, HALF * PACK], BF16, align_bytes=64, name="grouped", tag=tag))
 
         def cast_w(loaded, t0, t1, engine):
             raw, grouped = loaded
-            src = raw[:].rearrange("p j (q t r) -> p t q j r", t=PACK, r=RUN)
-            dst = grouped[:].rearrange("p (t q r j) -> p t q j r", t=PACK, r=RUN, j=PACK)
+            order = "p t q r j" if engine == "G" else "p t q j r"
+            src = raw[:].rearrange("p j (q t r) -> " + order, t=PACK, r=RUN)
+            dst = grouped[:].rearrange("p (t q r j) -> " + order, t=PACK, r=RUN, j=PACK)
             if engine == "S":
                 nc.scalar.copy(dst[:, t0:t1], src[:, t0:t1])
+            elif engine == "G":
+                for t in range(t0, t1):
+                    nc.gpsimd.tensor_scalar(dst[:, t], src[:, t], 1.0, 0.0, mult, add)
             else:
                 nc.vector.tensor_copy(dst[:, t0:t1], src[:, t0:t1])
 
         def quantize_w(name, h, loaded):
-            codes = keep.tile([P, HALF], U32, align_bytes=64, name=f"{name}_codes{h}")
+            codes = keep.tile([P, HALF], U32, align_bytes=64, name="codes", tag=f"{name}_codes{h}")
             scales = keep.tile([P, HALF], U8, align_bytes=64, name=f"{name}_scales{h}")
             nc.vector.quantize_mx(out=codes[:].bitcast(FP8X4), scales=scales[:], in_=loaded[1][:])
             w_codes[name, h] = codes
@@ -114,6 +121,8 @@ def tile_picked_pick_glu_sigmoid_sub_e_kernel(tc, xT, w1, w3, w2, offs, out):
             for t in range(PACK):
                 nc.sync.dma_start(out=w2_raw[:, g, t, :], in_=w2_rows[g, t])
 
+        make_room(w1a, "w1_grouped0")
+        make_room(w3a, "w3_grouped0")
         quantize_x(0, "x_codes0")
         cast_w(w1a, 0, 3, "S")
         cast_w(w1a, 3, 4, "V")
@@ -124,12 +133,18 @@ def tile_picked_pick_glu_sigmoid_sub_e_kernel(tc, xT, w1, w3, w2, offs, out):
         quantize_w("w3", 0, w3a)
         quantize_x(2, "w3_raw0")
 
+        make_room(w1b, "picked2")
+        cast_w(w1b, 0, 4, "G")
+        handed_on = {6: "w3_grouped1", 7: "w1_codes1", 8: "h_codes0_0", 9: "h_codes0_1"}
+
         h_codes = {}
         h_scales = {}
         hiddens = {}
 
         def finish(h, s, start, done):
             n_cols = slice(start, done)
+            if start == 0:
+                h_codes[h, s] = keep.tile([P, SLICE], U32, align_bytes=64, name="h_codes", tag=f"h_codes{h}_{s}")
             nc.vector.quantize_mx(
                 out=h_codes[h, s][:, n_cols].bitcast(FP8X4),
                 scales=h_scales[h, s][:, n_cols],
@@ -157,9 +172,8 @@ def tile_picked_pick_glu_sigmoid_sub_e_kernel(tc, xT, w1, w3, w2, offs, out):
 
         for h in range(halves):
             for s in range(slices):
-                hidden = work.tile([P, SLICE * PACK], BF16, align_bytes=64, name="hidden", bufs=2)
+                hidden = keep.tile([P, SLICE * PACK], BF16, align_bytes=64, name="hidden", tag=f"hidden{s}")
                 hiddens[h, s] = hidden
-                h_codes[h, s] = keep.tile([P, SLICE], U32, align_bytes=64, name=f"h_codes{h}_{s}")
                 h_scales[h, s] = keep.tile([P, SLICE], U8, align_bytes=64, name=f"h_scales{h}_{s}")
                 for c in range(groups):
                     n_cols = slice(c * GROUP, (c + 1) * GROUP)
@@ -180,7 +194,10 @@ def tile_picked_pick_glu_sigmoid_sub_e_kernel(tc, xT, w1, w3, w2, offs, out):
                             )
                         banks.append(bank)
                     step = (h * slices + s) * groups + c
-                    gate = work.tile([P, GROUP * PACK], F32, name="gate")
+                    if step in handed_on:
+                        gate = keep.tile([P, GROUP * PACK], F32, align_bytes=64, name="gate", tag=handed_on[step])
+                    else:
+                        gate = work.tile([P, GROUP * PACK], F32, name="gate")
                     by_token = "p (t c) -> p c t"
                     nc.scalar.activation(
                         gate[:].rearrange("p (c t) -> p c t", t=PACK),
@@ -194,18 +211,18 @@ def tile_picked_pick_glu_sigmoid_sub_e_kernel(tc, xT, w1, w3, w2, offs, out):
                         banks[1][:].rearrange(by_token, t=PACK),
                         mult,
                     )
-                    if step in (2, 3):
-                        cast_w(w1b, step - 2, step - 1, "S")
-                    if step == 2:
-                        cast_w(w1b, 2, 4, "V")
-                    if step == 5:
+                    if step == 8:
                         quantize_w("w1", 1, w1b)
-                    if step in (5, 6, 7):
-                        cast_w(w3b, step - 5, step - 4, "S")
-                    if step == 6:
-                        cast_w(w3b, 3, 4, "V")
+                        finish(0, 0, 0, SLICE)
                     if step == 9:
+                        finish(0, 1, 0, SLICE)
+                    if step == 10:
+                        make_room(w3b, "w3_grouped1")
+                        cast_w(w3b, 0, 2, "S")
+                        cast_w(w3b, 2, 4, "S")
                         quantize_w("w3", 1, w3b)
+                    if step == 11:
+                        finish(0, 2, 0, SLICE)
                     if step == 12:
                         nc.scalar.copy(
                             w2_grouped[:].rearrange("p (g m t) -> p g m t", g=halves, t=PACK),
@@ -213,10 +230,10 @@ def tile_picked_pick_glu_sigmoid_sub_e_kernel(tc, xT, w1, w3, w2, offs, out):
                         )
                     if step == 14:
                         nc.vector.quantize_mx(out=w2_codes[:].bitcast(FP8X4), scales=w2_scales[:], in_=w2_grouped[:])
+                    if step in (15, 19):
+                        finish(h, s, 0, SLICE)
                     if step == 22:
                         finish(1, 2, 0, 256)
                     if step == 23:
                         finish(1, 2, 256, 384)
                         finish(1, 2, 384, 512)
-                    elif c == groups - 1:
-                        finish(h, s, 0, SLICE)

@@ -70,11 +70,10 @@ def tile_picked_pick_glu_sigmoid_sub_e_kernel(tc, xT, w1, w3, w2, offs, out):
                 nc.sync.dma_start(offsets[:], offs)
             for s in range(slices):
                 gather_plane(j, s)
-            if j % 2 == 1:
-                nc.scalar.copy(
-                    picked[SCALAR_SLICE][:].rearrange("p (n j) -> p n j", j=PACK)[:, :, j - 1 : j + 1],
-                    rows[:].rearrange("p (j n) -> p n j", j=PACK)[:, :, j - 1 : j + 1],
-                )
+            nc.scalar.copy(
+                picked[SCALAR_SLICE][:].rearrange("p (n j) -> p n j", j=PACK)[:, :, j],
+                rows[:, j * SLICE : (j + 1) * SLICE],
+            )
 
         w_codes = {}
         w_scales = {}

@@ -20,8 +20,9 @@ add = mybir.AluOpType.add
 
 SLICE = 512
 GROUP = 128
-RUN = 2
+PAIR = 2
 HALF = 512
+PLACE_SPLIT = 192
 SCALAR_SLICE = 1
 
 
@@ -64,16 +65,18 @@ def tile_picked_pick_glu_sigmoid_sub_e_kernel(tc, xT, w1, w3, w2, offs, out):
             x_codes[s] = keep.tile([P, SLICE], U32, align_bytes=64, name="x_codes", tag=tag)
             nc.vector.quantize_mx(out=x_codes[s][:].bitcast(FP8X4), scales=x_scales[s][:], in_=picked[s][:])
 
+        placed = picked[SCALAR_SLICE][:].rearrange("p (n j) -> p n j", j=PACK)
+        by_entry = rows[:].rearrange("p (j n) -> p n j", j=PACK)
         for j in range(PACK):
             nc.sync.dma_start(out=planes[j][:], in_=x_rows[:, j, :])
             if j == 0:
                 nc.sync.dma_start(offsets[:], offs)
             for s in range(slices):
                 gather_plane(j, s)
-            nc.scalar.copy(
-                picked[SCALAR_SLICE][:].rearrange("p (n j) -> p n j", j=PACK)[:, :, j],
-                rows[:, j * SLICE : (j + 1) * SLICE],
-            )
+            if j == 1:
+                nc.scalar.copy(placed[:, :, 0:2], by_entry[:, :, 0:2])
+        nc.scalar.copy(placed[:, :PLACE_SPLIT, 2:4], by_entry[:, :PLACE_SPLIT, 2:4])
+        nc.gpsimd.tensor_scalar(placed[:, PLACE_SPLIT:, 2:4], by_entry[:, PLACE_SPLIT:, 2:4], 1.0, 0.0, mult, add)
 
         w_codes = {}
         w_scales = {}
@@ -89,16 +92,14 @@ def tile_picked_pick_glu_sigmoid_sub_e_kernel(tc, xT, w1, w3, w2, offs, out):
 
         def cast_w(loaded, t0, t1, engine):
             raw, grouped = loaded
-            order = "p t q r j" if engine == "G" else "p t q j r"
-            src = raw[:].rearrange("p j (q t r) -> " + order, t=PACK, r=RUN)
-            dst = grouped[:].rearrange("p (t q r j) -> " + order, t=PACK, r=RUN, j=PACK)
-            if engine == "S":
-                nc.scalar.copy(dst[:, t0:t1], src[:, t0:t1])
-            elif engine == "G":
-                for t in range(t0, t1):
-                    nc.gpsimd.tensor_scalar(dst[:, t], src[:, t], 1.0, 0.0, mult, add)
-            else:
-                nc.vector.tensor_copy(dst[:, t0:t1], src[:, t0:t1])
+            if engine == "G":
+                src = raw[:].rearrange("p j (m t) -> p m t j", t=PACK)
+                dst = grouped[:].rearrange("p (t m j) -> p m t j", t=PACK, j=PACK)
+                nc.gpsimd.tensor_scalar(dst, src, 1.0, 0.0, mult, add)
+                return
+            src = raw[:].rearrange("p j (m u r) -> p m u j r", u=PACK // PAIR, r=PAIR)
+            dst = grouped[:].rearrange("p (u r m j) -> p m u j r", u=PACK // PAIR, r=PAIR, j=PACK)
+            nc.scalar.copy(dst[:, :, t0 // PAIR : t1 // PAIR], src[:, :, t0 // PAIR : t1 // PAIR])
 
         def quantize_w(name, h, loaded):
             codes = keep.tile([P, HALF], U32, align_bytes=64, name="codes", tag=f"{name}_codes{h}")
@@ -110,47 +111,59 @@ def tile_picked_pick_glu_sigmoid_sub_e_kernel(tc, xT, w1, w3, w2, offs, out):
         w1a = load_w("w1", w1, 0)
         w3a = load_w("w3", w3, 0)
         w1b = load_w("w1", w1, 1)
-        w3b = load_w("w3", w3, 1)
         w2_raw = keep.tile([P, halves, PACK, N], F32, name="w2_raw")
         w2_grouped = keep.tile([P, halves * N * PACK], BF16, align_bytes=64, name="w2_grouped")
-        w2_codes = keep.tile([P, halves * N], U32, align_bytes=64, name="w2_codes")
         w2_scales = keep.tile([P, halves * N], U8, align_bytes=64, name="w2_scales")
-        w2_rows = w2.rearrange("(g q t r) m -> g t q r m", g=halves, t=PACK, r=RUN)
-        for g in range(halves):
-            for t in range(PACK):
-                nc.sync.dma_start(out=w2_raw[:, g, t, :], in_=w2_rows[g, t])
+        w3b = load_w("w3", w3, 1)
+        nc.sync.dma_start(
+            out=w2_raw[:].rearrange("p g t m -> p g (t m)"), in_=w2.rearrange("(g p t) m -> p g (t m)", g=halves, t=PACK)
+        )
 
         make_room(w1a, "w1_grouped0")
-        make_room(w3a, "w3_grouped0")
         quantize_x(0, "x_codes0")
-        cast_w(w1a, 0, 3, "S")
-        cast_w(w1a, 3, 4, "V")
+        quantize_x(2, "x_codes2")
+        cast_w(w1a, 0, 4, "S")
         quantize_w("w1", 0, w1a)
-        cast_w(w3a, 0, 2, "S")
-        cast_w(w3a, 2, 4, "V")
-        quantize_x(1, "w1_raw0")
-        quantize_w("w3", 0, w3a)
-        quantize_x(2, "w3_raw0")
 
-        make_room(w1b, "picked2")
+        w3_codes = keep.tile([P, HALF], U32, align_bytes=64, name="w3_codes0")
+        w3_scales = keep.tile([P, HALF], U8, align_bytes=64, name="w3_scales0")
+        w_codes["w3", 0] = w3_codes
+        w_scales["w3", 0] = w3_scales
+        w3_src = w3a[0][:].rearrange("p j (m u r) -> p u m j r", u=2, r=PAIR)
+        parts = []
+        for part, tag in enumerate(("w3_part0", "w1_grouped0")):
+            grouped = keep.tile([P, HALF * 2], BF16, align_bytes=64, name="part", tag=tag)
+            dst = grouped[:].rearrange("p (r m j) -> p m j r", r=PAIR, j=PACK)
+            if part == 0:
+                nc.scalar.copy(dst, w3_src[:, 0])
+            else:
+                nc.vector.tensor_copy(dst, w3_src[:, 1])
+            parts.append(grouped)
+        for part in range(2):
+            cols = slice(part * 2 * P, (part + 1) * 2 * P)
+            nc.vector.quantize_mx(out=w3_codes[:, cols].bitcast(FP8X4), scales=w3_scales[:, cols], in_=parts[part][:])
+        quantize_x(1, "w3_part0")
+
+        make_room(w1b, "picked1")
         cast_w(w1b, 0, 4, "G")
-        handed_on = {6: "w3_grouped1", 7: "w1_codes1", 8: "h_codes0_0", 9: "h_codes0_1"}
+        handed_on = {4: "w1_codes1", 10: "w3_codes1", 11: "w2_codes", 15: "gate15", 19: "gate19"}
+        w2_codes = []
 
         h_codes = {}
         h_scales = {}
         hiddens = {}
 
-        def finish(h, s, start, done):
-            n_cols = slice(start, done)
-            if start == 0:
-                h_codes[h, s] = keep.tile([P, SLICE], U32, align_bytes=64, name="h_codes", tag=f"h_codes{h}_{s}")
+        def open_h(h, s, tag):
+            h_codes[h, s] = keep.tile([P, SLICE], U32, align_bytes=64, name="h_codes", tag=tag)
+            h_scales[h, s] = keep.tile([P, SLICE], U8, align_bytes=64, name=f"h_scales{h}_{s}")
+
+        def quantize_h(h, s, start, done, values):
             nc.vector.quantize_mx(
-                out=h_codes[h, s][:, n_cols].bitcast(FP8X4),
-                scales=h_scales[h, s][:, n_cols],
-                in_=hiddens[h, s][:, start * PACK : done * PACK],
+                out=h_codes[h, s][:, start:done].bitcast(FP8X4), scales=h_scales[h, s][:, start:done], in_=values
             )
-            if h < halves - 1:
-                return
+
+        def finish(s, start, done):
+            n_cols = slice(start, done)
             if done - start == SLICE:
                 acc = psum_y.tile([P, SLICE], F32, name="acc")
             else:
@@ -158,7 +171,7 @@ def tile_picked_pick_glu_sigmoid_sub_e_kernel(tc, xT, w1, w3, w2, offs, out):
             for g in range(halves):
                 nc.tensor.matmul_mx(
                     out=acc[:],
-                    lhsT=w2_codes[:, g * N : (g + 1) * N].bitcast(FP8X4),
+                    lhsT=w2_codes[0][:, g * N : (g + 1) * N].bitcast(FP8X4),
                     lhsT_scale=w2_scales[:, g * N : (g + 1) * N],
                     rhs=h_codes[g, s][:, n_cols].bitcast(FP8X4),
                     rhs_scale=h_scales[g, s][:, n_cols],
@@ -169,17 +182,19 @@ def tile_picked_pick_glu_sigmoid_sub_e_kernel(tc, xT, w1, w3, w2, offs, out):
             nc.scalar.copy(y[:], acc[:])
             nc.sync.dma_start(out=out[:, s * SLICE + start : s * SLICE + done], in_=y[:])
 
+        width = GROUP * PACK
+        by_token = "p (t c) -> p c t"
+        on_gpsimd = {12: "hidden0_2", 16: "hidden1_0"}
         for h in range(halves):
             for s in range(slices):
-                hidden = keep.tile([P, SLICE * PACK], BF16, align_bytes=64, name="hidden", tag=f"hidden{s}")
+                hidden = keep.tile([P, SLICE * PACK], BF16, align_bytes=64, name="hidden", tag=f"hidden{h}_{s}")
                 hiddens[h, s] = hidden
-                h_scales[h, s] = keep.tile([P, SLICE], U8, align_bytes=64, name=f"h_scales{h}_{s}")
                 for c in range(groups):
                     n_cols = slice(c * GROUP, (c + 1) * GROUP)
                     banks = []
                     for name in ("w1", "w3"):
                         pool = psum_1 if name == "w1" else psum_3
-                        bank = pool.tile([P, PACK * GROUP], F32, name=f"{name}_bank", tag=f"{name}_bank")
+                        bank = pool.tile([P, width], F32, name=f"{name}_bank", tag=f"{name}_bank")
                         for t in range(PACK):
                             m_cols = slice(t * P, (t + 1) * P)
                             nc.tensor.matmul_mx(
@@ -194,45 +209,55 @@ def tile_picked_pick_glu_sigmoid_sub_e_kernel(tc, xT, w1, w3, w2, offs, out):
                         banks.append(bank)
                     step = (h * slices + s) * groups + c
                     if step in handed_on:
-                        gate = keep.tile([P, GROUP * PACK], F32, align_bytes=64, name="gate", tag=handed_on[step])
+                        gate = keep.tile([P, width], F32, align_bytes=64, name="gate", tag=handed_on[step])
                     else:
-                        gate = work.tile([P, GROUP * PACK], F32, name="gate")
-                    by_token = "p (t c) -> p c t"
+                        gate = work.tile([P, width], F32, name="gate")
                     nc.scalar.activation(
-                        gate[:].rearrange("p (c t) -> p c t", t=PACK),
-                        banks[0][:].rearrange(by_token, t=PACK),
-                        Sigmoid,
+                        gate[:].rearrange("p (c t) -> p c t", t=PACK), banks[0][:].rearrange(by_token, t=PACK), Sigmoid
                     )
-                    into = hidden[:, c * GROUP * PACK : (c + 1) * GROUP * PACK]
-                    nc.vector.tensor_tensor(
-                        into.rearrange("p (c t) -> p c t", t=PACK),
-                        gate[:].rearrange("p (c t) -> p c t", t=PACK),
-                        banks[1][:].rearrange(by_token, t=PACK),
-                        mult,
-                    )
-                    if step == 8:
+                    if step in on_gpsimd:
+                        up = keep.tile([P, width], F32, name=f"up{step}")
+                        nc.scalar.copy(up[:].rearrange("p (c t) -> p c t", t=PACK), banks[1][:].rearrange(by_token, t=PACK))
+                        first = keep.tile([P, width], BF16, align_bytes=64, name="first", tag=on_gpsimd[step])
+                        nc.gpsimd.tensor_tensor(first[:], gate[:], up[:], mult)
+                    else:
+                        nc.vector.tensor_tensor(
+                            hidden[:, c * width : (c + 1) * width].rearrange("p (c t) -> p c t", t=PACK),
+                            gate[:].rearrange("p (c t) -> p c t", t=PACK),
+                            banks[1][:].rearrange(by_token, t=PACK),
+                            mult,
+                        )
+                    if step == 4:
                         quantize_w("w1", 1, w1b)
-                        finish(0, 0, 0, SLICE)
+                        open_h(0, 0, "picked1")
+                        quantize_h(0, 0, 0, SLICE, hiddens[0, 0][:])
+                        make_room(w3b, "hidden0_0")
+                        cast_w(w3b, 0, 4, "G")
                     if step == 9:
-                        finish(0, 1, 0, SLICE)
-                    if step == 10:
-                        make_room(w3b, "w3_grouped1")
-                        cast_w(w3b, 0, 2, "S")
-                        cast_w(w3b, 2, 4, "S")
-                        quantize_w("w3", 1, w3b)
-                    if step == 11:
-                        finish(0, 2, 0, SLICE)
-                    if step == 12:
                         nc.scalar.copy(
                             w2_grouped[:].rearrange("p (g m t) -> p g m t", g=halves, t=PACK),
                             w2_raw[:].rearrange("p g t m -> p g m t"),
                         )
-                    if step == 14:
-                        nc.vector.quantize_mx(out=w2_codes[:].bitcast(FP8X4), scales=w2_scales[:], in_=w2_grouped[:])
+                    if step == 10:
+                        quantize_w("w3", 1, w3b)
+                        open_h(0, 1, "hidden0_0")
+                        quantize_h(0, 1, 0, SLICE, hiddens[0, 1][:])
+                    if step == 11:
+                        w2_codes.append(keep.tile([P, halves * N], U32, align_bytes=64, name="w2_codes", tag="w2_codes"))
+                        nc.vector.quantize_mx(out=w2_codes[0][:].bitcast(FP8X4), scales=w2_scales[:], in_=w2_grouped[:])
+                        open_h(0, 2, "h_codes0_2")
+                        quantize_h(0, 2, 0, SLICE, hidden[:])
                     if step in (15, 19):
-                        finish(h, s, 0, SLICE)
+                        open_h(1, s, f"gate{step}")
+                        quantize_h(1, s, 0, GROUP, first[:])
+                        quantize_h(1, s, GROUP, SLICE, hidden[:, width:])
+                        finish(s, 0, SLICE)
                     if step == 22:
-                        finish(1, 2, 0, 256)
+                        open_h(1, 2, "h_codes1_2")
+                        quantize_h(1, 2, 0, 256, hidden[:, : 2 * width])
+                        finish(2, 0, 256)
                     if step == 23:
-                        finish(1, 2, 256, 384)
-                        finish(1, 2, 384, 512)
+                        quantize_h(1, 2, 256, 384, hidden[:, 2 * width : 3 * width])
+                        finish(2, 256, 384)
+                        quantize_h(1, 2, 384, 512, hidden[:, 3 * width :])
+                        finish(2, 384, 512)

@@ -23,6 +23,7 @@ GROUP = 128
 PAIR = 2
 HALF = 512
 PLACE_SPLIT = 192
+WARM_PASSES = 4
 SCALAR_SLICE = 1
 
 
@@ -122,6 +123,17 @@ def tile_picked_pick_glu_sigmoid_sub_e_kernel(tc, xT, w1, w3, w2, offs, out):
         make_room(w1a, "w1_grouped0")
         quantize_x(0, "x_codes0")
         quantize_x(2, "x_codes2")
+        idle = psum_y.tile([P, SLICE], F32, name="acc")
+        for i in range(WARM_PASSES):
+            nc.tensor.matmul_mx(
+                out=idle[:],
+                lhsT=x_codes[0][:, :P].bitcast(FP8X4),
+                lhsT_scale=x_scales[0][:, :P],
+                rhs=x_codes[0][:].bitcast(FP8X4),
+                rhs_scale=x_scales[0][:],
+                start=True,
+                stop=True,
+            )
         cast_w(w1a, 0, 4, "S")
         quantize_w("w1", 0, w1a)
 

@@ -158,7 +158,7 @@ def tile_picked_pick_glu_sigmoid_sub_e_kernel(tc, xT, w1, w3, w2, offs, out):
 
         make_room(w1b, "picked1")
         cast_w(w1b, 0, 4, "G")
-        handed_on = {4: "w1_codes1", 10: "w3_codes1", 11: "w2_codes", 15: "gate15", 19: "gate19"}
+        handed_on = {4: "w1_codes1", 10: "w3_codes1", 11: "w2_codes", 16: "h_codes1_0", 20: "h_codes1_1"}
         w2_codes = []
 
         h_codes = {}
@@ -196,7 +196,6 @@ def tile_picked_pick_glu_sigmoid_sub_e_kernel(tc, xT, w1, w3, w2, offs, out):
 
         width = GROUP * PACK
         by_token = "p (t c) -> p c t"
-        on_gpsimd = {12: "hidden0_2", 16: "hidden1_0"}
         for h in range(halves):
             for s in range(slices):
                 hidden = keep.tile([P, SLICE * PACK], BF16, align_bytes=64, name="hidden", tag=f"hidden{h}_{s}")
@@ -227,18 +226,12 @@ def tile_picked_pick_glu_sigmoid_sub_e_kernel(tc, xT, w1, w3, w2, offs, out):
                     nc.scalar.activation(
                         gate[:].rearrange("p (c t) -> p c t", t=PACK), banks[0][:].rearrange(by_token, t=PACK), Sigmoid
                     )
-                    if step in on_gpsimd:
-                        up = keep.tile([P, width], F32, name=f"up{step}")
-                        nc.scalar.copy(up[:].rearrange("p (c t) -> p c t", t=PACK), banks[1][:].rearrange(by_token, t=PACK))
-                        first = keep.tile([P, width], BF16, align_bytes=64, name="first", tag=on_gpsimd[step])
-                        nc.gpsimd.tensor_tensor(first[:], gate[:], up[:], mult)
-                    else:
-                        nc.vector.tensor_tensor(
-                            hidden[:, c * width : (c + 1) * width].rearrange("p (c t) -> p c t", t=PACK),
-                            gate[:].rearrange("p (c t) -> p c t", t=PACK),
-                            banks[1][:].rearrange(by_token, t=PACK),
-                            mult,
-                        )
+                    nc.vector.tensor_tensor(
+                        hidden[:, c * width : (c + 1) * width].rearrange("p (c t) -> p c t", t=PACK),
+                        gate[:].rearrange("p (c t) -> p c t", t=PACK),
+                        banks[1][:].rearrange(by_token, t=PACK),
+                        mult,
+                    )
                     if step == 4:
                         quantize_w("w1", 1, w1b)
                         open_h(0, 0, "picked1")
@@ -259,11 +252,10 @@ def tile_picked_pick_glu_sigmoid_sub_e_kernel(tc, xT, w1, w3, w2, offs, out):
                         nc.vector.quantize_mx(out=w2_codes[0][:].bitcast(FP8X4), scales=w2_scales[:], in_=w2_grouped[:])
                         open_h(0, 2, "h_codes0_2")
                         quantize_h(0, 2, 0, SLICE, hidden[:])
-                    if step in (15, 19):
-                        open_h(1, s, f"gate{step}")
-                        quantize_h(1, s, 0, GROUP, first[:])
-                        quantize_h(1, s, GROUP, SLICE, hidden[:, width:])
-                        finish(s, 0, SLICE)
+                    if step in (16, 20):
+                        open_h(1, s - 1, f"h_codes1_{s - 1}")
+                        quantize_h(1, s - 1, 0, SLICE, hiddens[1, s - 1][:])
+                        finish(s - 1, 0, SLICE)
                     if step == 22:
                         open_h(1, 2, "h_codes1_2")
                         quantize_h(1, 2, 0, 256, hidden[:, : 2 * width])

@@ -23,7 +23,7 @@ GROUP = 128
 PAIR = 2
 HALF = 512
 PLACE_SPLIT = 192
-WARM_PASSES = 4
+WARM_PASSES = 2
 SCALAR_SLICE = 1
 
 
@@ -98,9 +98,10 @@ def tile_picked_pick_glu_sigmoid_sub_e_kernel(tc, xT, w1, w3, w2, offs, out):
                 dst = grouped[:].rearrange("p (t m j) -> p m t j", t=PACK, j=PACK)
                 nc.gpsimd.tensor_scalar(dst, src, 1.0, 0.0, mult, add)
                 return
-            src = raw[:].rearrange("p j (m u r) -> p m u j r", u=PACK // PAIR, r=PAIR)
-            dst = grouped[:].rearrange("p (u r m j) -> p m u j r", u=PACK // PAIR, r=PAIR, j=PACK)
-            nc.scalar.copy(dst[:, :, t0 // PAIR : t1 // PAIR], src[:, :, t0 // PAIR : t1 // PAIR])
+            src = raw[:].rearrange("p j (q t r) -> p t q j r", t=PACK, r=PAIR)
+            dst = grouped[:].rearrange("p (t q r j) -> p t q j r", t=PACK, r=PAIR, j=PACK)
+            copy = nc.scalar.copy if engine == "S" else nc.vector.tensor_copy
+            copy(dst[:, t0:t1], src[:, t0:t1])
 
         def quantize_w(name, h, loaded):
             codes = keep.tile([P, HALF], U32, align_bytes=64, name="codes", tag=f"{name}_codes{h}")
@@ -113,16 +114,17 @@ def tile_picked_pick_glu_sigmoid_sub_e_kernel(tc, xT, w1, w3, w2, offs, out):
         w3a = load_w("w3", w3, 0)
         w1b = load_w("w1", w1, 1)
         w2_raw = keep.tile([P, halves, PACK, N], F32, name="w2_raw")
-        w2_grouped = keep.tile([P, halves * N * PACK], BF16, align_bytes=64, name="w2_grouped")
         w2_scales = keep.tile([P, halves * N], U8, align_bytes=64, name="w2_scales")
         w3b = load_w("w3", w3, 1)
+        w2_first = w2[:HALF].rearrange("(q t r) m -> t q r m", t=PACK, r=PAIR)
+        for t in range(PACK):
+            nc.sync.dma_start(out=w2_raw[:, 0, t, :], in_=w2_first[t])
         nc.sync.dma_start(
-            out=w2_raw[:].rearrange("p g t m -> p g (t m)"), in_=w2.rearrange("(g p t) m -> p g (t m)", g=halves, t=PACK)
+            out=w2_raw[:, 1].rearrange("p t m -> p (t m)"), in_=w2[HALF:].rearrange("(p t) m -> p (t m)", t=PACK)
         )
 
         make_room(w1a, "w1_grouped0")
         quantize_x(0, "x_codes0")
-        quantize_x(2, "x_codes2")
         idle = psum_y.tile([P, SLICE], F32, name="acc")
         for i in range(WARM_PASSES):
             nc.tensor.matmul_mx(
@@ -134,31 +136,33 @@ def tile_picked_pick_glu_sigmoid_sub_e_kernel(tc, xT, w1, w3, w2, offs, out):
                 start=True,
                 stop=True,
             )
-        cast_w(w1a, 0, 4, "S")
+        cast_w(w1a, 0, 3, "S")
+        cast_w(w1a, 3, 4, "V")
         quantize_w("w1", 0, w1a)
 
         w3_codes = keep.tile([P, HALF], U32, align_bytes=64, name="w3_codes0")
         w3_scales = keep.tile([P, HALF], U8, align_bytes=64, name="w3_scales0")
         w_codes["w3", 0] = w3_codes
         w_scales["w3", 0] = w3_scales
-        w3_src = w3a[0][:].rearrange("p j (m u r) -> p u m j r", u=2, r=PAIR)
+        w3_src = w3a[0][:].rearrange("p j (q t r) -> p t q j r", t=PACK, r=PAIR)
         parts = []
-        for part, tag in enumerate(("w3_part0", "w1_grouped0")):
+        for part, tag in enumerate(("w1_grouped0", "w3_part1")):
             grouped = keep.tile([P, HALF * 2], BF16, align_bytes=64, name="part", tag=tag)
-            dst = grouped[:].rearrange("p (r m j) -> p m j r", r=PAIR, j=PACK)
+            dst = grouped[:].rearrange("p (t q r j) -> p t q j r", t=2, r=PAIR, j=PACK)
             if part == 0:
-                nc.scalar.copy(dst, w3_src[:, 0])
+                nc.vector.tensor_copy(dst, w3_src[:, 0:2])
             else:
-                nc.vector.tensor_copy(dst, w3_src[:, 1])
+                nc.scalar.copy(dst, w3_src[:, 2:4])
             parts.append(grouped)
+        quantize_x(2, "w1_raw0")
         for part in range(2):
             cols = slice(part * 2 * P, (part + 1) * 2 * P)
             nc.vector.quantize_mx(out=w3_codes[:, cols].bitcast(FP8X4), scales=w3_scales[:, cols], in_=parts[part][:])
-        quantize_x(1, "w3_part0")
+        quantize_x(1, "w3_part1")
 
         make_room(w1b, "picked1")
         cast_w(w1b, 0, 4, "G")
-        handed_on = {4: "w1_codes1", 10: "w3_codes1", 11: "w2_codes", 16: "h_codes1_0", 20: "h_codes1_1"}
+        handed_on = {5: "high", 6: "w1_codes1", 9: "w2_grouped", 10: "w3_codes1", 13: "w2_codes", 16: "h_codes1_0", 20: "h_codes1_1"}
         w2_codes = []
 
         h_codes = {}
@@ -205,7 +209,10 @@ def tile_picked_pick_glu_sigmoid_sub_e_kernel(tc, xT, w1, w3, w2, offs, out):
                     banks = []
                     for name in ("w1", "w3"):
                         pool = psum_1 if name == "w1" else psum_3
-                        bank = pool.tile([P, width], F32, name=f"{name}_bank", tag=f"{name}_bank")
+                        if (name, h, s, c) == ("w1", 0, 0, groups - 1):
+                            bank = psum_y.tile([P, width], F32, name="acc")
+                        else:
+                            bank = pool.tile([P, width], F32, name=f"{name}_bank", tag=f"{name}_bank")
                         for t in range(PACK):
                             m_cols = slice(t * P, (t + 1) * P)
                             nc.tensor.matmul_mx(
@@ -232,24 +239,45 @@ def tile_picked_pick_glu_sigmoid_sub_e_kernel(tc, xT, w1, w3, w2, offs, out):
                         banks[1][:].rearrange(by_token, t=PACK),
                         mult,
                     )
-                    if step == 4:
+                    if step == 8:
+                        high = keep.tile([P, HALF * 2], BF16, align_bytes=64, name="high", tag="high")
+                        nc.scalar.copy(
+                            high[:].rearrange("p (r m j) -> p m j r", r=PAIR, j=PACK),
+                            w3b[0][:].rearrange("p j (m u r) -> p u m j r", u=2, r=PAIR)[:, 1],
+                        )
+                    if step == 6:
                         quantize_w("w1", 1, w1b)
                         open_h(0, 0, "picked1")
                         quantize_h(0, 0, 0, SLICE, hiddens[0, 0][:])
-                        make_room(w3b, "hidden0_0")
-                        cast_w(w3b, 0, 4, "G")
-                    if step == 9:
+                        low = keep.tile([P, HALF * 2], BF16, align_bytes=64, name="low", tag="hidden0_0")
+                        nc.gpsimd.tensor_scalar(
+                            low[:].rearrange("p (t m j) -> p m t j", t=2, j=PACK),
+                            w3b[0][:].rearrange("p j (m t) -> p m t j", t=PACK)[:, :, 0:2],
+                            1.0,
+                            0.0,
+                            mult,
+                            add,
+                        )
+                    if step == 12:
+                        w2_grouped = keep.tile([P, halves * N * PACK], BF16, align_bytes=64, name="w2_grouped", tag="w2_grouped")
                         nc.scalar.copy(
                             w2_grouped[:].rearrange("p (g m t) -> p g m t", g=halves, t=PACK),
                             w2_raw[:].rearrange("p g t m -> p g m t"),
                         )
                     if step == 10:
-                        quantize_w("w3", 1, w3b)
+                        codes = keep.tile([P, HALF], U32, align_bytes=64, name="codes", tag="w3_codes1")
+                        scales = keep.tile([P, HALF], U8, align_bytes=64, name="w3_scales1")
+                        w_codes["w3", 1] = codes
+                        w_scales["w3", 1] = scales
+                        for part, values in enumerate((high, low)):
+                            cols = slice((1 - part) * 2 * P, (2 - part) * 2 * P)
+                            nc.vector.quantize_mx(out=codes[:, cols].bitcast(FP8X4), scales=scales[:, cols], in_=values[:])
                         open_h(0, 1, "hidden0_0")
                         quantize_h(0, 1, 0, SLICE, hiddens[0, 1][:])
-                    if step == 11:
+                    if step == 13:
                         w2_codes.append(keep.tile([P, halves * N], U32, align_bytes=64, name="w2_codes", tag="w2_codes"))
                         nc.vector.quantize_mx(out=w2_codes[0][:].bitcast(FP8X4), scales=w2_scales[:], in_=w2_grouped[:])
+                    if step == 11:
                         open_h(0, 2, "h_codes0_2")
                         quantize_h(0, 2, 0, SLICE, hidden[:])
                     if step in (16, 20):

@@ -34,7 +34,7 @@ def tile_picked_pick_glu_sigmoid_sub_e_kernel(tc, xT, w1, w3, w2, offs, out):
     groups = SLICE // GROUP
     with ExitStack() as ctx:
         keep = ctx.enter_context(tc.tile_pool(name="keep", bufs=1))
-        work = ctx.enter_context(tc.tile_pool(name="work", bufs=4))
+        work = ctx.enter_context(tc.tile_pool(name="work", bufs=8))
         psum_1 = ctx.enter_context(tc.psum_pool(name="psum_1", bufs=3))
         psum_y = ctx.enter_context(tc.psum_pool(name="psum_y", bufs=1))
         psum_3 = ctx.enter_context(tc.psum_pool(name="psum_3", bufs=4))
@@ -162,7 +162,7 @@ def tile_picked_pick_glu_sigmoid_sub_e_kernel(tc, xT, w1, w3, w2, offs, out):
 
         make_room(w1b, "picked1")
         cast_w(w1b, 0, 4, "G")
-        handed_on = {5: "high", 6: "w1_codes1", 9: "w2_grouped", 10: "w3_codes1", 13: "w2_codes", 16: "h_codes1_0", 20: "h_codes1_1"}
+        handed_on = {5: "high", 6: "w1_codes1", 11: "h_codes0_1", 10: "w3_codes1", 17: "w2_codes", 20: "h_codes1_1"}
         w2_codes = []
 
         h_codes = {}
@@ -200,6 +200,15 @@ def tile_picked_pick_glu_sigmoid_sub_e_kernel(tc, xT, w1, w3, w2, offs, out):
 
         width = GROUP * PACK
         by_token = "p (t c) -> p c t"
+        on_gpsimd = {12: "hidden0_2"}
+        late = {}
+        firsts = {}
+
+        def multiply_first(s):
+            gate, up = late[s]
+            firsts[s] = keep.tile([P, width], BF16, align_bytes=64, name="first", tag=on_gpsimd[12 + 4 * s])
+            nc.gpsimd.tensor_tensor(firsts[s][:], gate[:], up[:], mult)
+
         for h in range(halves):
             for s in range(slices):
                 hidden = keep.tile([P, SLICE * PACK], BF16, align_bytes=64, name="hidden", tag=f"hidden{h}_{s}")
@@ -226,19 +235,28 @@ def tile_picked_pick_glu_sigmoid_sub_e_kernel(tc, xT, w1, w3, w2, offs, out):
                             )
                         banks.append(bank)
                     step = (h * slices + s) * groups + c
-                    if step in handed_on:
+                    if step in on_gpsimd:
+                        gate = keep.tile([P, width], F32, name=f"gate{step}")
+                    elif step in handed_on:
                         gate = keep.tile([P, width], F32, align_bytes=64, name="gate", tag=handed_on[step])
                     else:
                         gate = work.tile([P, width], F32, name="gate")
                     nc.scalar.activation(
                         gate[:].rearrange("p (c t) -> p c t", t=PACK), banks[0][:].rearrange(by_token, t=PACK), Sigmoid
                     )
-                    nc.vector.tensor_tensor(
-                        hidden[:, c * width : (c + 1) * width].rearrange("p (c t) -> p c t", t=PACK),
-                        gate[:].rearrange("p (c t) -> p c t", t=PACK),
-                        banks[1][:].rearrange(by_token, t=PACK),
-                        mult,
-                    )
+                    if step in on_gpsimd:
+                        up = keep.tile([P, width], F32, name=f"up{step}")
+                        nc.scalar.copy(up[:].rearrange("p (c t) -> p c t", t=PACK), banks[1][:].rearrange(by_token, t=PACK))
+                        late[s] = (gate, up)
+                        if step == 12:
+                            multiply_first(0)
+                    else:
+                        nc.vector.tensor_tensor(
+                            hidden[:, c * width : (c + 1) * width].rearrange("p (c t) -> p c t", t=PACK),
+                            gate[:].rearrange("p (c t) -> p c t", t=PACK),
+                            banks[1][:].rearrange(by_token, t=PACK),
+                            mult,
+                        )
                     if step == 8:
                         high = keep.tile([P, HALF * 2], BF16, align_bytes=64, name="high", tag="high")
                         nc.scalar.copy(
@@ -258,11 +276,11 @@ def tile_picked_pick_glu_sigmoid_sub_e_kernel(tc, xT, w1, w3, w2, offs, out):
                             mult,
                             add,
                         )
-                    if step == 12:
-                        w2_grouped = keep.tile([P, halves * N * PACK], BF16, align_bytes=64, name="w2_grouped", tag="w2_grouped")
+                    if step == 14:
+                        w2_grouped = keep.tile([P, halves * N * PACK], BF16, align_bytes=64, name="w2_grouped", tag="hidden0_1")
                         nc.scalar.copy(
-                            w2_grouped[:].rearrange("p (g m t) -> p g m t", g=halves, t=PACK),
-                            w2_raw[:].rearrange("p g t m -> p g m t"),
+                            w2_grouped[:].rearrange("p (g m r t) -> p g m t r", g=halves, r=PAIR, t=PACK),
+                            w2_raw[:].rearrange("p g t (m r) -> p g m t r", r=PAIR),
                         )
                     if step == 10:
                         codes = keep.tile([P, HALF], U32, align_bytes=64, name="codes", tag="w3_codes1")
@@ -272,18 +290,23 @@ def tile_picked_pick_glu_sigmoid_sub_e_kernel(tc, xT, w1, w3, w2, offs, out):
                         for part, values in enumerate((high, low)):
                             cols = slice((1 - part) * 2 * P, (2 - part) * 2 * P)
                             nc.vector.quantize_mx(out=codes[:, cols].bitcast(FP8X4), scales=scales[:, cols], in_=values[:])
-                        open_h(0, 1, "hidden0_0")
-                        quantize_h(0, 1, 0, SLICE, hiddens[0, 1][:])
-                    if step == 13:
+                    if step == 17:
                         w2_codes.append(keep.tile([P, halves * N], U32, align_bytes=64, name="w2_codes", tag="w2_codes"))
                         nc.vector.quantize_mx(out=w2_codes[0][:].bitcast(FP8X4), scales=w2_scales[:], in_=w2_grouped[:])
                     if step == 11:
+                        open_h(0, 1, "h_codes0_1")
+                        quantize_h(0, 1, 0, SLICE, hiddens[0, 1][:])
                         open_h(0, 2, "h_codes0_2")
                         quantize_h(0, 2, 0, SLICE, hidden[:])
-                    if step in (16, 20):
-                        open_h(1, s - 1, f"h_codes1_{s - 1}")
-                        quantize_h(1, s - 1, 0, SLICE, hiddens[1, s - 1][:])
-                        finish(s - 1, 0, SLICE)
+                    if step == 17:
+                        open_h(1, 0, "hidden0_1")
+                        quantize_h(1, 0, 0, GROUP, firsts[0][:])
+                        quantize_h(1, 0, GROUP, SLICE, hiddens[1, 0][:, width:])
+                        finish(0, 0, SLICE)
+                    if step == 20:
+                        open_h(1, 1, "h_codes1_1")
+                        quantize_h(1, 1, 0, SLICE, hiddens[1, 1][:])
+                        finish(1, 0, SLICE)
                     if step == 22:
                         open_h(1, 2, "h_codes1_2")
                         quantize_h(1, 2, 0, 256, hidden[:, : 2 * width])

@@ -23,21 +23,38 @@ GROUP = 128
 PAIR = 2
 HALF = 512
 PLACE_SPLIT = 192
-WARM_PASSES = 2
 SCALAR_SLICE = 1
+WARM_PASSES = 2
+GROUPS = SLICE // GROUP
+STEPS = S // GROUP
+WIDTH = GROUP * PACK
+GPSIMD_GROUPS = 2
+W1B_AFTER = 5
+W2_AFTER = 7
+END_AFTER = 19
 
 
 def tile_picked_pick_glu_sigmoid_sub_e_kernel(tc, xT, w1, w3, w2, offs, out):
     nc = tc.nc
     slices = S // SLICE
-    halves = H // HALF
-    groups = SLICE // GROUP
     with ExitStack() as ctx:
         keep = ctx.enter_context(tc.tile_pool(name="keep", bufs=1))
-        work = ctx.enter_context(tc.tile_pool(name="work", bufs=8))
-        psum_1 = ctx.enter_context(tc.psum_pool(name="psum_1", bufs=3))
-        psum_y = ctx.enter_context(tc.psum_pool(name="psum_y", bufs=1))
+        psum_1 = ctx.enter_context(tc.psum_pool(name="psum_1", bufs=4))
         psum_3 = ctx.enter_context(tc.psum_pool(name="psum_3", bufs=4))
+
+        def quantize(codes, scales, values):
+            nc.vector.quantize_mx(out=codes.bitcast(FP8X4), scales=scales, in_=values)
+
+        def multiply(bank, left, left_scales, right, right_scales, start=True, stop=True):
+            nc.tensor.matmul_mx(
+                out=bank,
+                lhsT=left.bitcast(FP8X4),
+                lhsT_scale=left_scales,
+                rhs=right.bitcast(FP8X4),
+                rhs_scale=right_scales,
+                start=start,
+                stop=stop,
+            )
 
         offsets = keep.tile([P, S // 16], U16, name="offsets")
 
@@ -46,17 +63,14 @@ def tile_picked_pick_glu_sigmoid_sub_e_kernel(tc, xT, w1, w3, w2, offs, out):
         nc.scalar.activation(warm[:, 0:1], warm[:, 0:1], Sigmoid)
 
         x_rows = xT.rearrange("(p j) t -> p j t", j=PACK)
-        planes = {j: keep.tile([P, T], F32, align_bytes=64, name=f"plane{j}") for j in range(PACK)}
+        planes = [keep.tile([P, T], F32, align_bytes=64, name="plane", tag=f"plane{j}") for j in range(PACK)]
         picked = [keep.tile([P, SLICE * PACK], BF16, align_bytes=64, name="picked", tag=f"picked{s}") for s in range(slices)]
         rows = keep.tile([P, PACK * SLICE], BF16, align_bytes=64, name="rows")
         x_codes = {}
         x_scales = [keep.tile([P, SLICE], U8, align_bytes=64, name=f"x_scales{s}") for s in range(slices)]
 
-        def entries(s):
-            return offsets[:, s * (SLICE // 16) : (s + 1) * (SLICE // 16)]
-
         def gather_plane(j, s):
-            window = planes[j][:].indirect(entries(s))
+            window = planes[j][:].indirect(offsets[:, s * (SLICE // 16) : (s + 1) * (SLICE // 16)])
             if s == SCALAR_SLICE:
                 nc.scalar.activation(rows[:, j * SLICE : (j + 1) * SLICE], window, Copy)
             else:
@@ -64,7 +78,7 @@ def tile_picked_pick_glu_sigmoid_sub_e_kernel(tc, xT, w1, w3, w2, offs, out):
 
         def quantize_x(s, tag):
             x_codes[s] = keep.tile([P, SLICE], U32, align_bytes=64, name="x_codes", tag=tag)
-            nc.vector.quantize_mx(out=x_codes[s][:].bitcast(FP8X4), scales=x_scales[s][:], in_=picked[s][:])
+            quantize(x_codes[s][:], x_scales[s][:], picked[s][:])
 
         placed = picked[SCALAR_SLICE][:].rearrange("p (n j) -> p n j", j=PACK)
         by_entry = rows[:].rearrange("p (j n) -> p n j", j=PACK)
@@ -79,240 +93,177 @@ def tile_picked_pick_glu_sigmoid_sub_e_kernel(tc, xT, w1, w3, w2, offs, out):
         nc.scalar.copy(placed[:, :PLACE_SPLIT, 2:4], by_entry[:, :PLACE_SPLIT, 2:4])
         nc.gpsimd.tensor_scalar(placed[:, PLACE_SPLIT:, 2:4], by_entry[:, PLACE_SPLIT:, 2:4], 1.0, 0.0, mult, add)
 
+        def load_w(w, h, tag):
+            raw = keep.tile([P, PACK, HALF], F32, align_bytes=64, name="raw", tag=tag)
+            nc.sync.dma_start(out=raw[:], in_=w.rearrange("(p j) c -> p j c", j=PACK)[:, :, h * HALF : (h + 1) * HALF])
+            return raw
+
+        w1a = load_w(w1, 0, "w1a")
+        w3a = load_w(w3, 0, "w3a")
+        w1b = load_w(w1, 1, "w1b")
+        w3b = load_w(w3, 1, "w3b")
+        w2_raw = keep.tile([P, 2, PACK, N], F32, name="w2_raw")
+        for g in range(2):
+            w2_rows = w2[g * HALF : (g + 1) * HALF].rearrange("(q t r) m -> r q t m", t=PACK, r=PAIR)
+            for r in range(PAIR):
+                nc.sync.dma_start(out=w2_raw[r:P:PAIR, g], in_=w2_rows[r])
+
+        def round_places(copy, grouped, raw, t0, t1):
+            src = raw[:].rearrange("p j (q t r) -> p t q j r", t=PACK, r=PAIR)[:, t0:t1]
+            copy(grouped.rearrange("p (t q r j) -> p t q j r", t=t1 - t0, r=PAIR, j=PACK), src)
+
+        def round_on_gpsimd(raw, tag):
+            grouped = keep.tile([P, HALF * PACK], BF16, align_bytes=64, name="grouped", tag=tag)
+            nc.gpsimd.tensor_scalar(
+                grouped[:].rearrange("p (t q r j) -> p q t r j", t=PACK, r=PAIR, j=PACK),
+                raw[:].rearrange("p j (q t r) -> p q t r j", t=PACK, r=PAIR),
+                1.0,
+                0.0,
+                mult,
+                add,
+            )
+            return grouped
+
         w_codes = {}
         w_scales = {}
+        for name in ("w1", "w3"):
+            w_codes[name, 0] = keep.tile([P, HALF], U32, align_bytes=64, name=f"{name}a_codes")
+            w_scales[name, 0] = keep.tile([P, HALF], U8, align_bytes=64, name=f"{name}a_scales")
 
-        def load_w(name, w, h):
-            raw = keep.tile([P, PACK, HALF], F32, align_bytes=64, name="raw", tag=f"{name}_raw{h}")
-            rows = w.rearrange("(p j) c -> p j c", j=PACK)
-            nc.sync.dma_start(out=raw[:], in_=rows[:, :, h * HALF : (h + 1) * HALF])
-            return [raw]
-
-        def make_room(loaded, tag):
-            loaded.append(keep.tile([P, HALF * PACK], BF16, align_bytes=64, name="grouped", tag=tag))
-
-        def cast_w(loaded, t0, t1, engine):
-            raw, grouped = loaded
-            if engine == "G":
-                src = raw[:].rearrange("p j (m t) -> p m t j", t=PACK)
-                dst = grouped[:].rearrange("p (t m j) -> p m t j", t=PACK, j=PACK)
-                nc.gpsimd.tensor_scalar(dst, src, 1.0, 0.0, mult, add)
-                return
-            src = raw[:].rearrange("p j (q t r) -> p t q j r", t=PACK, r=PAIR)
-            dst = grouped[:].rearrange("p (t q r j) -> p t q j r", t=PACK, r=PAIR, j=PACK)
-            copy = nc.scalar.copy if engine == "S" else nc.vector.tensor_copy
-            copy(dst[:, t0:t1], src[:, t0:t1])
-
-        def quantize_w(name, h, loaded):
-            codes = keep.tile([P, HALF], U32, align_bytes=64, name="codes", tag=f"{name}_codes{h}")
-            scales = keep.tile([P, HALF], U8, align_bytes=64, name=f"{name}_scales{h}")
-            nc.vector.quantize_mx(out=codes[:].bitcast(FP8X4), scales=scales[:], in_=loaded[1][:])
-            w_codes[name, h] = codes
-            w_scales[name, h] = scales
-
-        w1a = load_w("w1", w1, 0)
-        w3a = load_w("w3", w3, 0)
-        w1b = load_w("w1", w1, 1)
-        w2_raw = keep.tile([P, halves, PACK, N], F32, name="w2_raw")
-        w2_scales = keep.tile([P, halves * N], U8, align_bytes=64, name="w2_scales")
-        w3b = load_w("w3", w3, 1)
-        w2_first = w2[:HALF].rearrange("(q t r) m -> t q r m", t=PACK, r=PAIR)
-        for t in range(PACK):
-            nc.sync.dma_start(out=w2_raw[:, 0, t, :], in_=w2_first[t])
-        nc.sync.dma_start(
-            out=w2_raw[:, 1].rearrange("p t m -> p (t m)"), in_=w2[HALF:].rearrange("(p t) m -> p (t m)", t=PACK)
-        )
-
-        make_room(w1a, "w1_grouped0")
         quantize_x(0, "x_codes0")
-        idle = psum_y.tile([P, SLICE], F32, name="acc")
+        idle = psum_3.tile([P, SLICE], F32, name="idle", tag="w3_bank")
         for i in range(WARM_PASSES):
-            nc.tensor.matmul_mx(
-                out=idle[:],
-                lhsT=x_codes[0][:, :P].bitcast(FP8X4),
-                lhsT_scale=x_scales[0][:, :P],
-                rhs=x_codes[0][:].bitcast(FP8X4),
-                rhs_scale=x_scales[0][:],
-                start=True,
-                stop=True,
-            )
-        cast_w(w1a, 0, 3, "S")
-        cast_w(w1a, 3, 4, "V")
-        quantize_w("w1", 0, w1a)
+            multiply(idle[:], x_codes[0][:, :P], x_scales[0][:, :P], x_codes[0][:], x_scales[0][:])
+        w1a_grouped = keep.tile([P, HALF * PACK], BF16, align_bytes=64, name="grouped", tag="w1a_grouped")
+        round_places(nc.scalar.copy, w1a_grouped[:, : 3 * HALF], w1a, 0, 3)
+        round_places(nc.vector.tensor_copy, w1a_grouped[:, 3 * HALF :], w1a, 3, 4)
+        quantize(w_codes["w1", 0][:], w_scales["w1", 0][:], w1a_grouped[:])
 
-        w3_codes = keep.tile([P, HALF], U32, align_bytes=64, name="w3_codes0")
-        w3_scales = keep.tile([P, HALF], U8, align_bytes=64, name="w3_scales0")
-        w_codes["w3", 0] = w3_codes
-        w_scales["w3", 0] = w3_scales
-        w3_src = w3a[0][:].rearrange("p j (q t r) -> p t q j r", t=PACK, r=PAIR)
         parts = []
-        for part, tag in enumerate(("w1_grouped0", "w3_part1")):
+        for part, (copy, tag) in enumerate(((nc.vector.tensor_copy, "w1a_grouped"), (nc.scalar.copy, "w3a_part1"))):
             grouped = keep.tile([P, HALF * 2], BF16, align_bytes=64, name="part", tag=tag)
-            dst = grouped[:].rearrange("p (t q r j) -> p t q j r", t=2, r=PAIR, j=PACK)
-            if part == 0:
-                nc.vector.tensor_copy(dst, w3_src[:, 0:2])
-            else:
-                nc.scalar.copy(dst, w3_src[:, 2:4])
+            round_places(copy, grouped[:], w3a, 2 * part, 2 * part + 2)
             parts.append(grouped)
-        quantize_x(2, "w1_raw0")
+        quantize_x(2, "w1a")
         for part in range(2):
             cols = slice(part * 2 * P, (part + 1) * 2 * P)
-            nc.vector.quantize_mx(out=w3_codes[:, cols].bitcast(FP8X4), scales=w3_scales[:, cols], in_=parts[part][:])
-        quantize_x(1, "w3_part1")
+            quantize(w_codes["w3", 0][:, cols], w_scales["w3", 0][:, cols], parts[part][:])
+        quantize_x(1, "w3a_part1")
 
-        make_room(w1b, "picked1")
-        cast_w(w1b, 0, 4, "G")
-        handed_on = {5: "high", 6: "w1_codes1", 11: "h_codes0_1", 10: "w3_codes1", 17: "w2_codes", 20: "h_codes1_1"}
-        w2_codes = []
+        w1b_grouped = round_on_gpsimd(w1b, "picked1")
 
-        h_codes = {}
-        h_scales = {}
-        hiddens = {}
+        holds = {W1B_AFTER: "w1b_scales", W2_AFTER: "w2_grouped", STEPS - 2: "middle_scales", END_AFTER: "end_scales"}
+        by_token = "p (t c) -> p c t"
+        in_order = "p (c t) -> p c t"
+        gate_rows = [keep.tile([P, T], F32, align_bytes=64, name="gates", tag=f"plane{j}") for j in range(slices)]
+        ups = keep.tile([P, GPSIMD_GROUPS * WIDTH], F32, align_bytes=64, name="ups", tag="plane3")
+        hidden = {}
+        late = []
 
-        def open_h(h, s, tag):
-            h_codes[h, s] = keep.tile([P, SLICE], U32, align_bytes=64, name="h_codes", tag=tag)
-            h_scales[h, s] = keep.tile([P, SLICE], U8, align_bytes=64, name=f"h_scales{h}_{s}")
+        def passes(name, h, group, pool):
+            bank = pool.tile([P, WIDTH], F32, name="bank", tag=f"{name}_bank")
+            s, c = divmod(group, GROUPS)
+            n_cols = slice(c * GROUP, (c + 1) * GROUP)
+            for t in range(PACK):
+                m_cols = slice(t * P, (t + 1) * P)
+                multiply(
+                    bank[:, t * GROUP : (t + 1) * GROUP],
+                    w_codes[name, h][:, m_cols],
+                    w_scales[name, h][:, m_cols],
+                    x_codes[s][:, n_cols],
+                    x_scales[s][:, n_cols],
+                )
+            return bank[:].rearrange(by_token, t=PACK)
 
-        def quantize_h(h, s, start, done, values):
-            nc.vector.quantize_mx(
-                out=h_codes[h, s][:, start:done].bitcast(FP8X4), scales=h_scales[h, s][:, start:done], in_=values
-            )
+        def step(h, group):
+            number = h * STEPS + group
+            s, c = divmod(group, GROUPS)
+            if c == 0:
+                hidden[h, s] = keep.tile([P, SLICE * PACK], BF16, align_bytes=64, name="hidden", tag=f"hidden{h}_{s}")
+            if number in holds:
+                gate = keep.tile([P, WIDTH], F32, align_bytes=64, name="gate", tag=holds[number])[:]
+            else:
+                row, place = divmod(number, T // WIDTH)
+                gate = gate_rows[row][:, place * WIDTH : (place + 1) * WIDTH]
+            nc.scalar.activation(gate.rearrange(in_order, t=PACK), passes("w1", h, group, psum_1), Sigmoid)
+            bank = passes("w3", h, group, psum_3)
+            if h == 1 and group < GPSIMD_GROUPS:
+                up = ups[:, group * WIDTH : (group + 1) * WIDTH]
+                nc.scalar.copy(up.rearrange(in_order, t=PACK), bank)
+                late.append((gate, up))
+            else:
+                values = hidden[h, s][:, c * WIDTH : (c + 1) * WIDTH]
+                nc.vector.tensor_tensor(values.rearrange(in_order, t=PACK), gate.rearrange(in_order, t=PACK), bank, mult)
+
+        h_codes = {(h, s): keep.tile([P, SLICE], U32, align_bytes=64, name=f"h_codes{h}_{s}") for h in range(2) for s in range(slices)}
+        w2_codes = keep.tile([P, 2 * N], U32, align_bytes=64, name="w2_codes")
+
+        for group in range(STEPS):
+            step(0, group)
+            if group == W1B_AFTER + 1:
+                w_codes["w1", 1] = keep.tile([P, HALF], U32, align_bytes=64, name="w1b_codes")
+                w_scales["w1", 1] = keep.tile([P, HALF], U8, align_bytes=64, name="scales", tag="w1b_scales")
+                quantize(w_codes["w1", 1][:], w_scales["w1", 1][:], w1b_grouped[:])
+                w3b_grouped = round_on_gpsimd(w3b, "picked1")
+
+        w2_grouped = keep.tile([P, 2 * N * PACK], BF16, align_bytes=64, name="w2_grouped", tag="w2_grouped")
+        nc.scalar.copy(
+            w2_grouped[:].rearrange("p (g m r t) -> p g m t r", g=2, r=PAIR, t=PACK),
+            w2_raw[:].rearrange("p g t (m r) -> p g m t r", r=PAIR),
+        )
+
+        middle = keep.tile([P, HALF + S + 2 * N], U8, align_bytes=64, name="scales", tag="middle_scales")
+        w_codes["w3", 1] = keep.tile([P, HALF], U32, align_bytes=64, name="w3b_codes")
+        w_scales["w3", 1] = middle[:, :HALF]
+        w2_scales = middle[:, HALF + S :]
+        h_scales = {(0, s): middle[:, HALF + s * SLICE : HALF + (s + 1) * SLICE] for s in range(slices)}
+        quantize(w_codes["w3", 1][:], w_scales["w3", 1], w3b_grouped[:])
+        quantize(w2_codes[:], w2_scales, w2_grouped[:])
+        for s in range(slices):
+            quantize(h_codes[0, s][:], h_scales[0, s], hidden[0, s][:])
+
+        firsts = keep.tile([P, GPSIMD_GROUPS * WIDTH], BF16, align_bytes=64, name="firsts", tag=f"hidden0_{slices - 1}")
+        for group in range(END_AFTER + 2 - STEPS):
+            step(1, group)
+            if group < GPSIMD_GROUPS:
+                gate, up = late[group]
+                nc.gpsimd.tensor_tensor(firsts[:, group * WIDTH : (group + 1) * WIDTH], gate, up, mult)
+
+        end = keep.tile([P, S], U8, align_bytes=64, name="scales", tag="end_scales")
+        for s in range(slices):
+            h_scales[1, s] = end[:, s * SLICE : (s + 1) * SLICE]
+
+        def quantize_h(s, start, done, values):
+            quantize(h_codes[1, s][:, start:done], h_scales[1, s][:, start:done], values)
 
         def finish(s, start, done):
-            n_cols = slice(start, done)
-            if done - start == SLICE:
-                acc = psum_y.tile([P, SLICE], F32, name="acc")
-            else:
-                acc = psum_1.tile([P, done - start], F32, name="acc", tag="w1_bank")
-            for g in range(halves):
-                nc.tensor.matmul_mx(
-                    out=acc[:],
-                    lhsT=w2_codes[0][:, g * N : (g + 1) * N].bitcast(FP8X4),
-                    lhsT_scale=w2_scales[:, g * N : (g + 1) * N],
-                    rhs=h_codes[g, s][:, n_cols].bitcast(FP8X4),
-                    rhs_scale=h_scales[g, s][:, n_cols],
+            acc = psum_1.tile([P, done - start], F32, name="acc", tag="w1_bank")
+            for g in range(2):
+                multiply(
+                    acc[:],
+                    w2_codes[:, g * N : (g + 1) * N],
+                    w2_scales[:, g * N : (g + 1) * N],
+                    h_codes[g, s][:, start:done],
+                    h_scales[g, s][:, start:done],
                     start=(g == 0),
-                    stop=(g == halves - 1),
+                    stop=(g == 1),
                 )
             y = keep.tile([P, done - start], F32, name=f"y{s}_{start}")
             nc.scalar.copy(y[:], acc[:])
             nc.sync.dma_start(out=out[:, s * SLICE + start : s * SLICE + done], in_=y[:])
 
-        width = GROUP * PACK
-        by_token = "p (t c) -> p c t"
-        on_gpsimd = {12: "hidden0_2"}
-        late = {}
-        firsts = {}
-
-        def multiply_first(s):
-            gate, up = late[s]
-            firsts[s] = keep.tile([P, width], BF16, align_bytes=64, name="first", tag=on_gpsimd[12 + 4 * s])
-            nc.gpsimd.tensor_tensor(firsts[s][:], gate[:], up[:], mult)
-
-        for h in range(halves):
-            for s in range(slices):
-                hidden = keep.tile([P, SLICE * PACK], BF16, align_bytes=64, name="hidden", tag=f"hidden{h}_{s}")
-                hiddens[h, s] = hidden
-                for c in range(groups):
-                    n_cols = slice(c * GROUP, (c + 1) * GROUP)
-                    banks = []
-                    for name in ("w1", "w3"):
-                        pool = psum_1 if name == "w1" else psum_3
-                        if (name, h, s, c) == ("w1", 0, 0, groups - 1):
-                            bank = psum_y.tile([P, width], F32, name="acc")
-                        else:
-                            bank = pool.tile([P, width], F32, name=f"{name}_bank", tag=f"{name}_bank")
-                        for t in range(PACK):
-                            m_cols = slice(t * P, (t + 1) * P)
-                            nc.tensor.matmul_mx(
-                                out=bank[:, t * GROUP : (t + 1) * GROUP],
-                                lhsT=w_codes[name, h][:, m_cols].bitcast(FP8X4),
-                                lhsT_scale=w_scales[name, h][:, m_cols],
-                                rhs=x_codes[s][:, n_cols].bitcast(FP8X4),
-                                rhs_scale=x_scales[s][:, n_cols],
-                                start=True,
-                                stop=True,
-                            )
-                        banks.append(bank)
-                    step = (h * slices + s) * groups + c
-                    if step in on_gpsimd:
-                        gate = keep.tile([P, width], F32, name=f"gate{step}")
-                    elif step in handed_on:
-                        gate = keep.tile([P, width], F32, align_bytes=64, name="gate", tag=handed_on[step])
-                    else:
-                        gate = work.tile([P, width], F32, name="gate")
-                    nc.scalar.activation(
-                        gate[:].rearrange("p (c t) -> p c t", t=PACK), banks[0][:].rearrange(by_token, t=PACK), Sigmoid
-                    )
-                    if step in on_gpsimd:
-                        up = keep.tile([P, width], F32, name=f"up{step}")
-                        nc.scalar.copy(up[:].rearrange("p (c t) -> p c t", t=PACK), banks[1][:].rearrange(by_token, t=PACK))
-                        late[s] = (gate, up)
-                        if step == 12:
-                            multiply_first(0)
-                    else:
-                        nc.vector.tensor_tensor(
-                            hidden[:, c * width : (c + 1) * width].rearrange("p (c t) -> p c t", t=PACK),
-                            gate[:].rearrange("p (c t) -> p c t", t=PACK),
-                            banks[1][:].rearrange(by_token, t=PACK),
-                            mult,
-                        )
-                    if step == 8:
-                        high = keep.tile([P, HALF * 2], BF16, align_bytes=64, name="high", tag="high")
-                        nc.scalar.copy(
-                            high[:].rearrange("p (r m j) -> p m j r", r=PAIR, j=PACK),
-                            w3b[0][:].rearrange("p j (m u r) -> p u m j r", u=2, r=PAIR)[:, 1],
-                        )
-                    if step == 6:
-                        quantize_w("w1", 1, w1b)
-                        open_h(0, 0, "picked1")
-                        quantize_h(0, 0, 0, SLICE, hiddens[0, 0][:])
-                        low = keep.tile([P, HALF * 2], BF16, align_bytes=64, name="low", tag="hidden0_0")
-                        nc.gpsimd.tensor_scalar(
-                            low[:].rearrange("p (t m j) -> p m t j", t=2, j=PACK),
-                            w3b[0][:].rearrange("p j (m t) -> p m t j", t=PACK)[:, :, 0:2],
-                            1.0,
-                            0.0,
-                            mult,
-                            add,
-                        )
-                    if step == 14:
-                        w2_grouped = keep.tile([P, halves * N * PACK], BF16, align_bytes=64, name="w2_grouped", tag="hidden0_1")
-                        nc.scalar.copy(
-                            w2_grouped[:].rearrange("p (g m r t) -> p g m t r", g=halves, r=PAIR, t=PACK),
-                            w2_raw[:].rearrange("p g t (m r) -> p g m t r", r=PAIR),
-                        )
-                    if step == 10:
-                        codes = keep.tile([P, HALF], U32, align_bytes=64, name="codes", tag="w3_codes1")
-                        scales = keep.tile([P, HALF], U8, align_bytes=64, name="w3_scales1")
-                        w_codes["w3", 1] = codes
-                        w_scales["w3", 1] = scales
-                        for part, values in enumerate((high, low)):
-                            cols = slice((1 - part) * 2 * P, (2 - part) * 2 * P)
-                            nc.vector.quantize_mx(out=codes[:, cols].bitcast(FP8X4), scales=scales[:, cols], in_=values[:])
-                    if step == 17:
-                        w2_codes.append(keep.tile([P, halves * N], U32, align_bytes=64, name="w2_codes", tag="w2_codes"))
-                        nc.vector.quantize_mx(out=w2_codes[0][:].bitcast(FP8X4), scales=w2_scales[:], in_=w2_grouped[:])
-                    if step == 11:
-                        open_h(0, 1, "h_codes0_1")
-                        quantize_h(0, 1, 0, SLICE, hiddens[0, 1][:])
-                        open_h(0, 2, "h_codes0_2")
-                        quantize_h(0, 2, 0, SLICE, hidden[:])
-                    if step == 17:
-                        open_h(1, 0, "hidden0_1")
-                        quantize_h(1, 0, 0, GROUP, firsts[0][:])
-                        quantize_h(1, 0, GROUP, SLICE, hiddens[1, 0][:, width:])
-                        finish(0, 0, SLICE)
-                    if step == 20:
-                        open_h(1, 1, "h_codes1_1")
-                        quantize_h(1, 1, 0, SLICE, hiddens[1, 1][:])
-                        finish(1, 0, SLICE)
-                    if step == 22:
-                        open_h(1, 2, "h_codes1_2")
-                        quantize_h(1, 2, 0, 256, hidden[:, : 2 * width])
-                        finish(2, 0, 256)
-                    if step == 23:
-                        quantize_h(1, 2, 256, 384, hidden[:, 2 * width : 3 * width])
-                        finish(2, 256, 384)
-                        quantize_h(1, 2, 384, 512, hidden[:, 3 * width :])
-                        finish(2, 384, 512)
+        split = GPSIMD_GROUPS * GROUP
+        quantize_h(0, 0, split, firsts[:])
+        quantize_h(0, split, SLICE, hidden[1, 0][:, split * PACK :])
+        finish(0, 0, SLICE)
+        quantize_h(1, 0, SLICE, hidden[1, 1][:])
+        finish(1, 0, SLICE)
+        last = slices - 1
+        for group in range(END_AFTER + 2 - STEPS, 2 * GROUPS + 2 + 1):
+            step(1, group)
+        quantize_h(last, 0, 2 * GROUP, hidden[1, last][:, : 2 * WIDTH])
+        finish(last, 0, 2 * GROUP)
+        step(1, STEPS - 1)
+        for c in (2, 3):
+            quantize_h(last, c * GROUP, (c + 1) * GROUP, hidden[1, last][:, c * WIDTH : (c + 1) * WIDTH])
+            finish(last, c * GROUP, (c + 1) * GROUP)

@@ -29,8 +29,9 @@ GROUPS = SLICE // GROUP
 STEPS = S // GROUP
 WIDTH = GROUP * PACK
 GPSIMD_GROUPS = 2
-W1B_AFTER = 5
-W2_AFTER = 7
+W1B_AFTER = 7
+W3B_AFTER = 6
+W2_AFTER = 8
 END_AFTER = 19
 
 
@@ -112,11 +113,11 @@ def tile_picked_pick_glu_sigmoid_sub_e_kernel(tc, xT, w1, w3, w2, offs, out):
             src = raw[:].rearrange("p j (q t r) -> p t q j r", t=PACK, r=PAIR)[:, t0:t1]
             copy(grouped.rearrange("p (t q r j) -> p t q j r", t=t1 - t0, r=PAIR, j=PACK), src)
 
-        def round_on_gpsimd(raw, tag):
-            grouped = keep.tile([P, HALF * PACK], BF16, align_bytes=64, name="grouped", tag=tag)
+        def round_on_gpsimd(raw, tag, places):
+            grouped = keep.tile([P, HALF * places], BF16, align_bytes=64, name="grouped", tag=tag)
             nc.gpsimd.tensor_scalar(
-                grouped[:].rearrange("p (t q r j) -> p q t r j", t=PACK, r=PAIR, j=PACK),
-                raw[:].rearrange("p j (q t r) -> p q t r j", t=PACK, r=PAIR),
+                grouped[:].rearrange("p (t q r j) -> p q t r j", t=places, r=PAIR, j=PACK),
+                raw[:].rearrange("p j (q t r) -> p q t r j", t=PACK, r=PAIR)[:, :, :places],
                 1.0,
                 0.0,
                 mult,
@@ -150,15 +151,14 @@ def tile_picked_pick_glu_sigmoid_sub_e_kernel(tc, xT, w1, w3, w2, offs, out):
             quantize(w_codes["w3", 0][:, cols], w_scales["w3", 0][:, cols], parts[part][:])
         quantize_x(1, "w3a_part1")
 
-        w1b_grouped = round_on_gpsimd(w1b, "picked1")
+        w1b_grouped = round_on_gpsimd(w1b, "picked1", PACK)
 
-        holds = {W1B_AFTER: "w1b_scales", W2_AFTER: "w2_grouped", STEPS - 2: "middle_scales", END_AFTER: "end_scales"}
+        holds = {W3B_AFTER: "w3b_high", W1B_AFTER: "w1b_scales", W2_AFTER: "w2_grouped", STEPS - 2: "middle_scales", END_AFTER: "end_scales"}
         by_token = "p (t c) -> p c t"
         in_order = "p (c t) -> p c t"
         gate_rows = [keep.tile([P, T], F32, align_bytes=64, name="gates", tag=f"plane{j}") for j in range(slices)]
         ups = keep.tile([P, GPSIMD_GROUPS * WIDTH], F32, align_bytes=64, name="ups", tag="plane3")
         hidden = {}
-        late = []
 
         def passes(name, h, group, pool):
             bank = pool.tile([P, WIDTH], F32, name="bank", tag=f"{name}_bank")
@@ -190,7 +190,6 @@ def tile_picked_pick_glu_sigmoid_sub_e_kernel(tc, xT, w1, w3, w2, offs, out):
             if h == 1 and group < GPSIMD_GROUPS:
                 up = ups[:, group * WIDTH : (group + 1) * WIDTH]
                 nc.scalar.copy(up.rearrange(in_order, t=PACK), bank)
-                late.append((gate, up))
             else:
                 values = hidden[h, s][:, c * WIDTH : (c + 1) * WIDTH]
                 nc.vector.tensor_tensor(values.rearrange(in_order, t=PACK), gate.rearrange(in_order, t=PACK), bank, mult)
@@ -200,11 +199,14 @@ def tile_picked_pick_glu_sigmoid_sub_e_kernel(tc, xT, w1, w3, w2, offs, out):
 
         for group in range(STEPS):
             step(0, group)
-            if group == W1B_AFTER + 1:
+            if group == W3B_AFTER:
+                w3b_high = keep.tile([P, HALF * 2], BF16, align_bytes=64, name="high", tag="w3b_high")
+                round_places(nc.scalar.copy, w3b_high[:], w3b, 2, 4)
+            if group == W1B_AFTER:
                 w_codes["w1", 1] = keep.tile([P, HALF], U32, align_bytes=64, name="w1b_codes")
                 w_scales["w1", 1] = keep.tile([P, HALF], U8, align_bytes=64, name="scales", tag="w1b_scales")
                 quantize(w_codes["w1", 1][:], w_scales["w1", 1][:], w1b_grouped[:])
-                w3b_grouped = round_on_gpsimd(w3b, "picked1")
+                w3b_low = round_on_gpsimd(w3b, "picked1", 2)
 
         w2_grouped = keep.tile([P, 2 * N * PACK], BF16, align_bytes=64, name="w2_grouped", tag="w2_grouped")
         nc.scalar.copy(
@@ -217,17 +219,21 @@ def tile_picked_pick_glu_sigmoid_sub_e_kernel(tc, xT, w1, w3, w2, offs, out):
         w_scales["w3", 1] = middle[:, :HALF]
         w2_scales = middle[:, HALF + S :]
         h_scales = {(0, s): middle[:, HALF + s * SLICE : HALF + (s + 1) * SLICE] for s in range(slices)}
-        quantize(w_codes["w3", 1][:], w_scales["w3", 1], w3b_grouped[:])
-        quantize(w2_codes[:], w2_scales, w2_grouped[:])
+        for part, values in enumerate((w3b_low, w3b_high)):
+            cols = slice(part * 2 * P, (part + 1) * 2 * P)
+            quantize(w_codes["w3", 1][:, cols], w_scales["w3", 1][:, cols], values[:])
         for s in range(slices):
+            if s == slices - 1:
+                quantize(w2_codes[:], w2_scales, w2_grouped[:])
             quantize(h_codes[0, s][:], h_scales[0, s], hidden[0, s][:])
 
         firsts = keep.tile([P, GPSIMD_GROUPS * WIDTH], BF16, align_bytes=64, name="firsts", tag=f"hidden0_{slices - 1}")
         for group in range(END_AFTER + 2 - STEPS):
             step(1, group)
-            if group < GPSIMD_GROUPS:
-                gate, up = late[group]
-                nc.gpsimd.tensor_tensor(firsts[:, group * WIDTH : (group + 1) * WIDTH], gate, up, mult)
+            if group == GPSIMD_GROUPS - 1:
+                row, place = divmod(STEPS, T // WIDTH)
+                gates = gate_rows[row][:, place * WIDTH : (place + GPSIMD_GROUPS) * WIDTH]
+                nc.gpsimd.tensor_tensor(firsts[:], gates, ups[:], mult)
 
         end = keep.tile([P, S], U8, align_bytes=64, name="scales", tag="end_scales")
         for s in range(slices):

@@ -23,15 +23,18 @@ GROUP = 128
 PAIR = 2
 HALF = 512
 PLACE_SPLIT = 192
-SCALAR_SLICE = 1
+SCALAR_SLICE = 2
 WARM_PASSES = 2
+BANKS = 4
+BORROWED = 2
+LEAD = 3
 GROUPS = SLICE // GROUP
 STEPS = S // GROUP
 WIDTH = GROUP * PACK
 GPSIMD_GROUPS = 2
-W1B_AFTER = 7
-W3B_AFTER = 6
-W2_AFTER = 8
+W1B_AFTER = 6
+W3B_AFTER = 5
+W2_AFTER = 15
 END_AFTER = 19
 
 
@@ -145,13 +148,13 @@ def tile_picked_pick_glu_sigmoid_sub_e_kernel(tc, xT, w1, w3, w2, offs, out):
             grouped = keep.tile([P, HALF * 2], BF16, align_bytes=64, name="part", tag=tag)
             round_places(copy, grouped[:], w3a, 2 * part, 2 * part + 2)
             parts.append(grouped)
-        quantize_x(2, "w1a")
+        quantize_x(1, "w1a")
         for part in range(2):
             cols = slice(part * 2 * P, (part + 1) * 2 * P)
             quantize(w_codes["w3", 0][:, cols], w_scales["w3", 0][:, cols], parts[part][:])
-        quantize_x(1, "w3a_part1")
+        quantize_x(2, "w3a_part1")
 
-        w1b_grouped = round_on_gpsimd(w1b, "picked1", PACK)
+        w1b_grouped = round_on_gpsimd(w1b, "picked2", PACK)
 
         holds = {W3B_AFTER: "w3b_high", W1B_AFTER: "w1b_scales", W2_AFTER: "w2_grouped", STEPS - 2: "middle_scales", END_AFTER: "end_scales"}
         by_token = "p (t c) -> p c t"
@@ -159,9 +162,10 @@ def tile_picked_pick_glu_sigmoid_sub_e_kernel(tc, xT, w1, w3, w2, offs, out):
         gate_rows = [keep.tile([P, T], F32, align_bytes=64, name="gates", tag=f"plane{j}") for j in range(slices)]
         ups = keep.tile([P, GPSIMD_GROUPS * WIDTH], F32, align_bytes=64, name="ups", tag="plane3")
         hidden = {}
+        rings = {"w1": psum_1, "w3": psum_3}
 
-        def passes(name, h, group, pool):
-            bank = pool.tile([P, WIDTH], F32, name="bank", tag=f"{name}_bank")
+        def passes(name, h, group, ring):
+            bank = rings[ring].tile([P, WIDTH], F32, name="bank", tag=f"{ring}_bank")
             s, c = divmod(group, GROUPS)
             n_cols = slice(c * GROUP, (c + 1) * GROUP)
             for t in range(PACK):
@@ -175,67 +179,74 @@ def tile_picked_pick_glu_sigmoid_sub_e_kernel(tc, xT, w1, w3, w2, offs, out):
                 )
             return bank[:].rearrange(by_token, t=PACK)
 
-        def step(h, group):
+        gates = {}
+
+        def make_gate(h, group):
             number = h * STEPS + group
-            s, c = divmod(group, GROUPS)
-            if c == 0:
-                hidden[h, s] = keep.tile([P, SLICE * PACK], BF16, align_bytes=64, name="hidden", tag=f"hidden{h}_{s}")
             if number in holds:
                 gate = keep.tile([P, WIDTH], F32, align_bytes=64, name="gate", tag=holds[number])[:]
             else:
                 row, place = divmod(number, T // WIDTH)
                 gate = gate_rows[row][:, place * WIDTH : (place + 1) * WIDTH]
-            nc.scalar.activation(gate.rearrange(in_order, t=PACK), passes("w1", h, group, psum_1), Sigmoid)
-            bank = passes("w3", h, group, psum_3)
-            if h == 1 and group < GPSIMD_GROUPS:
-                up = ups[:, group * WIDTH : (group + 1) * WIDTH]
-                nc.scalar.copy(up.rearrange(in_order, t=PACK), bank)
-            else:
-                values = hidden[h, s][:, c * WIDTH : (c + 1) * WIDTH]
-                nc.vector.tensor_tensor(values.rearrange(in_order, t=PACK), gate.rearrange(in_order, t=PACK), bank, mult)
+            ring = "w3" if number < BORROWED else "w1"
+            nc.scalar.activation(gate.rearrange(in_order, t=PACK), passes("w1", h, group, ring), Sigmoid)
+            gates[h, group] = gate
+
+        def product(h, group):
+            s, c = divmod(group, GROUPS)
+            if (h, s) not in hidden:
+                hidden[h, s] = keep.tile([P, SLICE * PACK], BF16, align_bytes=64, name="hidden", tag=f"hidden{h}_{s}")
+            values = hidden[h, s][:, c * WIDTH : (c + 1) * WIDTH]
+            bank = passes("w3", h, group, "w3")
+            nc.vector.tensor_tensor(values.rearrange(in_order, t=PACK), gates[h, group].rearrange(in_order, t=PACK), bank, mult)
 
         h_codes = {(h, s): keep.tile([P, SLICE], U32, align_bytes=64, name=f"h_codes{h}_{s}") for h in range(2) for s in range(slices)}
         w2_codes = keep.tile([P, 2 * N], U32, align_bytes=64, name="w2_codes")
 
         for group in range(STEPS):
-            step(0, group)
-            if group == W3B_AFTER:
-                w3b_high = keep.tile([P, HALF * 2], BF16, align_bytes=64, name="high", tag="w3b_high")
-                round_places(nc.scalar.copy, w3b_high[:], w3b, 2, 4)
-            if group == W1B_AFTER:
+            for ahead in range(len(gates), min(STEPS, max(BANKS + BORROWED, group + LEAD + 1))):
+                make_gate(0, ahead)
+            product(0, group)
+            if group == W1B_AFTER + 1:
                 w_codes["w1", 1] = keep.tile([P, HALF], U32, align_bytes=64, name="w1b_codes")
                 w_scales["w1", 1] = keep.tile([P, HALF], U8, align_bytes=64, name="scales", tag="w1b_scales")
                 quantize(w_codes["w1", 1][:], w_scales["w1", 1][:], w1b_grouped[:])
-                w3b_low = round_on_gpsimd(w3b, "picked1", 2)
+                w3b_low = round_on_gpsimd(w3b, "picked2", 2)
 
-        w2_grouped = keep.tile([P, 2 * N * PACK], BF16, align_bytes=64, name="w2_grouped", tag="w2_grouped")
-        nc.scalar.copy(
-            w2_grouped[:].rearrange("p (g m r t) -> p g m t r", g=2, r=PAIR, t=PACK),
-            w2_raw[:].rearrange("p g t (m r) -> p g m t r", r=PAIR),
-        )
+        w3b_high = keep.tile([P, HALF * 2], BF16, align_bytes=64, name="high", tag="w3b_high")
+        round_places(nc.scalar.copy, w3b_high[:], w3b, 2, 4)
 
-        middle = keep.tile([P, HALF + S + 2 * N], U8, align_bytes=64, name="scales", tag="middle_scales")
+        middle = keep.tile([P, HALF + S], U8, align_bytes=64, name="scales", tag="middle_scales")
         w_codes["w3", 1] = keep.tile([P, HALF], U32, align_bytes=64, name="w3b_codes")
         w_scales["w3", 1] = middle[:, :HALF]
-        w2_scales = middle[:, HALF + S :]
         h_scales = {(0, s): middle[:, HALF + s * SLICE : HALF + (s + 1) * SLICE] for s in range(slices)}
         for part, values in enumerate((w3b_low, w3b_high)):
             cols = slice(part * 2 * P, (part + 1) * 2 * P)
             quantize(w_codes["w3", 1][:, cols], w_scales["w3", 1][:, cols], values[:])
         for s in range(slices):
-            if s == slices - 1:
-                quantize(w2_codes[:], w2_scales, w2_grouped[:])
             quantize(h_codes[0, s][:], h_scales[0, s], hidden[0, s][:])
 
         firsts = keep.tile([P, GPSIMD_GROUPS * WIDTH], BF16, align_bytes=64, name="firsts", tag=f"hidden0_{slices - 1}")
-        for group in range(END_AFTER + 2 - STEPS):
-            step(1, group)
-            if group == GPSIMD_GROUPS - 1:
-                row, place = divmod(STEPS, T // WIDTH)
-                gates = gate_rows[row][:, place * WIDTH : (place + GPSIMD_GROUPS) * WIDTH]
-                nc.gpsimd.tensor_tensor(firsts[:], gates, ups[:], mult)
+        for group in range(GPSIMD_GROUPS):
+            make_gate(1, group)
+        for group in range(GPSIMD_GROUPS):
+            up = ups[:, group * WIDTH : (group + 1) * WIDTH]
+            nc.scalar.copy(up.rearrange(in_order, t=PACK), passes("w3", 1, group, "w3"))
+        row, place = divmod(STEPS, T // WIDTH)
+        nc.gpsimd.tensor_tensor(firsts[:], gate_rows[row][:, place * WIDTH : (place + GPSIMD_GROUPS) * WIDTH], ups[:], mult)
+        for group in range(GPSIMD_GROUPS, END_AFTER + 2 - STEPS):
+            for ahead in range(len(gates) - STEPS, min(STEPS, group + LEAD + 1)):
+                make_gate(1, ahead)
+                if STEPS + ahead == END_AFTER:
+                    w2_grouped = keep.tile([P, 2 * N * PACK], BF16, align_bytes=64, name="w2_grouped", tag="w2_grouped")
+                    nc.scalar.copy(
+                        w2_grouped[:].rearrange("p (g m r t) -> p g m t r", g=2, r=PAIR, t=PACK),
+                        w2_raw[:].rearrange("p g t (m r) -> p g m t r", r=PAIR),
+                    )
+            product(1, group)
 
-        end = keep.tile([P, S], U8, align_bytes=64, name="scales", tag="end_scales")
+        end = keep.tile([P, S + 2 * N], U8, align_bytes=64, name="scales", tag="end_scales")
+        w2_scales = end[:, S:]
         for s in range(slices):
             h_scales[1, s] = end[:, s * SLICE : (s + 1) * SLICE]
 
@@ -261,15 +272,16 @@ def tile_picked_pick_glu_sigmoid_sub_e_kernel(tc, xT, w1, w3, w2, offs, out):
         split = GPSIMD_GROUPS * GROUP
         quantize_h(0, 0, split, firsts[:])
         quantize_h(0, split, SLICE, hidden[1, 0][:, split * PACK :])
+        quantize(w2_codes[:], w2_scales, w2_grouped[:])
         finish(0, 0, SLICE)
         quantize_h(1, 0, SLICE, hidden[1, 1][:])
         finish(1, 0, SLICE)
         last = slices - 1
         for group in range(END_AFTER + 2 - STEPS, 2 * GROUPS + 2 + 1):
-            step(1, group)
+            product(1, group)
         quantize_h(last, 0, 2 * GROUP, hidden[1, last][:, : 2 * WIDTH])
         finish(last, 0, 2 * GROUP)
-        step(1, STEPS - 1)
+        product(1, STEPS - 1)
         for c in (2, 3):
             quantize_h(last, c * GROUP, (c + 1) * GROUP, hidden[1, last][:, c * WIDTH : (c + 1) * WIDTH])
             finish(last, c * GROUP, (c + 1) * GROUP)

@@ -26,7 +26,7 @@ PLACE_SPLIT = 192
 SCALAR_SLICE = 2
 WARM_PASSES = 2
 BANKS = 4
-BORROWED = 2
+BORROWED = 0
 LEAD = 3
 GROUPS = SLICE // GROUP
 STEPS = S // GROUP

@@ -22,12 +22,11 @@ SLICE = 512
 GROUP = 128
 PAIR = 2
 HALF = 512
-PLACE_SPLIT = 192
+PLACE_SPLIT = 128
 SCALAR_SLICE = 2
-WARM_PASSES = 2
+WARM_PASSES = 3
 BANKS = 4
-BORROWED = 0
-LEAD = 3
+LEAD = (3, 3)
 GROUPS = SLICE // GROUP
 STEPS = S // GROUP
 WIDTH = GROUP * PACK
@@ -69,23 +68,33 @@ def tile_picked_pick_glu_sigmoid_sub_e_kernel(tc, xT, w1, w3, w2, offs, out):
         x_rows = xT.rearrange("(p j) t -> p j t", j=PACK)
         planes = [keep.tile([P, T], F32, align_bytes=64, name="plane", tag=f"plane{j}") for j in range(PACK)]
         picked = [keep.tile([P, SLICE * PACK], BF16, align_bytes=64, name="picked", tag=f"picked{s}") for s in range(slices)]
-        rows = keep.tile([P, PACK * SLICE], BF16, align_bytes=64, name="rows")
+        shares = {"gpsimd": (PLACE_SPLIT, SLICE), "scalar": (0, PLACE_SPLIT)}
+        early_rows = keep.tile([P, 2 * SLICE], BF16, align_bytes=64, name="early_rows")
+        late_rows = {
+            who: keep.tile([P, 2 * (done - start)], BF16, align_bytes=64, name="late_rows", tag=f"rows_{who}")
+            for who, (start, done) in shares.items()
+        }
         x_codes = {}
         x_scales = [keep.tile([P, SLICE], U8, align_bytes=64, name=f"x_scales{s}") for s in range(slices)]
 
         def gather_plane(j, s):
-            window = planes[j][:].indirect(offsets[:, s * (SLICE // 16) : (s + 1) * (SLICE // 16)])
-            if s == SCALAR_SLICE:
-                nc.scalar.activation(rows[:, j * SLICE : (j + 1) * SLICE], window, Copy)
+            def window(start, done):
+                return planes[j][:].indirect(offsets[:, (s * SLICE + start) // 16 : (s * SLICE + done) // 16])
+
+            if s != SCALAR_SLICE:
+                nc.vector.tensor_copy(picked[s][:].rearrange("p (n j) -> p n j", j=PACK)[:, :, j], window(0, SLICE))
+            elif j < 2:
+                nc.scalar.activation(early_rows[:, j * SLICE : (j + 1) * SLICE], window(0, SLICE), Copy)
             else:
-                nc.vector.tensor_copy(picked[s][:].rearrange("p (n j) -> p n j", j=PACK)[:, :, j], window)
+                for who, (start, done) in shares.items():
+                    count = done - start
+                    nc.scalar.activation(late_rows[who][:, (j - 2) * count : (j - 1) * count], window(start, done), Copy)
 
         def quantize_x(s, tag):
             x_codes[s] = keep.tile([P, SLICE], U32, align_bytes=64, name="x_codes", tag=tag)
             quantize(x_codes[s][:], x_scales[s][:], picked[s][:])
 
         placed = picked[SCALAR_SLICE][:].rearrange("p (n j) -> p n j", j=PACK)
-        by_entry = rows[:].rearrange("p (j n) -> p n j", j=PACK)
         for j in range(PACK):
             nc.sync.dma_start(out=planes[j][:], in_=x_rows[:, j, :])
             if j == 0:
@@ -93,9 +102,20 @@ def tile_picked_pick_glu_sigmoid_sub_e_kernel(tc, xT, w1, w3, w2, offs, out):
             for s in range(slices):
                 gather_plane(j, s)
             if j == 1:
-                nc.scalar.copy(placed[:, :, 0:2], by_entry[:, :, 0:2])
-        nc.scalar.copy(placed[:, :PLACE_SPLIT, 2:4], by_entry[:, :PLACE_SPLIT, 2:4])
-        nc.gpsimd.tensor_scalar(placed[:, PLACE_SPLIT:, 2:4], by_entry[:, PLACE_SPLIT:, 2:4], 1.0, 0.0, mult, add)
+                nc.scalar.copy(placed[:, :, 0:2], early_rows[:].rearrange("p (j n) -> p n j", j=2))
+        nc.scalar.copy(placed[:, :PLACE_SPLIT, 2:4], late_rows["scalar"][:].rearrange("p (j n) -> p n j", j=2))
+        nc.gpsimd.tensor_scalar(placed[:, PLACE_SPLIT:, 2:4], late_rows["gpsimd"][:].rearrange("p (j n) -> p n j", j=2), 1.0, 0.0, mult, add)
+
+        warm_values = keep.tile([P, SLICE * PACK], BF16, align_bytes=64, name="warm_values")
+        warm_codes = keep.tile([P, SLICE], U32, align_bytes=64, name="warm_codes")
+        warm_scales = keep.tile([P, SLICE], U8, align_bytes=64, name="warm_scales")
+        nc.vector.tensor_copy(warm_values[:], planes[0][:, : SLICE * PACK])
+        quantize(warm_codes[:], warm_scales[:], warm_values[:])
+        warm_left = keep.tile([P, P], U32, align_bytes=64, name="warm_left", tag="rows_scalar")
+        nc.scalar.copy(warm_left[:], warm_codes[:, :P])
+        idle = psum_3.tile([P, SLICE], F32, name="idle", tag="w3_bank")
+        for i in range(WARM_PASSES):
+            multiply(idle[:], warm_left[:], warm_scales[:, :P], warm_codes[:], warm_scales[:])
 
         def load_w(w, h, tag):
             raw = keep.tile([P, PACK, HALF], F32, align_bytes=64, name="raw", tag=tag)
@@ -135,9 +155,6 @@ def tile_picked_pick_glu_sigmoid_sub_e_kernel(tc, xT, w1, w3, w2, offs, out):
             w_scales[name, 0] = keep.tile([P, HALF], U8, align_bytes=64, name=f"{name}a_scales")
 
         quantize_x(0, "x_codes0")
-        idle = psum_3.tile([P, SLICE], F32, name="idle", tag="w3_bank")
-        for i in range(WARM_PASSES):
-            multiply(idle[:], x_codes[0][:, :P], x_scales[0][:, :P], x_codes[0][:], x_scales[0][:])
         w1a_grouped = keep.tile([P, HALF * PACK], BF16, align_bytes=64, name="grouped", tag="w1a_grouped")
         round_places(nc.scalar.copy, w1a_grouped[:, : 3 * HALF], w1a, 0, 3)
         round_places(nc.vector.tensor_copy, w1a_grouped[:, 3 * HALF :], w1a, 3, 4)
@@ -188,8 +205,7 @@ def tile_picked_pick_glu_sigmoid_sub_e_kernel(tc, xT, w1, w3, w2, offs, out):
             else:
                 row, place = divmod(number, T // WIDTH)
                 gate = gate_rows[row][:, place * WIDTH : (place + 1) * WIDTH]
-            ring = "w3" if number < BORROWED else "w1"
-            nc.scalar.activation(gate.rearrange(in_order, t=PACK), passes("w1", h, group, ring), Sigmoid)
+            nc.scalar.activation(gate.rearrange(in_order, t=PACK), passes("w1", h, group, "w1"), Sigmoid)
             gates[h, group] = gate
 
         def product(h, group):
@@ -204,7 +220,7 @@ def tile_picked_pick_glu_sigmoid_sub_e_kernel(tc, xT, w1, w3, w2, offs, out):
         w2_codes = keep.tile([P, 2 * N], U32, align_bytes=64, name="w2_codes")
 
         for group in range(STEPS):
-            for ahead in range(len(gates), min(STEPS, max(BANKS + BORROWED, group + LEAD + 1))):
+            for ahead in range(len(gates), min(STEPS, max(BANKS, group + LEAD[0] + 1))):
                 make_gate(0, ahead)
             product(0, group)
             if group == W1B_AFTER + 1:
@@ -235,15 +251,18 @@ def tile_picked_pick_glu_sigmoid_sub_e_kernel(tc, xT, w1, w3, w2, offs, out):
         row, place = divmod(STEPS, T // WIDTH)
         nc.gpsimd.tensor_tensor(firsts[:], gate_rows[row][:, place * WIDTH : (place + GPSIMD_GROUPS) * WIDTH], ups[:], mult)
         for group in range(GPSIMD_GROUPS, END_AFTER + 2 - STEPS):
-            for ahead in range(len(gates) - STEPS, min(STEPS, group + LEAD + 1)):
+            for ahead in range(len(gates) - STEPS, min(STEPS, group + LEAD[1] + 1)):
                 make_gate(1, ahead)
-                if STEPS + ahead == END_AFTER:
+                if STEPS + ahead == END_AFTER + 2:
                     w2_grouped = keep.tile([P, 2 * N * PACK], BF16, align_bytes=64, name="w2_grouped", tag="w2_grouped")
                     nc.scalar.copy(
                         w2_grouped[:].rearrange("p (g m r t) -> p g m t r", g=2, r=PAIR, t=PACK),
                         w2_raw[:].rearrange("p g t (m r) -> p g m t r", r=PAIR),
                     )
             product(1, group)
+
+        for ahead in range(len(gates) - STEPS, STEPS):
+            make_gate(1, ahead)
 
         end = keep.tile([P, S + 2 * N], U8, align_bytes=64, name="scales", tag="end_scales")
         w2_scales = end[:, S:]

@@ -26,6 +26,7 @@ PLACE_SPLIT = 128
 SCALAR_SLICE = 2
 WARM_PASSES = 3
 BANKS = 4
+BORROWED = 2
 LEAD = (3, 3)
 GROUPS = SLICE // GROUP
 STEPS = S // GROUP
@@ -205,7 +206,8 @@ def tile_picked_pick_glu_sigmoid_sub_e_kernel(tc, xT, w1, w3, w2, offs, out):
             else:
                 row, place = divmod(number, T // WIDTH)
                 gate = gate_rows[row][:, place * WIDTH : (place + 1) * WIDTH]
-            nc.scalar.activation(gate.rearrange(in_order, t=PACK), passes("w1", h, group, "w1"), Sigmoid)
+            ring = "w3" if number < BORROWED else "w1"
+            nc.scalar.activation(gate.rearrange(in_order, t=PACK), passes("w1", h, group, ring), Sigmoid)
             gates[h, group] = gate
 
         def product(h, group):
@@ -220,7 +222,7 @@ def tile_picked_pick_glu_sigmoid_sub_e_kernel(tc, xT, w1, w3, w2, offs, out):
         w2_codes = keep.tile([P, 2 * N], U32, align_bytes=64, name="w2_codes")
 
         for group in range(STEPS):
-            for ahead in range(len(gates), min(STEPS, max(BANKS, group + LEAD[0] + 1))):
+            for ahead in range(len(gates), min(STEPS, max(BANKS + BORROWED, group + LEAD[0] + 1))):
                 make_gate(0, ahead)
             product(0, group)
             if group == W1B_AFTER + 1:

@@ -20,11 +20,12 @@ add = mybir.AluOpType.add
 
 SLICE = 512
 GROUP = 128
-PAIR = 2
+PAIR = 4
 HALF = 512
 PLACE_SPLIT = 128
 SCALAR_SLICE = 2
 WARM_PASSES = 3
+STORE = 256
 BANKS = 4
 BORROWED = 2
 LEAD = (3, 3)
@@ -129,9 +130,9 @@ def tile_picked_pick_glu_sigmoid_sub_e_kernel(tc, xT, w1, w3, w2, offs, out):
         w3b = load_w(w3, 1, "w3b")
         w2_raw = keep.tile([P, 2, PACK, N], F32, name="w2_raw")
         for g in range(2):
-            w2_rows = w2[g * HALF : (g + 1) * HALF].rearrange("(q t r) m -> r q t m", t=PACK, r=PAIR)
-            for r in range(PAIR):
-                nc.sync.dma_start(out=w2_raw[r:P:PAIR, g], in_=w2_rows[r])
+            w2_rows = w2[g * HALF : (g + 1) * HALF].rearrange("(q t r) m -> t q r m", t=PACK, r=PAIR)
+            for t in range(PACK):
+                nc.sync.dma_start(out=w2_raw[:, g, t, :], in_=w2_rows[t])
 
         def round_places(copy, grouped, raw, t0, t1):
             src = raw[:].rearrange("p j (q t r) -> p t q j r", t=PACK, r=PAIR)[:, t0:t1]
@@ -288,7 +289,9 @@ def tile_picked_pick_glu_sigmoid_sub_e_kernel(tc, xT, w1, w3, w2, offs, out):
                 )
             y = keep.tile([P, done - start], F32, name=f"y{s}_{start}")
             nc.scalar.copy(y[:], acc[:])
-            nc.sync.dma_start(out=out[:, s * SLICE + start : s * SLICE + done], in_=y[:])
+            for first in range(start, done, STORE):
+                until = min(done, first + STORE)
+                nc.sync.dma_start(out=out[:, s * SLICE + first : s * SLICE + until], in_=y[:, first - start : until - start])
 
         split = GPSIMD_GROUPS * GROUP
         quantize_h(0, 0, split, firsts[:])

@@ -10,6 +10,7 @@ PACK = 4
 F32 = mybir.dt.float32
 BF16 = mybir.dt.bfloat16
 U32 = mybir.dt.uint32
+I32 = mybir.dt.int32
 U16 = mybir.dt.uint16
 U8 = mybir.dt.uint8
 FP8X4 = mybir.dt.float8_e4m3fn_x4
@@ -22,8 +23,8 @@ SLICE = 512
 GROUP = 128
 PAIR = 4
 HALF = 512
-PLACE_SPLIT = 128
-SCALAR_SLICE = 2
+VECTOR_UNTIL = 640
+PLACED_FROM = 1152
 WARM_PASSES = 3
 STORE = 256
 BANKS = 4
@@ -69,62 +70,58 @@ def tile_picked_pick_glu_sigmoid_sub_e_kernel(tc, xT, w1, w3, w2, offs, out):
 
         x_rows = xT.rearrange("(p j) t -> p j t", j=PACK)
         planes = [keep.tile([P, T], F32, align_bytes=64, name="plane", tag=f"plane{j}") for j in range(PACK)]
-        picked = [keep.tile([P, SLICE * PACK], BF16, align_bytes=64, name="picked", tag=f"picked{s}") for s in range(slices)]
-        shares = {"gpsimd": (PLACE_SPLIT, SLICE), "scalar": (0, PLACE_SPLIT)}
-        early_rows = keep.tile([P, 2 * SLICE], BF16, align_bytes=64, name="early_rows")
-        late_rows = {
-            who: keep.tile([P, 2 * (done - start)], BF16, align_bytes=64, name="late_rows", tag=f"rows_{who}")
-            for who, (start, done) in shares.items()
-        }
+        picked = keep.tile([P, S * PACK], BF16, align_bytes=64, name="picked", tag="picked")
+        placed = picked[:].rearrange("p (n j) -> p n j", j=PACK)
+        late_rows = keep.tile([P, 2 * (S - PLACED_FROM)], BF16, align_bytes=64, name="late_rows")
         x_codes = {}
         x_scales = [keep.tile([P, SLICE], U8, align_bytes=64, name=f"x_scales{s}") for s in range(slices)]
 
-        def gather_plane(j, s):
+        def gather_plane(j):
             def window(start, done):
-                return planes[j][:].indirect(offsets[:, (s * SLICE + start) // 16 : (s * SLICE + done) // 16])
+                return planes[j][:].indirect(offsets[:, start // 16 : done // 16])
 
-            if s != SCALAR_SLICE:
-                nc.vector.tensor_copy(picked[s][:].rearrange("p (n j) -> p n j", j=PACK)[:, :, j], window(0, SLICE))
-            elif j < 2:
-                nc.scalar.activation(early_rows[:, j * SLICE : (j + 1) * SLICE], window(0, SLICE), Copy)
+            nc.vector.tensor_copy(placed[:, :VECTOR_UNTIL, j], window(0, VECTOR_UNTIL))
+            if j < 2:
+                nc.scalar.activation(placed[:, VECTOR_UNTIL:, j], window(VECTOR_UNTIL, S), Copy)
             else:
-                for who, (start, done) in shares.items():
-                    count = done - start
-                    nc.scalar.activation(late_rows[who][:, (j - 2) * count : (j - 1) * count], window(start, done), Copy)
+                count = S - PLACED_FROM
+                nc.scalar.activation(late_rows[:, (j - 2) * count : (j - 1) * count], window(PLACED_FROM, S), Copy)
+                nc.scalar.activation(placed[:, VECTOR_UNTIL:PLACED_FROM, j], window(VECTOR_UNTIL, PLACED_FROM), Copy)
 
         def quantize_x(s, tag):
             x_codes[s] = keep.tile([P, SLICE], U32, align_bytes=64, name="x_codes", tag=tag)
-            quantize(x_codes[s][:], x_scales[s][:], picked[s][:])
+            quantize(x_codes[s][:], x_scales[s][:], picked[:, s * SLICE * PACK : (s + 1) * SLICE * PACK])
 
-        placed = picked[SCALAR_SLICE][:].rearrange("p (n j) -> p n j", j=PACK)
         for j in range(PACK):
             nc.sync.dma_start(out=planes[j][:], in_=x_rows[:, j, :])
             if j == 0:
                 nc.sync.dma_start(offsets[:], offs)
-            for s in range(slices):
-                gather_plane(j, s)
-            if j == 1:
-                nc.scalar.copy(placed[:, :, 0:2], early_rows[:].rearrange("p (j n) -> p n j", j=2))
-        nc.scalar.copy(placed[:, :PLACE_SPLIT, 2:4], late_rows["scalar"][:].rearrange("p (j n) -> p n j", j=2))
-        nc.gpsimd.tensor_scalar(placed[:, PLACE_SPLIT:, 2:4], late_rows["gpsimd"][:].rearrange("p (j n) -> p n j", j=2), 1.0, 0.0, mult, add)
+            gather_plane(j)
+        nc.gpsimd.tensor_scalar(placed[:, PLACED_FROM:, 2:4], late_rows[:].rearrange("p (j n) -> p n j", j=2), 1.0, 0.0, mult, add)
+
+        def rows_of(w, h):
+            return w.rearrange("(p j) c -> p j c", j=PACK)[:, :, h * HALF : (h + 1) * HALF]
+
+        def load_w(w, h, tag):
+            raw = keep.tile([P, PACK, HALF], F32, align_bytes=64, name="raw", tag=tag)
+            nc.sync.dma_start(out=raw[:], in_=rows_of(w, h))
+            return raw
 
         warm_values = keep.tile([P, SLICE * PACK], BF16, align_bytes=64, name="warm_values")
         warm_codes = keep.tile([P, SLICE], U32, align_bytes=64, name="warm_codes")
         warm_scales = keep.tile([P, SLICE], U8, align_bytes=64, name="warm_scales")
+        warm_left = keep.tile([P, P], U8, align_bytes=64, name="warm_left")
+        nc.gpsimd.memset(warm_scales[:], 0)
         nc.vector.tensor_copy(warm_values[:], planes[0][:, : SLICE * PACK])
         quantize(warm_codes[:], warm_scales[:], warm_values[:])
-        warm_left = keep.tile([P, P], U32, align_bytes=64, name="warm_left", tag="rows_scalar")
-        nc.scalar.copy(warm_left[:], warm_codes[:, :P])
+        w1a = keep.tile([P, PACK, HALF], F32, align_bytes=64, name="raw", tag="w1a")
+        nc.sync.dma_start(out=w1a[:, :2], in_=rows_of(w1, 0)[:, :2])
+        nc.sync.dma_start(out=warm_left[:].bitcast(I32), in_=warm_scales[:, :P].bitcast(I32))
+        nc.sync.dma_start(out=w1a[:, 2:], in_=rows_of(w1, 0)[:, 2:])
         idle = psum_3.tile([P, SLICE], F32, name="idle", tag="w3_bank")
         for i in range(WARM_PASSES):
-            multiply(idle[:], warm_left[:], warm_scales[:, :P], warm_codes[:], warm_scales[:])
+            multiply(idle[:], warm_codes[:, :P], warm_left[:], warm_codes[:], warm_scales[:])
 
-        def load_w(w, h, tag):
-            raw = keep.tile([P, PACK, HALF], F32, align_bytes=64, name="raw", tag=tag)
-            nc.sync.dma_start(out=raw[:], in_=w.rearrange("(p j) c -> p j c", j=PACK)[:, :, h * HALF : (h + 1) * HALF])
-            return raw
-
-        w1a = load_w(w1, 0, "w1a")
         w3a = load_w(w3, 0, "w3a")
         w1b = load_w(w1, 1, "w1b")
         w3b = load_w(w3, 1, "w3b")
@@ -156,24 +153,31 @@ def tile_picked_pick_glu_sigmoid_sub_e_kernel(tc, xT, w1, w3, w2, offs, out):
             w_codes[name, 0] = keep.tile([P, HALF], U32, align_bytes=64, name=f"{name}a_codes")
             w_scales[name, 0] = keep.tile([P, HALF], U8, align_bytes=64, name=f"{name}a_scales")
 
+        def quantize_places(name, t0, t1, values):
+            cols = slice(t0 * P, t1 * P)
+            quantize(w_codes[name, 0][:, cols], w_scales[name, 0][:, cols], values)
+
         quantize_x(0, "x_codes0")
-        w1a_grouped = keep.tile([P, HALF * PACK], BF16, align_bytes=64, name="grouped", tag="w1a_grouped")
-        round_places(nc.scalar.copy, w1a_grouped[:, : 3 * HALF], w1a, 0, 3)
-        round_places(nc.vector.tensor_copy, w1a_grouped[:, 3 * HALF :], w1a, 3, 4)
-        quantize(w_codes["w1", 0][:], w_scales["w1", 0][:], w1a_grouped[:])
-
-        parts = []
-        for part, (copy, tag) in enumerate(((nc.vector.tensor_copy, "w1a_grouped"), (nc.scalar.copy, "w3a_part1"))):
-            grouped = keep.tile([P, HALF * 2], BF16, align_bytes=64, name="part", tag=tag)
-            round_places(copy, grouped[:], w3a, 2 * part, 2 * part + 2)
-            parts.append(grouped)
+        w1a_low = keep.tile([P, HALF * 2], BF16, align_bytes=64, name="w1a_low")
+        w1a_high = keep.tile([P, HALF * 2], BF16, align_bytes=64, name="w1a_high")
+        round_places(nc.scalar.copy, w1a_high[:], w1a, 2, 4)
+        for t in range(2):
+            round_places(nc.vector.tensor_copy, w1a_low[:, t * HALF : (t + 1) * HALF], w1a, t, t + 1)
+        for t in range(2):
+            quantize_places("w1", t, t + 1, w1a_low[:, t * HALF : (t + 1) * HALF])
+        quantize_places("w1", 2, 4, w1a_high[:])
         quantize_x(1, "w1a")
-        for part in range(2):
-            cols = slice(part * 2 * P, (part + 1) * 2 * P)
-            quantize(w_codes["w3", 0][:, cols], w_scales["w3", 0][:, cols], parts[part][:])
-        quantize_x(2, "w3a_part1")
 
-        w1b_grouped = round_on_gpsimd(w1b, "picked2", PACK)
+        w3a_low = keep.tile([P, HALF * 2], BF16, align_bytes=64, name="w3a_low")
+        w3a_high = keep.tile([P, HALF * 2], BF16, align_bytes=64, name="w3a_high", tag="w3a_high")
+        round_places(nc.scalar.copy, w3a_high[:, HALF:], w3a, 3, 4)
+        round_places(nc.vector.tensor_copy, w3a_low[:], w3a, 0, 2)
+        round_places(nc.vector.tensor_copy, w3a_high[:, :HALF], w3a, 2, 3)
+        quantize_places("w3", 0, 2, w3a_low[:])
+        quantize_places("w3", 2, 4, w3a_high[:])
+        quantize_x(2, "w3a_high")
+
+        w1b_grouped = round_on_gpsimd(w1b, "picked", PACK)
 
         holds = {W3B_AFTER: "w3b_high", W1B_AFTER: "w1b_scales", W2_AFTER: "w2_grouped", STEPS - 2: "middle_scales", END_AFTER: "end_scales"}
         by_token = "p (t c) -> p c t"
@@ -230,7 +234,7 @@ def tile_picked_pick_glu_sigmoid_sub_e_kernel(tc, xT, w1, w3, w2, offs, out):
                 w_codes["w1", 1] = keep.tile([P, HALF], U32, align_bytes=64, name="w1b_codes")
                 w_scales["w1", 1] = keep.tile([P, HALF], U8, align_bytes=64, name="scales", tag="w1b_scales")
                 quantize(w_codes["w1", 1][:], w_scales["w1", 1][:], w1b_grouped[:])
-                w3b_low = round_on_gpsimd(w3b, "picked2", 2)
+                w3b_low = round_on_gpsimd(w3b, "picked", 2)
 
         w3b_high = keep.tile([P, HALF * 2], BF16, align_bytes=64, name="high", tag="w3b_high")
         round_places(nc.scalar.copy, w3b_high[:], w3b, 2, 4)

@@ -23,9 +23,9 @@ SLICE = 512
 GROUP = 128
 PAIR = 4
 HALF = 512
-VECTOR_UNTIL = 640
+VECTOR_UNTIL = 768
 PLACED_FROM = 1152
-WARM_PASSES = 3
+WARM_PASSES = 4
 STORE = 256
 BANKS = 4
 BORROWED = 2
@@ -34,8 +34,8 @@ GROUPS = SLICE // GROUP
 STEPS = S // GROUP
 WIDTH = GROUP * PACK
 GPSIMD_GROUPS = 2
-W1B_AFTER = 6
-W3B_AFTER = 5
+W1B_AFTER = 4
+GPSIMD_PLACES = 3
 W2_AFTER = 15
 END_AFTER = 19
 
@@ -136,9 +136,9 @@ def tile_picked_pick_glu_sigmoid_sub_e_kernel(tc, xT, w1, w3, w2, offs, out):
             copy(grouped.rearrange("p (t q r j) -> p t q j r", t=t1 - t0, r=PAIR, j=PACK), src)
 
         def round_on_gpsimd(raw, tag, places):
-            grouped = keep.tile([P, HALF * places], BF16, align_bytes=64, name="grouped", tag=tag)
+            grouped = keep.tile([P, HALF * PACK], BF16, align_bytes=64, name="grouped", tag=tag)
             nc.gpsimd.tensor_scalar(
-                grouped[:].rearrange("p (t q r j) -> p q t r j", t=places, r=PAIR, j=PACK),
+                grouped[:, : HALF * places].rearrange("p (t q r j) -> p q t r j", t=places, r=PAIR, j=PACK),
                 raw[:].rearrange("p j (q t r) -> p q t r j", t=PACK, r=PAIR)[:, :, :places],
                 1.0,
                 0.0,
@@ -177,9 +177,9 @@ def tile_picked_pick_glu_sigmoid_sub_e_kernel(tc, xT, w1, w3, w2, offs, out):
         quantize_places("w3", 2, 4, w3a_high[:])
         quantize_x(2, "w3a_high")
 
-        w1b_grouped = round_on_gpsimd(w1b, "picked", PACK)
+        w1b_grouped = round_on_gpsimd(w1b, "picked", GPSIMD_PLACES)
 
-        holds = {W3B_AFTER: "w3b_high", W1B_AFTER: "w1b_scales", W2_AFTER: "w2_grouped", STEPS - 2: "middle_scales", END_AFTER: "end_scales"}
+        holds = {W1B_AFTER: "w1b_scales", W2_AFTER: "w2_grouped", STEPS - 2: "middle_scales", END_AFTER: "end_scales"}
         by_token = "p (t c) -> p c t"
         in_order = "p (c t) -> p c t"
         gate_rows = [keep.tile([P, T], F32, align_bytes=64, name="gates", tag=f"plane{j}") for j in range(slices)]
@@ -229,23 +229,22 @@ def tile_picked_pick_glu_sigmoid_sub_e_kernel(tc, xT, w1, w3, w2, offs, out):
         for group in range(STEPS):
             for ahead in range(len(gates), min(STEPS, max(BANKS + BORROWED, group + LEAD[0] + 1))):
                 make_gate(0, ahead)
+            if group == 0:
+                round_places(nc.scalar.copy, w1b_grouped[:, GPSIMD_PLACES * HALF :], w1b, GPSIMD_PLACES, PACK)
             product(0, group)
             if group == W1B_AFTER + 1:
                 w_codes["w1", 1] = keep.tile([P, HALF], U32, align_bytes=64, name="w1b_codes")
                 w_scales["w1", 1] = keep.tile([P, HALF], U8, align_bytes=64, name="scales", tag="w1b_scales")
                 quantize(w_codes["w1", 1][:], w_scales["w1", 1][:], w1b_grouped[:])
-                w3b_low = round_on_gpsimd(w3b, "picked", 2)
+                w3b_grouped = round_on_gpsimd(w3b, "picked", GPSIMD_PLACES)
 
-        w3b_high = keep.tile([P, HALF * 2], BF16, align_bytes=64, name="high", tag="w3b_high")
-        round_places(nc.scalar.copy, w3b_high[:], w3b, 2, 4)
+        round_places(nc.scalar.copy, w3b_grouped[:, GPSIMD_PLACES * HALF :], w3b, GPSIMD_PLACES, PACK)
 
         middle = keep.tile([P, HALF + S], U8, align_bytes=64, name="scales", tag="middle_scales")
         w_codes["w3", 1] = keep.tile([P, HALF], U32, align_bytes=64, name="w3b_codes")
         w_scales["w3", 1] = middle[:, :HALF]
         h_scales = {(0, s): middle[:, HALF + s * SLICE : HALF + (s + 1) * SLICE] for s in range(slices)}
-        for part, values in enumerate((w3b_low, w3b_high)):
-            cols = slice(part * 2 * P, (part + 1) * 2 * P)
-            quantize(w_codes["w3", 1][:, cols], w_scales["w3", 1][:, cols], values[:])
+        quantize(w_codes["w3", 1][:], w_scales["w3", 1], w3b_grouped[:])
         for s in range(slices):
             quantize(h_codes[0, s][:], h_scales[0, s], hidden[0, s][:])
 

@@ -23,9 +23,10 @@ SLICE = 512
 GROUP = 128
 PAIR = 4
 HALF = 512
-VECTOR_UNTIL = 768
-PLACED_FROM = 1152
-WARM_PASSES = 4
+VECTOR_UNTIL = 704
+PLACED_FROM = 1280
+EARLY_UNTIL = 768
+WARM_PASSES = 5
 STORE = 256
 BANKS = 4
 BORROWED = 2
@@ -34,8 +35,9 @@ GROUPS = SLICE // GROUP
 STEPS = S // GROUP
 WIDTH = GROUP * PACK
 GPSIMD_GROUPS = 2
-W1B_AFTER = 4
-GPSIMD_PLACES = 3
+W1B_AFTER = 6
+RUNS = HALF // (PACK * PAIR)
+GPSIMD_RUNS = {"w1": 28, "w3": 16}
 W2_AFTER = 15
 END_AFTER = 19
 
@@ -72,9 +74,9 @@ def tile_picked_pick_glu_sigmoid_sub_e_kernel(tc, xT, w1, w3, w2, offs, out):
         planes = [keep.tile([P, T], F32, align_bytes=64, name="plane", tag=f"plane{j}") for j in range(PACK)]
         picked = keep.tile([P, S * PACK], BF16, align_bytes=64, name="picked", tag="picked")
         placed = picked[:].rearrange("p (n j) -> p n j", j=PACK)
-        late_rows = keep.tile([P, 2 * (S - PLACED_FROM)], BF16, align_bytes=64, name="late_rows")
+        late_rows = keep.tile([P, 2 * (S - PLACED_FROM)], BF16, align_bytes=64, name="late_rows", tag="late_rows")
         x_codes = {}
-        x_scales = [keep.tile([P, SLICE], U8, align_bytes=64, name=f"x_scales{s}") for s in range(slices)]
+        x_scales = {}
 
         def gather_plane(j):
             def window(start, done):
@@ -88,9 +90,13 @@ def tile_picked_pick_glu_sigmoid_sub_e_kernel(tc, xT, w1, w3, w2, offs, out):
                 nc.scalar.activation(late_rows[:, (j - 2) * count : (j - 1) * count], window(PLACED_FROM, S), Copy)
                 nc.scalar.activation(placed[:, VECTOR_UNTIL:PLACED_FROM, j], window(VECTOR_UNTIL, PLACED_FROM), Copy)
 
-        def quantize_x(s, tag):
-            x_codes[s] = keep.tile([P, SLICE], U32, align_bytes=64, name="x_codes", tag=tag)
-            quantize(x_codes[s][:], x_scales[s][:], picked[:, s * SLICE * PACK : (s + 1) * SLICE * PACK])
+        def quantize_x(start, done, tag):
+            codes = keep.tile([P, done - start], U32, align_bytes=64, name="x_codes", tag=tag)
+            scales = keep.tile([P, done - start], U8, align_bytes=64, name=f"x_scales{start}")
+            quantize(codes[:], scales[:], picked[:, start * PACK : done * PACK])
+            for first in range(start, done, GROUP):
+                x_codes[first // GROUP] = codes[:, first - start : first - start + GROUP]
+                x_scales[first // GROUP] = scales[:, first - start : first - start + GROUP]
 
         for j in range(PACK):
             nc.sync.dma_start(out=planes[j][:], in_=x_rows[:, j, :])
@@ -114,15 +120,17 @@ def tile_picked_pick_glu_sigmoid_sub_e_kernel(tc, xT, w1, w3, w2, offs, out):
         nc.gpsimd.memset(warm_scales[:], 0)
         nc.vector.tensor_copy(warm_values[:], planes[0][:, : SLICE * PACK])
         quantize(warm_codes[:], warm_scales[:], warm_values[:])
-        w1a = keep.tile([P, PACK, HALF], F32, align_bytes=64, name="raw", tag="w1a")
-        nc.sync.dma_start(out=w1a[:, :2], in_=rows_of(w1, 0)[:, :2])
         nc.sync.dma_start(out=warm_left[:].bitcast(I32), in_=warm_scales[:, :P].bitcast(I32))
-        nc.sync.dma_start(out=w1a[:, 2:], in_=rows_of(w1, 0)[:, 2:])
         idle = psum_3.tile([P, SLICE], F32, name="idle", tag="w3_bank")
         for i in range(WARM_PASSES):
             multiply(idle[:], warm_codes[:, :P], warm_left[:], warm_codes[:], warm_scales[:])
 
-        w3a = load_w(w3, 0, "w3a")
+        w1a = load_w(w1, 0, "w1a")
+        w3a = []
+        for piece in range(2):
+            raw = keep.tile([P, PACK, HALF // 2], F32, align_bytes=64, name=f"w3a_{piece}")
+            nc.sync.dma_start(out=raw[:], in_=rows_of(w3, 0)[:, :, piece * HALF // 2 : (piece + 1) * HALF // 2])
+            w3a.append(raw)
         w1b = load_w(w1, 1, "w1b")
         w3b = load_w(w3, 1, "w3b")
         w2_raw = keep.tile([P, 2, PACK, N], F32, name="w2_raw")
@@ -135,17 +143,23 @@ def tile_picked_pick_glu_sigmoid_sub_e_kernel(tc, xT, w1, w3, w2, offs, out):
             src = raw[:].rearrange("p j (q t r) -> p t q j r", t=PACK, r=PAIR)[:, t0:t1]
             copy(grouped.rearrange("p (t q r j) -> p t q j r", t=t1 - t0, r=PAIR, j=PACK), src)
 
-        def round_on_gpsimd(raw, tag, places):
-            grouped = keep.tile([P, HALF * PACK], BF16, align_bytes=64, name="grouped", tag=tag)
+        def round_on_gpsimd(raw, runs):
+            grouped = keep.tile([P, HALF * PACK], BF16, align_bytes=64, name="grouped", tag="picked")
             nc.gpsimd.tensor_scalar(
-                grouped[:, : HALF * places].rearrange("p (t q r j) -> p q t r j", t=places, r=PAIR, j=PACK),
-                raw[:].rearrange("p j (q t r) -> p q t r j", t=PACK, r=PAIR)[:, :, :places],
+                grouped[:].rearrange("p (t q r j) -> p q t r j", t=PACK, r=PAIR, j=PACK)[:, :runs],
+                raw[:].rearrange("p j (q t r) -> p q t r j", t=PACK, r=PAIR)[:, :runs],
                 1.0,
                 0.0,
                 mult,
                 add,
             )
             return grouped
+
+        def round_rest(grouped, raw, runs):
+            nc.scalar.copy(
+                grouped[:].rearrange("p (t q r j) -> p t q j r", t=PACK, r=PAIR, j=PACK)[:, :, runs:],
+                raw[:].rearrange("p j (q t r) -> p t q j r", t=PACK, r=PAIR)[:, :, runs:],
+            )
 
         w_codes = {}
         w_scales = {}
@@ -157,7 +171,8 @@ def tile_picked_pick_glu_sigmoid_sub_e_kernel(tc, xT, w1, w3, w2, offs, out):
             cols = slice(t0 * P, t1 * P)
             quantize(w_codes[name, 0][:, cols], w_scales[name, 0][:, cols], values)
 
-        quantize_x(0, "x_codes0")
+        quantize_x(PLACED_FROM, S, "x_codes_placed")
+        quantize_x(0, SLICE, "late_rows")
         w1a_low = keep.tile([P, HALF * 2], BF16, align_bytes=64, name="w1a_low")
         w1a_high = keep.tile([P, HALF * 2], BF16, align_bytes=64, name="w1a_high")
         round_places(nc.scalar.copy, w1a_high[:], w1a, 2, 4)
@@ -166,18 +181,25 @@ def tile_picked_pick_glu_sigmoid_sub_e_kernel(tc, xT, w1, w3, w2, offs, out):
         for t in range(2):
             quantize_places("w1", t, t + 1, w1a_low[:, t * HALF : (t + 1) * HALF])
         quantize_places("w1", 2, 4, w1a_high[:])
-        quantize_x(1, "w1a")
+        quantize_x(SLICE, EARLY_UNTIL, "w1a")
 
-        w3a_low = keep.tile([P, HALF * 2], BF16, align_bytes=64, name="w3a_low")
-        w3a_high = keep.tile([P, HALF * 2], BF16, align_bytes=64, name="w3a_high", tag="w3a_high")
-        round_places(nc.scalar.copy, w3a_high[:, HALF:], w3a, 3, 4)
-        round_places(nc.vector.tensor_copy, w3a_low[:], w3a, 0, 2)
-        round_places(nc.vector.tensor_copy, w3a_high[:, :HALF], w3a, 2, 3)
-        quantize_places("w3", 0, 2, w3a_low[:])
-        quantize_places("w3", 2, 4, w3a_high[:])
-        quantize_x(2, "w3a_high")
+        w3a_grouped = keep.tile([P, HALF * PACK], BF16, align_bytes=64, name="w3a_grouped", tag="w3a_grouped")
 
-        w1b_grouped = round_on_gpsimd(w1b, "picked", GPSIMD_PLACES)
+        def round_piece(copy, piece, t0, t1):
+            runs = HALF // 2 // (PACK * PAIR)
+            dst = w3a_grouped[:].rearrange("p (t q r j) -> p t q j r", t=PACK, r=PAIR, j=PACK)
+            src = w3a[piece][:].rearrange("p j (q t r) -> p t q j r", t=PACK, r=PAIR)
+            copy(dst[:, t0:t1, piece * runs : (piece + 1) * runs], src[:, t0:t1])
+
+        round_piece(nc.scalar.copy, 0, 0, PACK)
+        round_piece(nc.scalar.copy, 1, 3, PACK)
+        round_piece(nc.vector.tensor_copy, 1, 0, 2)
+        round_piece(nc.vector.tensor_copy, 1, 2, 3)
+        quantize_places("w3", 0, 2, w3a_grouped[:, : 2 * HALF])
+        quantize_places("w3", 2, 4, w3a_grouped[:, 2 * HALF :])
+        quantize_x(EARLY_UNTIL, PLACED_FROM, "w3a_grouped")
+
+        w1b_grouped = round_on_gpsimd(w1b, GPSIMD_RUNS["w1"])
 
         holds = {W1B_AFTER: "w1b_scales", W2_AFTER: "w2_grouped", STEPS - 2: "middle_scales", END_AFTER: "end_scales"}
         by_token = "p (t c) -> p c t"
@@ -189,16 +211,14 @@ def tile_picked_pick_glu_sigmoid_sub_e_kernel(tc, xT, w1, w3, w2, offs, out):
 
         def passes(name, h, group, ring):
             bank = rings[ring].tile([P, WIDTH], F32, name="bank", tag=f"{ring}_bank")
-            s, c = divmod(group, GROUPS)
-            n_cols = slice(c * GROUP, (c + 1) * GROUP)
             for t in range(PACK):
                 m_cols = slice(t * P, (t + 1) * P)
                 multiply(
                     bank[:, t * GROUP : (t + 1) * GROUP],
                     w_codes[name, h][:, m_cols],
                     w_scales[name, h][:, m_cols],
-                    x_codes[s][:, n_cols],
-                    x_scales[s][:, n_cols],
+                    x_codes[group],
+                    x_scales[group],
                 )
             return bank[:].rearrange(by_token, t=PACK)
 
@@ -230,15 +250,15 @@ def tile_picked_pick_glu_sigmoid_sub_e_kernel(tc, xT, w1, w3, w2, offs, out):
             for ahead in range(len(gates), min(STEPS, max(BANKS + BORROWED, group + LEAD[0] + 1))):
                 make_gate(0, ahead)
             if group == 0:
-                round_places(nc.scalar.copy, w1b_grouped[:, GPSIMD_PLACES * HALF :], w1b, GPSIMD_PLACES, PACK)
+                round_rest(w1b_grouped, w1b, GPSIMD_RUNS["w1"])
             product(0, group)
             if group == W1B_AFTER + 1:
                 w_codes["w1", 1] = keep.tile([P, HALF], U32, align_bytes=64, name="w1b_codes")
                 w_scales["w1", 1] = keep.tile([P, HALF], U8, align_bytes=64, name="scales", tag="w1b_scales")
                 quantize(w_codes["w1", 1][:], w_scales["w1", 1][:], w1b_grouped[:])
-                w3b_grouped = round_on_gpsimd(w3b, "picked", GPSIMD_PLACES)
+                w3b_grouped = round_on_gpsimd(w3b, GPSIMD_RUNS["w3"])
 
-        round_places(nc.scalar.copy, w3b_grouped[:, GPSIMD_PLACES * HALF :], w3b, GPSIMD_PLACES, PACK)
+        round_rest(w3b_grouped, w3b, GPSIMD_RUNS["w3"])
 
         middle = keep.tile([P, HALF + S], U8, align_bytes=64, name="scales", tag="middle_scales")
         w_codes["w3", 1] = keep.tile([P, HALF], U32, align_bytes=64, name="w3b_codes")

@@ -35,10 +35,11 @@ GROUPS = SLICE // GROUP
 STEPS = S // GROUP
 WIDTH = GROUP * PACK
 GPSIMD_GROUPS = 2
-W1B_AFTER = 6
+W1B_AFTER = 5
 RUNS = HALF // (PACK * PAIR)
-GPSIMD_RUNS = {"w1": 28, "w3": 16}
+GPSIMD_RUNS = {"w1": 29, "w3": 21}
 W2_AFTER = 15
+W2_GATE = 20
 END_AFTER = 19
 
 
@@ -120,12 +121,14 @@ def tile_picked_pick_glu_sigmoid_sub_e_kernel(tc, xT, w1, w3, w2, offs, out):
         nc.gpsimd.memset(warm_scales[:], 0)
         nc.vector.tensor_copy(warm_values[:], planes[0][:, : SLICE * PACK])
         quantize(warm_codes[:], warm_scales[:], warm_values[:])
+        w1a = keep.tile([P, PACK, HALF], F32, align_bytes=64, name="raw", tag="w1a")
+        nc.sync.dma_start(out=w1a[:, :2], in_=rows_of(w1, 0)[:, :2])
         nc.sync.dma_start(out=warm_left[:].bitcast(I32), in_=warm_scales[:, :P].bitcast(I32))
+        nc.sync.dma_start(out=w1a[:, 2:], in_=rows_of(w1, 0)[:, 2:])
         idle = psum_3.tile([P, SLICE], F32, name="idle", tag="w3_bank")
         for i in range(WARM_PASSES):
             multiply(idle[:], warm_codes[:, :P], warm_left[:], warm_codes[:], warm_scales[:])
 
-        w1a = load_w(w1, 0, "w1a")
         w3a = []
         for piece in range(2):
             raw = keep.tile([P, PACK, HALF // 2], F32, align_bytes=64, name=f"w3a_{piece}")
@@ -145,13 +148,9 @@ def tile_picked_pick_glu_sigmoid_sub_e_kernel(tc, xT, w1, w3, w2, offs, out):
 
         def round_on_gpsimd(raw, runs):
             grouped = keep.tile([P, HALF * PACK], BF16, align_bytes=64, name="grouped", tag="picked")
-            nc.gpsimd.tensor_scalar(
+            nc.gpsimd.tensor_copy(
                 grouped[:].rearrange("p (t q r j) -> p q t r j", t=PACK, r=PAIR, j=PACK)[:, :runs],
                 raw[:].rearrange("p j (q t r) -> p q t r j", t=PACK, r=PAIR)[:, :runs],
-                1.0,
-                0.0,
-                mult,
-                add,
             )
             return grouped
 
@@ -279,7 +278,7 @@ def tile_picked_pick_glu_sigmoid_sub_e_kernel(tc, xT, w1, w3, w2, offs, out):
         for group in range(GPSIMD_GROUPS, END_AFTER + 2 - STEPS):
             for ahead in range(len(gates) - STEPS, min(STEPS, group + LEAD[1] + 1)):
                 make_gate(1, ahead)
-                if STEPS + ahead == END_AFTER + 2:
+                if STEPS + ahead == W2_GATE:
                     w2_grouped = keep.tile([P, 2 * N * PACK], BF16, align_bytes=64, name="w2_grouped", tag="w2_grouped")
                     nc.scalar.copy(
                         w2_grouped[:].rearrange("p (g m r t) -> p g m t r", g=2, r=PAIR, t=PACK),
@@ -319,9 +318,10 @@ def tile_picked_pick_glu_sigmoid_sub_e_kernel(tc, xT, w1, w3, w2, offs, out):
         split = GPSIMD_GROUPS * GROUP
         quantize_h(0, 0, split, firsts[:])
         quantize_h(0, split, SLICE, hidden[1, 0][:, split * PACK :])
+        quantize_h(1, 0, SLICE // 2, hidden[1, 1][:, : SLICE * PACK // 2])
         quantize(w2_codes[:], w2_scales, w2_grouped[:])
         finish(0, 0, SLICE)
-        quantize_h(1, 0, SLICE, hidden[1, 1][:])
+        quantize_h(1, SLICE // 2, SLICE, hidden[1, 1][:, SLICE * PACK // 2 :])
         finish(1, 0, SLICE)
         last = slices - 1
         for group in range(END_AFTER + 2 - STEPS, 2 * GROUPS + 2 + 1):

@@ -37,7 +37,7 @@ WIDTH = GROUP * PACK
 GPSIMD_GROUPS = 2
 W1B_AFTER = 5
 RUNS = HALF // (PACK * PAIR)
-GPSIMD_RUNS = {"w1": 29, "w3": 21}
+GPSIMD_RUNS = {"w1": 26, "w3": 20}
 W2_AFTER = 15
 W2_GATE = 20
 END_AFTER = 19
@@ -318,10 +318,9 @@ def tile_picked_pick_glu_sigmoid_sub_e_kernel(tc, xT, w1, w3, w2, offs, out):
         split = GPSIMD_GROUPS * GROUP
         quantize_h(0, 0, split, firsts[:])
         quantize_h(0, split, SLICE, hidden[1, 0][:, split * PACK :])
-        quantize_h(1, 0, SLICE // 2, hidden[1, 1][:, : SLICE * PACK // 2])
         quantize(w2_codes[:], w2_scales, w2_grouped[:])
         finish(0, 0, SLICE)
-        quantize_h(1, SLICE // 2, SLICE, hidden[1, 1][:, SLICE * PACK // 2 :])
+        quantize_h(1, 0, SLICE, hidden[1, 1][:])
         finish(1, 0, SLICE)
         last = slices - 1
         for group in range(END_AFTER + 2 - STEPS, 2 * GROUPS + 2 + 1):

@@ -39,8 +39,9 @@ W1B_AFTER = 5
 RUNS = HALF // (PACK * PAIR)
 GPSIMD_RUNS = {"w1": 26, "w3": 20}
 W2_AFTER = 15
-W2_GATE = 20
-END_AFTER = 19
+W2_GATE = 21
+LAST_SHARE = 64
+END_AFTER = 20
 
 
 def tile_picked_pick_glu_sigmoid_sub_e_kernel(tc, xT, w1, w3, w2, offs, out):
@@ -317,17 +318,26 @@ def tile_picked_pick_glu_sigmoid_sub_e_kernel(tc, xT, w1, w3, w2, offs, out):
 
         split = GPSIMD_GROUPS * GROUP
         quantize_h(0, 0, split, firsts[:])
-        quantize_h(0, split, SLICE, hidden[1, 0][:, split * PACK :])
         quantize(w2_codes[:], w2_scales, w2_grouped[:])
+        quantize_h(0, split, SLICE, hidden[1, 0][:, split * PACK :])
         finish(0, 0, SLICE)
         quantize_h(1, 0, SLICE, hidden[1, 1][:])
         finish(1, 0, SLICE)
         last = slices - 1
-        for group in range(END_AFTER + 2 - STEPS, 2 * GROUPS + 2 + 1):
-            product(1, group)
         quantize_h(last, 0, 2 * GROUP, hidden[1, last][:, : 2 * WIDTH])
         finish(last, 0, 2 * GROUP)
-        product(1, STEPS - 1)
-        for c in (2, 3):
-            quantize_h(last, c * GROUP, (c + 1) * GROUP, hidden[1, last][:, c * WIDTH : (c + 1) * WIDTH])
+
+        cut = LAST_SHARE * PACK
+        final_bank = passes("w3", 1, STEPS - 1, "w3")
+        final_gate = gates[1, STEPS - 1]
+        final_up = keep.tile([P, cut], F32, align_bytes=64, name="final_up")
+        nc.scalar.copy(final_up[:].rearrange(in_order, t=PACK), final_bank[:, :LAST_SHARE])
+        final = keep.tile([P, WIDTH], BF16, align_bytes=64, name="final", tag="hidden1_1")
+        nc.gpsimd.tensor_tensor(final[:, :cut], final_gate[:, :cut], final_up[:], mult)
+        product(1, STEPS - 2)
+        nc.vector.tensor_tensor(
+            final[:, cut:].rearrange(in_order, t=PACK), final_gate[:, cut:].rearrange(in_order, t=PACK), final_bank[:, LAST_SHARE:], mult
+        )
+        for c, values in ((2, hidden[1, last][:, 2 * WIDTH : 3 * WIDTH]), (3, final[:])):
+            quantize_h(last, c * GROUP, (c + 1) * GROUP, values)
             finish(last, c * GROUP, (c + 1) * GROUP)

@@ -39,9 +39,9 @@ W1B_AFTER = 5
 RUNS = HALF // (PACK * PAIR)
 GPSIMD_RUNS = {"w1": 26, "w3": 20}
 W2_AFTER = 15
-W2_GATE = 21
-LAST_SHARE = 64
-END_AFTER = 20
+W2_GATE = 20
+LAST_SHARE = 48
+END_AFTER = 19
 
 
 def tile_picked_pick_glu_sigmoid_sub_e_kernel(tc, xT, w1, w3, w2, offs, out):
@@ -321,8 +321,11 @@ def tile_picked_pick_glu_sigmoid_sub_e_kernel(tc, xT, w1, w3, w2, offs, out):
         quantize(w2_codes[:], w2_scales, w2_grouped[:])
         quantize_h(0, split, SLICE, hidden[1, 0][:, split * PACK :])
         finish(0, 0, SLICE)
-        quantize_h(1, 0, SLICE, hidden[1, 1][:])
-        finish(1, 0, SLICE)
+        quantize_h(1, 0, 2 * GROUP, hidden[1, 1][:, : 2 * WIDTH])
+        finish(1, 0, 2 * GROUP)
+        product(1, STEPS - 3)
+        quantize_h(1, 2 * GROUP, SLICE, hidden[1, 1][:, 2 * WIDTH :])
+        finish(1, 2 * GROUP, SLICE)
         last = slices - 1
         quantize_h(last, 0, 2 * GROUP, hidden[1, last][:, : 2 * WIDTH])
         finish(last, 0, 2 * GROUP)

@@ -40,7 +40,7 @@ RUNS = HALF // (PACK * PAIR)
 GPSIMD_RUNS = {"w1": 26, "w3": 20}
 W2_AFTER = 15
 W2_GATE = 20
-LAST_SHARE = 48
+LAST_SHARE = 88
 END_AFTER = 19
 
 
@@ -323,12 +323,11 @@ def tile_picked_pick_glu_sigmoid_sub_e_kernel(tc, xT, w1, w3, w2, offs, out):
         finish(0, 0, SLICE)
         quantize_h(1, 0, 2 * GROUP, hidden[1, 1][:, : 2 * WIDTH])
         finish(1, 0, 2 * GROUP)
-        product(1, STEPS - 3)
         quantize_h(1, 2 * GROUP, SLICE, hidden[1, 1][:, 2 * WIDTH :])
         finish(1, 2 * GROUP, SLICE)
         last = slices - 1
-        quantize_h(last, 0, 2 * GROUP, hidden[1, last][:, : 2 * WIDTH])
-        finish(last, 0, 2 * GROUP)
+        quantize_h(last, 0, GROUP, hidden[1, last][:, :WIDTH])
+        finish(last, 0, GROUP)
 
         cut = LAST_SHARE * PACK
         final_bank = passes("w3", 1, STEPS - 1, "w3")
@@ -337,10 +336,11 @@ def tile_picked_pick_glu_sigmoid_sub_e_kernel(tc, xT, w1, w3, w2, offs, out):
         nc.scalar.copy(final_up[:].rearrange(in_order, t=PACK), final_bank[:, :LAST_SHARE])
         final = keep.tile([P, WIDTH], BF16, align_bytes=64, name="final", tag="hidden1_1")
         nc.gpsimd.tensor_tensor(final[:, :cut], final_gate[:, :cut], final_up[:], mult)
+        product(1, STEPS - 3)
         product(1, STEPS - 2)
         nc.vector.tensor_tensor(
             final[:, cut:].rearrange(in_order, t=PACK), final_gate[:, cut:].rearrange(in_order, t=PACK), final_bank[:, LAST_SHARE:], mult
         )
-        for c, values in ((2, hidden[1, last][:, 2 * WIDTH : 3 * WIDTH]), (3, final[:])):
+        for c, values in ((1, hidden[1, last][:, WIDTH : 2 * WIDTH]), (2, hidden[1, last][:, 2 * WIDTH : 3 * WIDTH]), (3, final[:])):
             quantize_h(last, c * GROUP, (c + 1) * GROUP, values)
             finish(last, c * GROUP, (c + 1) * GROUP)

@@ -40,6 +40,8 @@ RUNS = HALF // (PACK * PAIR)
 GPSIMD_RUNS = {"w1": 26, "w3": 20}
 W2_AFTER = 15
 W2_GATE = 20
+FIRST_SHARE = 48
+LAST_GROUP = STEPS - 3
 LAST_SHARE = 88
 END_AFTER = 19
 
@@ -205,7 +207,7 @@ def tile_picked_pick_glu_sigmoid_sub_e_kernel(tc, xT, w1, w3, w2, offs, out):
         by_token = "p (t c) -> p c t"
         in_order = "p (c t) -> p c t"
         gate_rows = [keep.tile([P, T], F32, align_bytes=64, name="gates", tag=f"plane{j}") for j in range(slices)]
-        ups = keep.tile([P, GPSIMD_GROUPS * WIDTH], F32, align_bytes=64, name="ups", tag="plane3")
+        ups = keep.tile([P, GPSIMD_GROUPS * WIDTH + FIRST_SHARE * PACK], F32, align_bytes=64, name="ups", tag="plane3")
         hidden = {}
         rings = {"w1": psum_1, "w3": psum_3}
 
@@ -268,16 +270,25 @@ def tile_picked_pick_glu_sigmoid_sub_e_kernel(tc, xT, w1, w3, w2, offs, out):
         for s in range(slices):
             quantize(h_codes[0, s][:], h_scales[0, s], hidden[0, s][:])
 
-        firsts = keep.tile([P, GPSIMD_GROUPS * WIDTH], BF16, align_bytes=64, name="firsts", tag=f"hidden0_{slices - 1}")
-        for group in range(GPSIMD_GROUPS):
+        firsts = keep.tile([P, (GPSIMD_GROUPS + 1) * WIDTH], BF16, align_bytes=64, name="firsts", tag=f"hidden0_{slices - 2}")
+        row, place = divmod(STEPS, T // WIDTH)
+        first_gates = gate_rows[row][:, place * WIDTH : (place + GPSIMD_GROUPS + 1) * WIDTH]
+        whole = GPSIMD_GROUPS * WIDTH
+        shared = whole + FIRST_SHARE * PACK
+        for group in range(GPSIMD_GROUPS + 1):
             make_gate(1, group)
         for group in range(GPSIMD_GROUPS):
             up = ups[:, group * WIDTH : (group + 1) * WIDTH]
             nc.scalar.copy(up.rearrange(in_order, t=PACK), passes("w3", 1, group, "w3"))
-        row, place = divmod(STEPS, T // WIDTH)
-        nc.gpsimd.tensor_tensor(firsts[:], gate_rows[row][:, place * WIDTH : (place + GPSIMD_GROUPS) * WIDTH], ups[:], mult)
-        for group in range(GPSIMD_GROUPS, END_AFTER + 2 - STEPS):
-            for ahead in range(len(gates) - STEPS, min(STEPS, group + LEAD[1] + 1)):
+        shared_bank = passes("w3", 1, GPSIMD_GROUPS, "w3")
+        nc.vector.tensor_tensor(
+            firsts[:, shared:].rearrange(in_order, t=PACK), first_gates[:, shared:].rearrange(in_order, t=PACK), shared_bank[:, FIRST_SHARE:], mult
+        )
+        nc.scalar.copy(ups[:, whole:].rearrange(in_order, t=PACK), shared_bank[:, :FIRST_SHARE])
+        for start, done in ((0, WIDTH), (WIDTH, shared)):
+            nc.gpsimd.tensor_tensor(firsts[:, start:done], first_gates[:, start:done], ups[:, start:done], mult)
+        for group in range(GPSIMD_GROUPS + 1, END_AFTER + 2 - STEPS):
+            for ahead in range(len(gates) - STEPS, min(LAST_GROUP + 1, group + LEAD[1] + 1)):
                 make_gate(1, ahead)
                 if STEPS + ahead == W2_GATE:
                     w2_grouped = keep.tile([P, 2 * N * PACK], BF16, align_bytes=64, name="w2_grouped", tag="w2_grouped")
@@ -287,7 +298,12 @@ def tile_picked_pick_glu_sigmoid_sub_e_kernel(tc, xT, w1, w3, w2, offs, out):
                     )
             product(1, group)
 
-        for ahead in range(len(gates) - STEPS, STEPS):
+        cut = LAST_SHARE * PACK
+        final_bank = passes("w3", 1, LAST_GROUP, "w3")
+        final_gate = gates[1, LAST_GROUP]
+        final_up = keep.tile([P, cut], F32, align_bytes=64, name="final_up")
+        nc.scalar.copy(final_up[:].rearrange(in_order, t=PACK), final_bank[:, :LAST_SHARE])
+        for ahead in range(LAST_GROUP + 1, STEPS):
             make_gate(1, ahead)
 
         end = keep.tile([P, S + 2 * N], U8, align_bytes=64, name="scales", tag="end_scales")
@@ -316,7 +332,7 @@ def tile_picked_pick_glu_sigmoid_sub_e_kernel(tc, xT, w1, w3, w2, offs, out):
                 until = min(done, first + STORE)
                 nc.sync.dma_start(out=out[:, s * SLICE + first : s * SLICE + until], in_=y[:, first - start : until - start])
 
-        split = GPSIMD_GROUPS * GROUP
+        split = (GPSIMD_GROUPS + 1) * GROUP
         quantize_h(0, 0, split, firsts[:])
         quantize(w2_codes[:], w2_scales, w2_grouped[:])
         quantize_h(0, split, SLICE, hidden[1, 0][:, split * PACK :])
@@ -329,18 +345,13 @@ def tile_picked_pick_glu_sigmoid_sub_e_kernel(tc, xT, w1, w3, w2, offs, out):
         quantize_h(last, 0, GROUP, hidden[1, last][:, :WIDTH])
         finish(last, 0, GROUP)
 
-        cut = LAST_SHARE * PACK
-        final_bank = passes("w3", 1, STEPS - 1, "w3")
-        final_gate = gates[1, STEPS - 1]
-        final_up = keep.tile([P, cut], F32, align_bytes=64, name="final_up")
-        nc.scalar.copy(final_up[:].rearrange(in_order, t=PACK), final_bank[:, :LAST_SHARE])
         final = keep.tile([P, WIDTH], BF16, align_bytes=64, name="final", tag="hidden1_1")
         nc.gpsimd.tensor_tensor(final[:, :cut], final_gate[:, :cut], final_up[:], mult)
-        product(1, STEPS - 3)
         product(1, STEPS - 2)
+        product(1, STEPS - 1)
         nc.vector.tensor_tensor(
             final[:, cut:].rearrange(in_order, t=PACK), final_gate[:, cut:].rearrange(in_order, t=PACK), final_bank[:, LAST_SHARE:], mult
         )
-        for c, values in ((1, hidden[1, last][:, WIDTH : 2 * WIDTH]), (2, hidden[1, last][:, 2 * WIDTH : 3 * WIDTH]), (3, final[:])):
+        for c, values in ((2, hidden[1, last][:, 2 * WIDTH : 3 * WIDTH]), (3, hidden[1, last][:, 3 * WIDTH :]), (1, final[:])):
             quantize_h(last, c * GROUP, (c + 1) * GROUP, values)
             finish(last, c * GROUP, (c + 1) * GROUP)

@@ -40,9 +40,9 @@ RUNS = HALF // (PACK * PAIR)
 GPSIMD_RUNS = {"w1": 26, "w3": 20}
 W2_AFTER = 15
 W2_GATE = 20
-FIRST_SHARE = 48
+FIRST_SHARE = 24
 LAST_GROUP = STEPS - 3
-LAST_SHARE = 88
+LAST_SHARE = 80
 END_AFTER = 19
 
 
@@ -208,7 +208,8 @@ def tile_picked_pick_glu_sigmoid_sub_e_kernel(tc, xT, w1, w3, w2, offs, out):
         in_order = "p (c t) -> p c t"
         gate_rows = [keep.tile([P, T], F32, align_bytes=64, name="gates", tag=f"plane{j}") for j in range(slices)]
         ups = keep.tile([P, GPSIMD_GROUPS * WIDTH + FIRST_SHARE * PACK], F32, align_bytes=64, name="ups", tag="plane3")
-        hidden = {}
+        early_hidden = keep.tile([P, 2 * SLICE * PACK], BF16, align_bytes=64, name="early_hidden", tag="hidden0_1")
+        hidden = {(0, s): early_hidden[:, s * SLICE * PACK : (s + 1) * SLICE * PACK] for s in range(2)}
         rings = {"w1": psum_1, "w3": psum_3}
 
         def passes(name, h, group, ring):
@@ -245,7 +246,8 @@ def tile_picked_pick_glu_sigmoid_sub_e_kernel(tc, xT, w1, w3, w2, offs, out):
             bank = passes("w3", h, group, "w3")
             nc.vector.tensor_tensor(values.rearrange(in_order, t=PACK), gates[h, group].rearrange(in_order, t=PACK), bank, mult)
 
-        h_codes = {(h, s): keep.tile([P, SLICE], U32, align_bytes=64, name=f"h_codes{h}_{s}") for h in range(2) for s in range(slices)}
+        half_codes = [keep.tile([P, S], U32, align_bytes=64, name=f"h_codes{h}") for h in range(2)]
+        h_codes = {(h, s): half_codes[h][:, s * SLICE : (s + 1) * SLICE] for h in range(2) for s in range(slices)}
         w2_codes = keep.tile([P, 2 * N], U32, align_bytes=64, name="w2_codes")
 
         for group in range(STEPS):
@@ -267,8 +269,8 @@ def tile_picked_pick_glu_sigmoid_sub_e_kernel(tc, xT, w1, w3, w2, offs, out):
         w_scales["w3", 1] = middle[:, :HALF]
         h_scales = {(0, s): middle[:, HALF + s * SLICE : HALF + (s + 1) * SLICE] for s in range(slices)}
         quantize(w_codes["w3", 1][:], w_scales["w3", 1], w3b_grouped[:])
-        for s in range(slices):
-            quantize(h_codes[0, s][:], h_scales[0, s], hidden[0, s][:])
+        quantize(half_codes[0][:, : 2 * SLICE], middle[:, HALF : HALF + 2 * SLICE], early_hidden[:])
+        quantize(h_codes[0, 2], h_scales[0, 2], hidden[0, 2][:])
 
         firsts = keep.tile([P, (GPSIMD_GROUPS + 1) * WIDTH], BF16, align_bytes=64, name="firsts", tag=f"hidden0_{slices - 2}")
         row, place = divmod(STEPS, T // WIDTH)

from contextlib import ExitStack

import concourse.mybir as mybir

K, T, S, H, N = 512, 4096, 1536, 1024, 128
FLOPS = 2 * S * (2 * K * H + H * N)

P = 128
PACK = 4
F32 = mybir.dt.float32
BF16 = mybir.dt.bfloat16
U32 = mybir.dt.uint32
I32 = mybir.dt.int32
U16 = mybir.dt.uint16
U8 = mybir.dt.uint8
FP8X4 = mybir.dt.float8_e4m3fn_x4
Copy = mybir.ActivationFunctionType.Copy
Sigmoid = mybir.ActivationFunctionType.Sigmoid
mult = mybir.AluOpType.mult
add = mybir.AluOpType.add

SLICE = 512
GROUP = 128
PAIR = 4
HALF = 512
VECTOR_UNTIL = 704
PLACED_FROM = 1280
EARLY_UNTIL = 768
WARM_PASSES = 5
STORE = 256
BANKS = 4
BORROWED = 2
LEAD = (3, 3)
GROUPS = SLICE // GROUP
STEPS = S // GROUP
WIDTH = GROUP * PACK
GPSIMD_GROUPS = 2
W1B_AFTER = 5
RUNS = HALF // (PACK * PAIR)
GPSIMD_RUNS = {"w1": 26, "w3": 20}
W2_AFTER = 15
W2_GATE = 20
FIRST_SHARE = 24
LAST_GROUP = STEPS - 3
LAST_SHARE = 80
END_AFTER = 19


def tile_picked_pick_glu_sigmoid_sub_e_kernel(tc, xT, w1, w3, w2, offs, out):
    nc = tc.nc
    slices = S // SLICE
    with ExitStack() as ctx:
        keep = ctx.enter_context(tc.tile_pool(name="keep", bufs=1))
        psum_1 = ctx.enter_context(tc.psum_pool(name="psum_1", bufs=4))
        psum_3 = ctx.enter_context(tc.psum_pool(name="psum_3", bufs=4))

        def quantize(codes, scales, values):
            nc.vector.quantize_mx(out=codes.bitcast(FP8X4), scales=scales, in_=values)

        def multiply(bank, left, left_scales, right, right_scales, start=True, stop=True):
            nc.tensor.matmul_mx(
                out=bank,
                lhsT=left.bitcast(FP8X4),
                lhsT_scale=left_scales,
                rhs=right.bitcast(FP8X4),
                rhs_scale=right_scales,
                start=start,
                stop=stop,
            )

        offsets = keep.tile([P, S // 16], U16, name="offsets")

        warm = keep.tile([P, 8], F32, name="warm")
        nc.vector.memset(warm[:], 0.0)
        nc.scalar.activation(warm[:, 0:1], warm[:, 0:1], Sigmoid)

        x_rows = xT.rearrange("(p j) t -> p j t", j=PACK)
        planes = [keep.tile([P, T], F32, align_bytes=64, name="plane", tag=f"plane{j}") for j in range(PACK)]
        picked = keep.tile([P, S * PACK], BF16, align_bytes=64, name="picked", tag="picked")
        placed = picked[:].rearrange("p (n j) -> p n j", j=PACK)
        late_rows = keep.tile([P, 2 * (S - PLACED_FROM)], BF16, align_bytes=64, name="late_rows", tag="late_rows")
        x_codes = {}
        x_scales = {}

        def gather_plane(j):
            def window(start, done):
                return planes[j][:].indirect(offsets[:, start // 16 : done // 16])

            nc.vector.tensor_copy(placed[:, :VECTOR_UNTIL, j], window(0, VECTOR_UNTIL))
            if j < 2:
                nc.scalar.activation(placed[:, VECTOR_UNTIL:, j], window(VECTOR_UNTIL, S), Copy)
            else:
                count = S - PLACED_FROM
                nc.scalar.activation(late_rows[:, (j - 2) * count : (j - 1) * count], window(PLACED_FROM, S), Copy)
                nc.scalar.activation(placed[:, VECTOR_UNTIL:PLACED_FROM, j], window(VECTOR_UNTIL, PLACED_FROM), Copy)

        def quantize_x(start, done, tag):
            codes = keep.tile([P, done - start], U32, align_bytes=64, name="x_codes", tag=tag)
            scales = keep.tile([P, done - start], U8, align_bytes=64, name=f"x_scales{start}")
            quantize(codes[:], scales[:], picked[:, start * PACK : done * PACK])
            for first in range(start, done, GROUP):
                x_codes[first // GROUP] = codes[:, first - start : first - start + GROUP]
                x_scales[first // GROUP] = scales[:, first - start : first - start + GROUP]

        for j in range(PACK):
            nc.sync.dma_start(out=planes[j][:], in_=x_rows[:, j, :])
            if j == 0:
                nc.sync.dma_start(offsets[:], offs)
            gather_plane(j)
        nc.gpsimd.tensor_scalar(placed[:, PLACED_FROM:, 2:4], late_rows[:].rearrange("p (j n) -> p n j", j=2), 1.0, 0.0, mult, add)

        def rows_of(w, h):
            return w.rearrange("(p j) c -> p j c", j=PACK)[:, :, h * HALF : (h + 1) * HALF]

        def load_w(w, h, tag):
            raw = keep.tile([P, PACK, HALF], F32, align_bytes=64, name="raw", tag=tag)
            nc.sync.dma_start(out=raw[:], in_=rows_of(w, h))
            return raw

        warm_values = keep.tile([P, SLICE * PACK], BF16, align_bytes=64, name="warm_values")
        warm_codes = keep.tile([P, SLICE], U32, align_bytes=64, name="warm_codes")
        warm_scales = keep.tile([P, SLICE], U8, align_bytes=64, name="warm_scales")
        warm_left = keep.tile([P, P], U8, align_bytes=64, name="warm_left")
        nc.gpsimd.memset(warm_scales[:], 0)
        nc.vector.tensor_copy(warm_values[:], planes[0][:, : SLICE * PACK])
        quantize(warm_codes[:], warm_scales[:], warm_values[:])
        w1a = keep.tile([P, PACK, HALF], F32, align_bytes=64, name="raw", tag="w1a")
        nc.sync.dma_start(out=w1a[:, :2], in_=rows_of(w1, 0)[:, :2])
        nc.sync.dma_start(out=warm_left[:].bitcast(I32), in_=warm_scales[:, :P].bitcast(I32))
        nc.sync.dma_start(out=w1a[:, 2:], in_=rows_of(w1, 0)[:, 2:])
        idle = psum_3.tile([P, SLICE], F32, name="idle", tag="w3_bank")
        for i in range(WARM_PASSES):
            multiply(idle[:], warm_codes[:, :P], warm_left[:], warm_codes[:], warm_scales[:])

        w3a = []
        for piece in range(2):
            raw = keep.tile([P, PACK, HALF // 2], F32, align_bytes=64, name=f"w3a_{piece}")
            nc.sync.dma_start(out=raw[:], in_=rows_of(w3, 0)[:, :, piece * HALF // 2 : (piece + 1) * HALF // 2])
            w3a.append(raw)
        w1b = load_w(w1, 1, "w1b")
        w3b = load_w(w3, 1, "w3b")
        w2_raw = keep.tile([P, 2, PACK, N], F32, name="w2_raw")
        for g in range(2):
            w2_rows = w2[g * HALF : (g + 1) * HALF].rearrange("(q t r) m -> t q r m", t=PACK, r=PAIR)
            for t in range(PACK):
                nc.sync.dma_start(out=w2_raw[:, g, t, :], in_=w2_rows[t])

        def round_places(copy, grouped, raw, t0, t1):
            src = raw[:].rearrange("p j (q t r) -> p t q j r", t=PACK, r=PAIR)[:, t0:t1]
            copy(grouped.rearrange("p (t q r j) -> p t q j r", t=t1 - t0, r=PAIR, j=PACK), src)

        def round_on_gpsimd(raw, runs):
            grouped = keep.tile([P, HALF * PACK], BF16, align_bytes=64, name="grouped", tag="picked")
            nc.gpsimd.tensor_copy(
                grouped[:].rearrange("p (t q r j) -> p q t r j", t=PACK, r=PAIR, j=PACK)[:, :runs],
                raw[:].rearrange("p j (q t r) -> p q t r j", t=PACK, r=PAIR)[:, :runs],
            )
            return grouped

        def round_rest(grouped, raw, runs):
            nc.scalar.copy(
                grouped[:].rearrange("p (t q r j) -> p t q j r", t=PACK, r=PAIR, j=PACK)[:, :, runs:],
                raw[:].rearrange("p j (q t r) -> p t q j r", t=PACK, r=PAIR)[:, :, runs:],
            )

        w_codes = {}
        w_scales = {}
        for name in ("w1", "w3"):
            w_codes[name, 0] = keep.tile([P, HALF], U32, align_bytes=64, name=f"{name}a_codes")
            w_scales[name, 0] = keep.tile([P, HALF], U8, align_bytes=64, name=f"{name}a_scales")

        def quantize_places(name, t0, t1, values):
            cols = slice(t0 * P, t1 * P)
            quantize(w_codes[name, 0][:, cols], w_scales[name, 0][:, cols], values)

        quantize_x(PLACED_FROM, S, "x_codes_placed")
        quantize_x(0, SLICE, "late_rows")
        w1a_low = keep.tile([P, HALF * 2], BF16, align_bytes=64, name="w1a_low")
        w1a_high = keep.tile([P, HALF * 2], BF16, align_bytes=64, name="w1a_high")
        round_places(nc.scalar.copy, w1a_high[:], w1a, 2, 4)
        for t in range(2):
            round_places(nc.vector.tensor_copy, w1a_low[:, t * HALF : (t + 1) * HALF], w1a, t, t + 1)
        for t in range(2):
            quantize_places("w1", t, t + 1, w1a_low[:, t * HALF : (t + 1) * HALF])
        quantize_places("w1", 2, 4, w1a_high[:])
        quantize_x(SLICE, EARLY_UNTIL, "w1a")

        w3a_grouped = keep.tile([P, HALF * PACK], BF16, align_bytes=64, name="w3a_grouped", tag="w3a_grouped")

        def round_piece(copy, piece, t0, t1):
            runs = HALF // 2 // (PACK * PAIR)
            dst = w3a_grouped[:].rearrange("p (t q r j) -> p t q j r", t=PACK, r=PAIR, j=PACK)
            src = w3a[piece][:].rearrange("p j (q t r) -> p t q j r", t=PACK, r=PAIR)
            copy(dst[:, t0:t1, piece * runs : (piece + 1) * runs], src[:, t0:t1])

        round_piece(nc.scalar.copy, 0, 0, PACK)
        round_piece(nc.scalar.copy, 1, 3, PACK)
        round_piece(nc.vector.tensor_copy, 1, 0, 2)
        round_piece(nc.vector.tensor_copy, 1, 2, 3)
        quantize_places("w3", 0, 2, w3a_grouped[:, : 2 * HALF])
        quantize_places("w3", 2, 4, w3a_grouped[:, 2 * HALF :])
        quantize_x(EARLY_UNTIL, PLACED_FROM, "w3a_grouped")

        w1b_grouped = round_on_gpsimd(w1b, GPSIMD_RUNS["w1"])

        holds = {W1B_AFTER: "w1b_scales", W2_AFTER: "w2_grouped", STEPS - 2: "middle_scales", END_AFTER: "end_scales"}
        by_token = "p (t c) -> p c t"
        in_order = "p (c t) -> p c t"
        gate_rows = [keep.tile([P, T], F32, align_bytes=64, name="gates", tag=f"plane{j}") for j in range(slices)]
        ups = keep.tile([P, GPSIMD_GROUPS * WIDTH + FIRST_SHARE * PACK], F32, align_bytes=64, name="ups", tag="plane3")
        early_hidden = keep.tile([P, 2 * SLICE * PACK], BF16, align_bytes=64, name="early_hidden", tag="hidden0_1")
        hidden = {(0, s): early_hidden[:, s * SLICE * PACK : (s + 1) * SLICE * PACK] for s in range(2)}
        rings = {"w1": psum_1, "w3": psum_3}

        def passes(name, h, group, ring):
            bank = rings[ring].tile([P, WIDTH], F32, name="bank", tag=f"{ring}_bank")
            for t in range(PACK):
                m_cols = slice(t * P, (t + 1) * P)
                multiply(
                    bank[:, t * GROUP : (t + 1) * GROUP],
                    w_codes[name, h][:, m_cols],
                    w_scales[name, h][:, m_cols],
                    x_codes[group],
                    x_scales[group],
                )
            return bank[:].rearrange(by_token, t=PACK)

        gates = {}

        def make_gate(h, group):
            number = h * STEPS + group
            if number in holds:
                gate = keep.tile([P, WIDTH], F32, align_bytes=64, name="gate", tag=holds[number])[:]
            else:
                row, place = divmod(number, T // WIDTH)
                gate = gate_rows[row][:, place * WIDTH : (place + 1) * WIDTH]
            ring = "w3" if number < BORROWED else "w1"
            nc.scalar.activation(gate.rearrange(in_order, t=PACK), passes("w1", h, group, ring), Sigmoid)
            gates[h, group] = gate

        def product(h, group):
            s, c = divmod(group, GROUPS)
            if (h, s) not in hidden:
                hidden[h, s] = keep.tile([P, SLICE * PACK], BF16, align_bytes=64, name="hidden", tag=f"hidden{h}_{s}")
            values = hidden[h, s][:, c * WIDTH : (c + 1) * WIDTH]
            bank = passes("w3", h, group, "w3")
            nc.vector.tensor_tensor(values.rearrange(in_order, t=PACK), gates[h, group].rearrange(in_order, t=PACK), bank, mult)

        half_codes = [keep.tile([P, S], U32, align_bytes=64, name=f"h_codes{h}") for h in range(2)]
        h_codes = {(h, s): half_codes[h][:, s * SLICE : (s + 1) * SLICE] for h in range(2) for s in range(slices)}
        w2_codes = keep.tile([P, 2 * N], U32, align_bytes=64, name="w2_codes")

        for group in range(STEPS):
            for ahead in range(len(gates), min(STEPS, max(BANKS + BORROWED, group + LEAD[0] + 1))):
                make_gate(0, ahead)
            if group == 0:
                round_rest(w1b_grouped, w1b, GPSIMD_RUNS["w1"])
            product(0, group)
            if group == W1B_AFTER + 1:
                w_codes["w1", 1] = keep.tile([P, HALF], U32, align_bytes=64, name="w1b_codes")
                w_scales["w1", 1] = keep.tile([P, HALF], U8, align_bytes=64, name="scales", tag="w1b_scales")
                quantize(w_codes["w1", 1][:], w_scales["w1", 1][:], w1b_grouped[:])
                w3b_grouped = round_on_gpsimd(w3b, GPSIMD_RUNS["w3"])

        round_rest(w3b_grouped, w3b, GPSIMD_RUNS["w3"])

        middle = keep.tile([P, HALF + S], U8, align_bytes=64, name="scales", tag="middle_scales")
        w_codes["w3", 1] = keep.tile([P, HALF], U32, align_bytes=64, name="w3b_codes")
        w_scales["w3", 1] = middle[:, :HALF]
        h_scales = {(0, s): middle[:, HALF + s * SLICE : HALF + (s + 1) * SLICE] for s in range(slices)}
        quantize(w_codes["w3", 1][:], w_scales["w3", 1], w3b_grouped[:])
        quantize(half_codes[0][:, : 2 * SLICE], middle[:, HALF : HALF + 2 * SLICE], early_hidden[:])
        quantize(h_codes[0, 2], h_scales[0, 2], hidden[0, 2][:])

        firsts = keep.tile([P, (GPSIMD_GROUPS + 1) * WIDTH], BF16, align_bytes=64, name="firsts", tag=f"hidden0_{slices - 2}")
        row, place = divmod(STEPS, T // WIDTH)
        first_gates = gate_rows[row][:, place * WIDTH : (place + GPSIMD_GROUPS + 1) * WIDTH]
        whole = GPSIMD_GROUPS * WIDTH
        shared = whole + FIRST_SHARE * PACK
        for group in range(GPSIMD_GROUPS + 1):
            make_gate(1, group)
        for group in range(GPSIMD_GROUPS):
            up = ups[:, group * WIDTH : (group + 1) * WIDTH]
            nc.scalar.copy(up.rearrange(in_order, t=PACK), passes("w3", 1, group, "w3"))
        shared_bank = passes("w3", 1, GPSIMD_GROUPS, "w3")
        nc.vector.tensor_tensor(
            firsts[:, shared:].rearrange(in_order, t=PACK), first_gates[:, shared:].rearrange(in_order, t=PACK), shared_bank[:, FIRST_SHARE:], mult
        )
        nc.scalar.copy(ups[:, whole:].rearrange(in_order, t=PACK), shared_bank[:, :FIRST_SHARE])
        for start, done in ((0, WIDTH), (WIDTH, shared)):
            nc.gpsimd.tensor_tensor(firsts[:, start:done], first_gates[:, start:done], ups[:, start:done], mult)
        for group in range(GPSIMD_GROUPS + 1, END_AFTER + 2 - STEPS):
            for ahead in range(len(gates) - STEPS, min(LAST_GROUP + 1, group + LEAD[1] + 1)):
                make_gate(1, ahead)
                if STEPS + ahead == W2_GATE:
                    w2_grouped = keep.tile([P, 2 * N * PACK], BF16, align_bytes=64, name="w2_grouped", tag="w2_grouped")
                    nc.scalar.copy(
                        w2_grouped[:].rearrange("p (g m r t) -> p g m t r", g=2, r=PAIR, t=PACK),
                        w2_raw[:].rearrange("p g t (m r) -> p g m t r", r=PAIR),
                    )
            product(1, group)

        cut = LAST_SHARE * PACK
        final_bank = passes("w3", 1, LAST_GROUP, "w3")
        final_gate = gates[1, LAST_GROUP]
        final_up = keep.tile([P, cut], F32, align_bytes=64, name="final_up")
        nc.scalar.copy(final_up[:].rearrange(in_order, t=PACK), final_bank[:, :LAST_SHARE])
        for ahead in range(LAST_GROUP + 1, STEPS):
            make_gate(1, ahead)

        end = keep.tile([P, S + 2 * N], U8, align_bytes=64, name="scales", tag="end_scales")
        w2_scales = end[:, S:]
        for s in range(slices):
            h_scales[1, s] = end[:, s * SLICE : (s + 1) * SLICE]

        def quantize_h(s, start, done, values):
            quantize(h_codes[1, s][:, start:done], h_scales[1, s][:, start:done], values)

        def finish(s, start, done):
            acc = psum_1.tile([P, done - start], F32, name="acc", tag="w1_bank")
            for g in range(2):
                multiply(
                    acc[:],
                    w2_codes[:, g * N : (g + 1) * N],
                    w2_scales[:, g * N : (g + 1) * N],
                    h_codes[g, s][:, start:done],
                    h_scales[g, s][:, start:done],
                    start=(g == 0),
                    stop=(g == 1),
                )
            y = keep.tile([P, done - start], F32, name=f"y{s}_{start}")
            nc.scalar.copy(y[:], acc[:])
            for first in range(start, done, STORE):
                until = min(done, first + STORE)
                nc.sync.dma_start(out=out[:, s * SLICE + first : s * SLICE + until], in_=y[:, first - start : until - start])

        split = (GPSIMD_GROUPS + 1) * GROUP
        quantize_h(0, 0, split, firsts[:])
        quantize(w2_codes[:], w2_scales, w2_grouped[:])
        quantize_h(0, split, SLICE, hidden[1, 0][:, split * PACK :])
        finish(0, 0, SLICE)
        quantize_h(1, 0, 2 * GROUP, hidden[1, 1][:, : 2 * WIDTH])
        finish(1, 0, 2 * GROUP)
        quantize_h(1, 2 * GROUP, SLICE, hidden[1, 1][:, 2 * WIDTH :])
        finish(1, 2 * GROUP, SLICE)
        last = slices - 1
        quantize_h(last, 0, GROUP, hidden[1, last][:, :WIDTH])
        finish(last, 0, GROUP)

        final = keep.tile([P, WIDTH], BF16, align_bytes=64, name="final", tag="hidden1_1")
        nc.gpsimd.tensor_tensor(final[:, :cut], final_gate[:, :cut], final_up[:], mult)
        product(1, STEPS - 2)
        product(1, STEPS - 1)
        nc.vector.tensor_tensor(
            final[:, cut:].rearrange(in_order, t=PACK), final_gate[:, cut:].rearrange(in_order, t=PACK), final_bank[:, LAST_SHARE:], mult
        )
        for c, values in ((2, hidden[1, last][:, 2 * WIDTH : 3 * WIDTH]), (3, hidden[1, last][:, 3 * WIDTH :]), (1, final[:])):
            quantize_h(last, c * GROUP, (c + 1) * GROUP, values)
            finish(last, c * GROUP, (c + 1) * GROUP)
